import numpy as np
import ml_dtypes


def mxq(x, axis, fmt="e4m3"):
    dtype, down = {"e4m3": (ml_dtypes.float8_e4m3fn, 7), "e5m2": (ml_dtypes.float8_e5m2, 14)}[fmt]
    v = np.moveaxis(np.asarray(x, np.float32).astype(ml_dtypes.bfloat16).astype(np.float64), axis, -1)
    blocks = v.reshape(v.shape[:-1] + (-1, 32))
    amax = np.abs(blocks).max(-1, keepdims=True)
    byte = np.maximum(np.where(amax > 0, np.frexp(amax)[1] - 1 + 127, 0) - down, 1)
    scale = np.exp2(byte - 127.0)
    codes = (blocks / scale).astype(np.float32).astype(dtype).astype(np.float64)
    return np.moveaxis((codes * scale).reshape(v.shape), -1, axis)


WIDE = False


def mx_kscale(k):
    if not WIDE:
        return np.ones(k)
    levels = np.array([18, -18])
    if k % 512:
        return np.exp2(np.random.permutation(np.resize(levels, k // 32))).repeat(32)
    a = np.empty((k // 512, 16))
    for p in range(k // 512):
        a[p, :8] = np.random.permutation(np.resize(levels, 8))
        for g in range(8):
            far = levels[np.abs(levels - a[p, g]) >= 10]
            a[p, g + 8] = far[np.random.randint(len(far))]
    return np.exp2(a.ravel()).repeat(32)


def f64(x):
    return np.asarray(x).astype(np.float64)


def striped(idx):
    return np.tile(np.asarray(idx).reshape(-1, 16).T, (8, 1)).astype(np.uint16)


def unstriped(offs):
    return offs[:16].T.reshape(-1).astype(np.int64)


N, T, D, V = 1024, 2048, 512, 512


def setup_inputs():
    n = np.random.standard_normal
    idx = np.random.permutation(T)[:N]
    s = mx_kscale(D)[:, None]
    z = mx_kscale(V)[:, None]
    w = n((D, V)) / np.sqrt(D)
    return {
        "xT": (n((D, T)) / s).astype(np.float32),
        "wd": (w * s).astype(np.float32),
        "wv": (w.T / z).astype(np.float32),
        "y": n((V, N)).astype(np.float32),
        "cw": (np.random.uniform(0.5, 1.5, (V, 1)) / np.sqrt(V) * z).astype(np.float32),
        "rw": np.tile(np.random.uniform(0.5, 1.5, N), (128, 1)).astype(np.float32),
        "offs": striped(idx),
    }


def reference(xT, wd, wv, y, cw, rw, offs):
    idx = unstriped(offs)
    a = mxq(f64(wd), 0, "e4m3").T @ mxq(f64(xT)[:, idx], 0, "e4m3")
    g = f64(cw) * f64(rw)[:1] * np.tanh(a - f64(y))
    dx = mxq(f64(wv), 0, "e4m3").T @ mxq(g, 0, "e5m2")
    gx = np.zeros((D, T))
    gx[:, idx] = dx
    return gx

@@ -1,0 +1,272 @@
+from contextlib import ExitStack
+
+import concourse.mybir as mybir
+
+N, T, D, V = 1024, 2048, 512, 512
+FLOPS = 2 * 2 * D * V * N
+
+F32 = mybir.dt.float32
+BF16 = mybir.dt.bfloat16
+U32 = mybir.dt.uint32
+U16 = mybir.dt.uint16
+U8 = mybir.dt.uint8
+E4M3 = mybir.dt.float8_e4m3fn_x4
+E5M2 = mybir.dt.float8_e5m2_x4
+COPY = mybir.ActivationFunctionType.Copy
+TANH = mybir.ActivationFunctionType.Tanh
+MULT = mybir.AluOpType.mult
+ADD = mybir.AluOpType.add
+SUB = mybir.AluOpType.subtract
+
+P = 128
+PACK = 4
+GROUP = 128
+PIECE = 256
+BANK = 512
+CHUNKS = [(0, 256), (256, 256), (512, 512)]
+X_LOADS = [(0, 0, 1024, 512), (0, 1024, 1024, 512), (1, 0, 1024, 0), (1, 1024, 512, 0), (1, 1536, 512, 320)]
+MID = ["vv"] * 8
+WENG = ["g", "s", "s"]
+WD_VEC = [0, 40]
+WV_ENG = ["s"] * 4
+
+
+def tile_attend_gml_lch_kernel(tc, xT, wd, wv, y, cw, rw, offs, out):
+    nc = tc.nc
+    with ExitStack() as ctx:
+        keep = ctx.enter_context(tc.tile_pool(name="keep", bufs=1))
+        ring = ctx.enter_context(tc.tile_pool(name="ring", bufs=4))
+        psum = ctx.enter_context(tc.psum_pool(name="psum", bufs=4))
+
+        offsets = keep.tile([P, N // 16], U16, name="offsets")
+        nc.sync.dma_start(offsets[:], offs)
+
+        def listed(c0, n):
+            return offsets[:, c0 // 16 : (c0 + n) // 16]
+
+        def cast(eng, dst, src):
+            if eng == "v":
+                nc.vector.tensor_copy(out=dst, in_=src)
+            elif eng == "s":
+                nc.scalar.activation(out=dst, in_=src, func=COPY)
+            else:
+                nc.gpsimd.tensor_scalar(out=dst, in0=src, scalar1=1.0, scalar2=0.0, op0=MULT, op1=ADD)
+
+        warm = keep.tile([P, 8], F32, name="warm")
+        warm_out = keep.tile([P, 8], F32, name="warm_out")
+        nc.vector.memset(warm[:], 0.0)
+        nc.scalar.activation(out=warm_out[:], in_=warm[:], func=TANH)
+
+        cw_sb = keep.tile([P, PACK], F32, name="cw_sb")
+        rw_sb = [keep.tile([P, n], F32, name="rw%d" % c) for c, (c0, n) in enumerate(CHUNKS)]
+        y_sb = [keep.tile([P, PACK, n], F32, name="y%d" % c) for c, (c0, n) in enumerate(CHUNKS)]
+        weight = [keep.tile([P, PACK, n], F32, name="weight%d" % c) for c, (c0, n) in enumerate(CHUNKS)]
+        y_rows = y.rearrange("(p t) n -> p t n", t=PACK)
+
+        def load_rw(c):
+            c0, n = CHUNKS[c]
+            nc.sync.dma_start(rw_sb[c][:], rw[:, c0 : c0 + n])
+
+        def load_y(c):
+            c0, n = CHUNKS[c]
+            nc.sync.dma_start(y_sb[c][:], y_rows[:, :, c0 : c0 + n])
+
+        def make_weight(c):
+            for t in range(PACK):
+                if WENG[c] == "g":
+                    nc.gpsimd.tensor_scalar(out=weight[c][:, t, :], in0=rw_sb[c][:], scalar1=cw_sb[:, t : t + 1], scalar2=0.0, op0=MULT, op1=ADD)
+                else:
+                    nc.scalar.activation(out=weight[c][:, t, :], in_=rw_sb[c][:], func=COPY, scale=cw_sb[:, t : t + 1])
+
+        x_rows = xT.rearrange("(p u e) n -> p u e n", u=2, e=2)
+        x_raw = []
+        for k, (u, n0, n, nv) in enumerate(X_LOADS):
+            raw = keep.tile([P, 2, n], F32, name="x_raw%d" % k)
+            nc.sync.dma_start(raw[:], x_rows[:, u, :, n0 : n0 + n])
+            x_raw.append(raw)
+            if k == 0:
+                nc.sync.dma_start(cw_sb[:], cw.rearrange("(p t) o -> p (t o)", t=PACK))
+                load_rw(0)
+        wd_rows = wd.rearrange("(p j) v -> p j v", j=PACK)
+        wv_rows = wv.rearrange("(p t) d -> p t d", t=PACK)
+        wd_raw = [keep.tile([P, PACK, V // 2], F32, name="wd_raw%d" % h) for h in range(2)]
+        wv_raw = [keep.tile([P, PACK, D // 2], F32, name="wv_raw%d" % h) for h in range(2)]
+        for h in range(2):
+            nc.sync.dma_start(wd_raw[h][:], wd_rows[:, :, h * 256 : (h + 1) * 256])
+        load_y(0)
+        for h in range(2):
+            nc.sync.dma_start(wv_raw[h][:], wv_rows[:, :, h * 256 : (h + 1) * 256])
+        for c in range(1, len(CHUNKS)):
+            load_y(c)
+            load_rw(c)
+
+        placed = [keep.tile([P, T], F32, name="placed%d" % j) for j in range(D // P)]
+        for j in range(D // P):
+            nc.vector.memset(placed[j][:].bitcast(U32), 0)
+        g_codes = [keep.tile([P, BANK], U32, name="g_codes%d" % c, align_bytes=64) for c in range(len(CHUNKS))]
+        g_scales = [keep.tile([P, BANK], U8, name="g_scales%d" % c, align_bytes=64) for c in range(len(CHUNKS))]
+        for c, (c0, n) in enumerate(CHUNKS):
+            if n < BANK:
+                nc.vector.memset(g_codes[c][:, n:], 0)
+                nc.vector.memset(g_scales[c][:, n:].bitcast(U32), 0)
+
+        make_weight(0)
+
+        pairs = [keep.tile([P, T, 2], BF16, name="pairs%d" % u, align_bytes=64) for u in range(2)]
+        windows = [pairs[u][:].rearrange("p n e -> p (n e)").bitcast(U32) for u in range(2)]
+        x_grouped = keep.tile([P, N, PACK], BF16, name="x_grouped", align_bytes=64)
+        x_words = x_grouped[:].rearrange("p n j -> p (n j)").bitcast(U32).rearrange("p (n u) -> p n u", u=2)
+        x_codes = keep.tile([P, N], U32, name="x_codes", align_bytes=64)
+        x_scales = keep.tile([P, N], U8, name="x_scales", align_bytes=64)
+
+        def pair_up(k):
+            u, n0, n, nv = X_LOADS[k]
+            for eng, a, b in (("s", 0, n - nv), ("v", n - nv, n)):
+                if b > a:
+                    cast(eng,
+                         pairs[u][:, n0 + a : n0 + b, :].rearrange("p (c i) e -> p c e i", i=4),
+                         x_raw[k][:, :, a:b].rearrange("p e (c i) -> p c e i", i=4))
+
+        def gather(u, c0):
+            nc.vector.tensor_copy(out=x_words[:, c0 : c0 + PIECE, u], in_=windows[u].indirect(listed(c0, PIECE)))
+
+        def quantize_x(c0):
+            nc.vector.quantize_mx(
+                out=x_codes[:, c0 : c0 + PIECE].bitcast(E4M3),
+                scales=x_scales[:, c0 : c0 + PIECE],
+                in_=x_grouped[:, c0 : c0 + PIECE, :].rearrange("p n j -> p (n j)"),
+            )
+
+        for k in range(len(X_LOADS)):
+            pair_up(k)
+            if X_LOADS[k][0] == 0 and X_LOADS[k + 1][0] == 1:
+                for c0 in range(0, N, PIECE):
+                    gather(0, c0)
+        gather(1, 0)
+        quantize_x(0)
+
+        wd_grouped = keep.tile([P, PACK, P, PACK], BF16, name="wd_grouped", align_bytes=64)
+        wd_codes = keep.tile([P, V], U32, name="wd_codes", align_bytes=64)
+        wd_scales = keep.tile([P, V], U8, name="wd_scales", align_bytes=64)
+        for h in range(2):
+            mv = WD_VEC[h]
+            for eng, a, b in (("s", 0, 64 - mv), ("v", 64 - mv, 64)):
+                if b > a:
+                    cast(eng,
+                         wd_grouped[:, :, 64 * h + a : 64 * h + b, :].rearrange("p t m j -> p m j t"),
+                         wd_raw[h][:, :, 4 * a : 4 * b].rearrange("p j (m t) -> p m j t", t=PACK))
+        nc.vector.quantize_mx(
+            out=wd_codes[:].bitcast(E4M3),
+            scales=wd_scales[:],
+            in_=wd_grouped[:].rearrange("p t m j -> p (t m j)"),
+        )
+
+        wv_grouped = keep.tile([P, D, PACK], BF16, name="wv_grouped", align_bytes=64)
+        wv_codes = keep.tile([P, D], U32, name="wv_codes", align_bytes=64)
+        wv_scales = keep.tile([P, D], U8, name="wv_scales", align_bytes=64)
+
+        def prepare_wv(j):
+            h, a = divmod(j * P, 256)
+            cast(WV_ENG[j],
+                 wv_grouped[:, j * P : (j + 1) * P, :].rearrange("p (c i) t -> p c t i", i=4),
+                 wv_raw[h][:, :, a : a + P].rearrange("p t (c i) -> p c t i", i=4))
+            nc.vector.quantize_mx(
+                out=wv_codes[:, j * P : (j + 1) * P].bitcast(E4M3),
+                scales=wv_scales[:, j * P : (j + 1) * P],
+                in_=wv_grouped[:, j * P : (j + 1) * P, :].rearrange("p d t -> p (d t)"),
+            )
+
+        g_grouped = keep.tile([P, N, PACK], BF16, name="g_grouped", align_bytes=64)
+
+        def runs(ap):
+            return ap.rearrange("p t (c i) -> p c t i", i=4)
+
+        def middle(c, i0):
+            c0, n = CHUNKS[c]
+            eng = MID[(c0 + i0) // GROUP]
+            cols = slice(c0 + i0, c0 + i0 + GROUP)
+            a = psum.tile([P, PACK, GROUP], F32, name="a")
+            for t in range(PACK):
+                nc.tensor.matmul_mx(
+                    out=a[:, t, :],
+                    lhsT=wd_codes[:, t * P : (t + 1) * P].bitcast(E4M3),
+                    lhsT_scale=wd_scales[:, t * P : (t + 1) * P],
+                    rhs=x_codes[:, cols].bitcast(E4M3),
+                    rhs_scale=x_scales[:, cols],
+                    start=True,
+                    stop=True,
+                )
+            diff = ring.tile([P, PACK, GROUP], F32, name="diff")
+            if eng[0] == "v":
+                nc.vector.tensor_tensor(out=diff[:], in0=a[:], in1=y_sb[c][:, :, i0 : i0 + GROUP], op=SUB)
+            else:
+                a_sb = ring.tile([P, PACK, GROUP], F32, name="a_sb")
+                nc.scalar.activation(out=a_sb[:], in_=a[:], func=COPY)
+                nc.gpsimd.tensor_tensor(out=diff[:], in0=a_sb[:], in1=y_sb[c][:, :, i0 : i0 + GROUP], op=SUB)
+            slope = ring.tile([P, PACK, GROUP], F32, name="slope")
+            nc.scalar.activation(out=slope[:], in_=diff[:], func=TANH)
+            (nc.vector if eng[1] == "v" else nc.gpsimd).tensor_tensor(
+                out=g_grouped[:, cols, :].rearrange("p (c i) t -> p c t i", i=4),
+                in0=runs(slope[:]),
+                in1=runs(weight[c][:, :, i0 : i0 + GROUP]),
+                op=MULT,
+            )
+
+        def quantize_g(c, i0, n):
+            c0 = CHUNKS[c][0]
+            nc.vector.quantize_mx(
+                out=g_codes[c][:, i0 : i0 + n].bitcast(E5M2),
+                scales=g_scales[c][:, i0 : i0 + n],
+                in_=g_grouped[:, c0 + i0 : c0 + i0 + n, :].rearrange("p n t -> p (n t)"),
+            )
+
+        dx_sb = {}
+
+        def second(c, j):
+            c0, n = CHUNKS[c]
+            dx = psum.tile([P, BANK], F32, name="dx")
+            nc.tensor.matmul_mx(
+                out=dx[:],
+                lhsT=wv_codes[:, j * P : (j + 1) * P].bitcast(E4M3),
+                lhsT_scale=wv_scales[:, j * P : (j + 1) * P],
+                rhs=g_codes[c][:].bitcast(E5M2),
+                rhs_scale=g_scales[c][:],
+                start=True,
+                stop=True,
+            )
+            dx_sb[c, j] = keep.tile([P, n], F32, name="dx_sb%d_%d" % (c, j))
+            nc.scalar.activation(out=dx_sb[c, j][:], in_=dx[:, :n], func=COPY)
+
+        def place(c, j):
+            c0, n = CHUNKS[c]
+            nc.vector.tensor_copy(out=placed[j][:].indirect(listed(c0, n)), in_=dx_sb[c, j][:])
+            if c == len(CHUNKS) - 1:
+                nc.sync.dma_start(out[j * P : (j + 1) * P, :], placed[j][:])
+
+        def front(c):
+            c0, n = CHUNKS[c]
+            if c > 0:
+                make_weight(c)
+            for i0 in range(0, n, GROUP):
+                middle(c, i0)
+                if c == 0 and i0 == 0:
+                    prepare_wv(0)
+            i0 = 0
+            for w in (512, 256, 128):
+                if n - i0 >= w:
+                    quantize_g(c, i0, w)
+                    i0 += w
+            for j in range(D // P):
+                if c == 0 and j > 0:
+                    prepare_wv(j)
+                second(c, j)
+
+        front(0)
+        for c0 in range(PIECE, N, PIECE):
+            gather(1, c0)
+            quantize_x(c0)
+        for c in range(len(CHUNKS)):
+            if c + 1 < len(CHUNKS):
+                front(c + 1)
+            for j in range(D // P):
+                place(c, j)

@@ -23,12 +23,14 @@ PACK = 4
 GROUP = 128
 PIECE = 256
 BANK = 512
-CHUNKS = [(0, 256), (256, 256), (512, 512)]
-X_LOADS = [(0, 0, 1024, 512), (0, 1024, 1024, 512), (1, 0, 1024, 0), (1, 1024, 512, 0), (1, 1536, 512, 320)]
-MID = ["vv"] * 8
-WENG = ["g", "s", "s"]
-WD_VEC = [0, 40]
-WV_ENG = ["s"] * 4
+HALF = 256
+X_COLS = 512
+X_TAIL_VEC = 320
+CHUNKS = [(0, 256), (256, 384), (640, 384)]
+LATE = [2, 3, 9]
+MID = ["vv"] * 2 + ["vg"] * 3 + ["gg"] * 3
+LATE_LOADS = [("wd", 0), ("wd", 1), ("y", 0), ("rw", 1), ("wv", 0), ("y", 1), ("wv", 1), ("y", 2), ("rw", 2), ("y", 3)]
+QX = [(0, 256), (256, 256), (512, 512)]
 
 
 def tile_attend_gml_lch_kernel(tc, xT, wd, wv, y, cw, rw, offs, out):
@@ -38,67 +40,52 @@ def tile_attend_gml_lch_kernel(tc, xT, wd, wv, y, cw, rw, offs, out):
         ring = ctx.enter_context(tc.tile_pool(name="ring", bufs=4))
         psum = ctx.enter_context(tc.psum_pool(name="psum", bufs=4))
 
-        offsets = keep.tile([P, N // 16], U16, name="offsets")
-        nc.sync.dma_start(offsets[:], offs)
+        def runs(ap):
+            return ap.rearrange("p t (c i) -> p c t i", i=4)
 
-        def listed(c0, n):
-            return offsets[:, c0 // 16 : (c0 + n) // 16]
-
-        def cast(eng, dst, src):
-            if eng == "v":
-                nc.vector.tensor_copy(out=dst, in_=src)
-            elif eng == "s":
-                nc.scalar.activation(out=dst, in_=src, func=COPY)
-            else:
-                nc.gpsimd.tensor_scalar(out=dst, in0=src, scalar1=1.0, scalar2=0.0, op0=MULT, op1=ADD)
+        def runs_packed(ap):
+            return ap.rearrange("p (c i) t -> p c t i", i=4)
 
         warm = keep.tile([P, 8], F32, name="warm")
         warm_out = keep.tile([P, 8], F32, name="warm_out")
         nc.vector.memset(warm[:], 0.0)
         nc.scalar.activation(out=warm_out[:], in_=warm[:], func=TANH)
 
+        offsets = keep.tile([P, N // 16], U16, name="offsets")
         cw_sb = keep.tile([P, PACK], F32, name="cw_sb")
         rw_sb = [keep.tile([P, n], F32, name="rw%d" % c) for c, (c0, n) in enumerate(CHUNKS)]
-        y_sb = [keep.tile([P, PACK, n], F32, name="y%d" % c) for c, (c0, n) in enumerate(CHUNKS)]
-        weight = [keep.tile([P, PACK, n], F32, name="weight%d" % c) for c, (c0, n) in enumerate(CHUNKS)]
-        y_rows = y.rearrange("(p t) n -> p t n", t=PACK)
-
-        def load_rw(c):
-            c0, n = CHUNKS[c]
-            nc.sync.dma_start(rw_sb[c][:], rw[:, c0 : c0 + n])
-
-        def load_y(c):
-            c0, n = CHUNKS[c]
-            nc.sync.dma_start(y_sb[c][:], y_rows[:, :, c0 : c0 + n])
-
-        def make_weight(c):
-            for t in range(PACK):
-                if WENG[c] == "g":
-                    nc.gpsimd.tensor_scalar(out=weight[c][:, t, :], in0=rw_sb[c][:], scalar1=cw_sb[:, t : t + 1], scalar2=0.0, op0=MULT, op1=ADD)
-                else:
-                    nc.scalar.activation(out=weight[c][:, t, :], in_=rw_sb[c][:], func=COPY, scale=cw_sb[:, t : t + 1])
-
+        y_sb = [keep.tile([P, PACK, PIECE], F32, name="y%d" % k) for k in range(N // PIECE)]
+        wd_raw = [keep.tile([P, PACK, HALF], F32, name="wd_raw%d" % h) for h in range(2)]
+        wv_raw = [keep.tile([P, PACK, HALF], F32, name="wv_raw%d" % h) for h in range(2)]
         x_rows = xT.rearrange("(p u e) n -> p u e n", u=2, e=2)
-        x_raw = []
-        for k, (u, n0, n, nv) in enumerate(X_LOADS):
-            raw = keep.tile([P, 2, n], F32, name="x_raw%d" % k)
-            nc.sync.dma_start(raw[:], x_rows[:, u, :, n0 : n0 + n])
-            x_raw.append(raw)
-            if k == 0:
-                nc.sync.dma_start(cw_sb[:], cw.rearrange("(p t) o -> p (t o)", t=PACK))
-                load_rw(0)
+        y_rows = y.rearrange("(p t) n -> p t n", t=PACK)
         wd_rows = wd.rearrange("(p j) v -> p j v", j=PACK)
         wv_rows = wv.rearrange("(p t) d -> p t d", t=PACK)
-        wd_raw = [keep.tile([P, PACK, V // 2], F32, name="wd_raw%d" % h) for h in range(2)]
-        wv_raw = [keep.tile([P, PACK, D // 2], F32, name="wv_raw%d" % h) for h in range(2)]
-        for h in range(2):
-            nc.sync.dma_start(wd_raw[h][:], wd_rows[:, :, h * 256 : (h + 1) * 256])
-        load_y(0)
-        for h in range(2):
-            nc.sync.dma_start(wv_raw[h][:], wv_rows[:, :, h * 256 : (h + 1) * 256])
-        for c in range(1, len(CHUNKS)):
-            load_y(c)
-            load_rw(c)
+
+        def load(kind, k):
+            if kind == "rw":
+                c0, n = CHUNKS[k]
+                nc.sync.dma_start(rw_sb[k][:], rw[:, c0 : c0 + n])
+            elif kind == "cw":
+                nc.sync.dma_start(cw_sb[:], cw.rearrange("(p t) o -> p (t o)", t=PACK))
+            else:
+                tiles, rows = {"y": (y_sb, y_rows), "wd": (wd_raw, wd_rows), "wv": (wv_raw, wv_rows)}[kind]
+                nc.sync.dma_start(tiles[k][:], rows[:, :, k * HALF : (k + 1) * HALF])
+
+        x_raw = {}
+        for u in range(2):
+            for n0 in range(0, T, X_COLS):
+                x_raw[u, n0] = keep.tile([P, 2, X_COLS], F32, name="x_raw%d_%d" % (u, n0))
+                nc.sync.dma_start(x_raw[u, n0][:], x_rows[:, u, :, n0 : n0 + X_COLS])
+                if (u, n0) == (0, 0):
+                    nc.sync.dma_start(offsets[:], offs)
+                    load("cw", 0)
+                    load("rw", 0)
+        for kind, k in LATE_LOADS:
+            load(kind, k)
+
+        def listed(c0, n):
+            return offsets[:, c0 // 16 : (c0 + n) // 16]
 
         placed = [keep.tile([P, T], F32, name="placed%d" % j) for j in range(D // P)]
         for j in range(D // P):
@@ -107,126 +94,145 @@ def tile_attend_gml_lch_kernel(tc, xT, wd, wv, y, cw, rw, offs, out):
         g_scales = [keep.tile([P, BANK], U8, name="g_scales%d" % c, align_bytes=64) for c in range(len(CHUNKS))]
         for c, (c0, n) in enumerate(CHUNKS):
             if n < BANK:
-                nc.vector.memset(g_codes[c][:, n:], 0)
-                nc.vector.memset(g_scales[c][:, n:].bitcast(U32), 0)
+                nc.gpsimd.memset(g_codes[c][:, n:], 0)
+                nc.gpsimd.memset(g_scales[c][:, n:].bitcast(U32), 0)
 
-        make_weight(0)
+        weight = [keep.tile([P, PACK, n], F32, name="weight%d" % c) for c, (c0, n) in enumerate(CHUNKS)]
+
+        def make_weight(c):
+            for t in range(PACK):
+                if c == 0 and True:
+                    nc.gpsimd.tensor_scalar(out=weight[c][:, t, :], in0=rw_sb[c][:], scalar1=cw_sb[:, t : t + 1], scalar2=0.0, op0=MULT, op1=ADD)
+                else:
+                    nc.scalar.activation(out=weight[c][:, t, :], in_=rw_sb[c][:], func=COPY, scale=cw_sb[:, t : t + 1])
 
         pairs = [keep.tile([P, T, 2], BF16, name="pairs%d" % u, align_bytes=64) for u in range(2)]
         windows = [pairs[u][:].rearrange("p n e -> p (n e)").bitcast(U32) for u in range(2)]
         x_grouped = keep.tile([P, N, PACK], BF16, name="x_grouped", align_bytes=64)
         x_words = x_grouped[:].rearrange("p n j -> p (n j)").bitcast(U32).rearrange("p (n u) -> p n u", u=2)
-        x_codes = keep.tile([P, N], U32, name="x_codes", align_bytes=64)
+        x_codes = [keep.tile([P, PIECE], U32, name="x_codes", align_bytes=64)]
         x_scales = keep.tile([P, N], U8, name="x_scales", align_bytes=64)
 
-        def pair_up(k):
-            u, n0, n, nv = X_LOADS[k]
-            for eng, a, b in (("s", 0, n - nv), ("v", n - nv, n)):
-                if b > a:
-                    cast(eng,
-                         pairs[u][:, n0 + a : n0 + b, :].rearrange("p (c i) e -> p c e i", i=4),
-                         x_raw[k][:, :, a:b].rearrange("p e (c i) -> p c e i", i=4))
+        def x_codes_of(c0, n):
+            return (x_codes[0][:, c0 : c0 + n] if c0 < PIECE else x_codes[1][:, c0 - PIECE : c0 - PIECE + n]).bitcast(E4M3)
 
-        def gather(u, c0):
-            nc.vector.tensor_copy(out=x_words[:, c0 : c0 + PIECE, u], in_=windows[u].indirect(listed(c0, PIECE)))
-
-        def quantize_x(c0):
+        def quantize_x(c0, n):
             nc.vector.quantize_mx(
-                out=x_codes[:, c0 : c0 + PIECE].bitcast(E4M3),
-                scales=x_scales[:, c0 : c0 + PIECE],
-                in_=x_grouped[:, c0 : c0 + PIECE, :].rearrange("p n j -> p (n j)"),
+                out=x_codes_of(c0, n),
+                scales=x_scales[:, c0 : c0 + n],
+                in_=x_grouped[:, c0 : c0 + n, :].rearrange("p n j -> p (n j)"),
             )
 
-        for k in range(len(X_LOADS)):
-            pair_up(k)
-            if X_LOADS[k][0] == 0 and X_LOADS[k + 1][0] == 1:
-                for c0 in range(0, N, PIECE):
-                    gather(0, c0)
-        gather(1, 0)
-        quantize_x(0)
+        for u in range(2):
+            for n0 in range(0, T, X_COLS):
+                cut = X_COLS - (X_TAIL_VEC if (u, n0) == (1, T - X_COLS) else 0)
+                nc.scalar.activation(out=runs_packed(pairs[u][:, n0 : n0 + cut, :]), in_=runs(x_raw[u, n0][:, :, :cut]), func=COPY)
+                if cut < X_COLS:
+                    nc.vector.tensor_copy(out=runs_packed(pairs[u][:, n0 + cut : n0 + X_COLS, :]), in_=runs(x_raw[u, n0][:, :, cut:]))
+            for c0 in range(0, N, 256):
+                nc.vector.tensor_copy(out=x_words[:, c0 : c0 + 256, u], in_=windows[u].indirect(listed(c0, 256)))
+        quantize_x(*QX[0])
 
         wd_grouped = keep.tile([P, PACK, P, PACK], BF16, name="wd_grouped", align_bytes=64)
         wd_codes = keep.tile([P, V], U32, name="wd_codes", align_bytes=64)
         wd_scales = keep.tile([P, V], U8, name="wd_scales", align_bytes=64)
         for h in range(2):
-            mv = WD_VEC[h]
-            for eng, a, b in (("s", 0, 64 - mv), ("v", 64 - mv, 64)):
-                if b > a:
-                    cast(eng,
-                         wd_grouped[:, :, 64 * h + a : 64 * h + b, :].rearrange("p t m j -> p m j t"),
-                         wd_raw[h][:, :, 4 * a : 4 * b].rearrange("p j (m t) -> p m j t", t=PACK))
+            nc.scalar.activation(
+                out=wd_grouped[:, :, 64 * h : 64 * (h + 1), :].rearrange("p t m j -> p m j t"),
+                in_=wd_raw[h][:].rearrange("p j (m t) -> p m j t", t=PACK),
+                func=COPY,
+            )
         nc.vector.quantize_mx(
             out=wd_codes[:].bitcast(E4M3),
             scales=wd_scales[:],
             in_=wd_grouped[:].rearrange("p t m j -> p (t m j)"),
         )
+        x_codes.append(keep.tile([P, N - PIECE], U32, name="x_codes_late", tag="wd_grouped", align_bytes=64))
+        make_weight(0)
 
         wv_grouped = keep.tile([P, D, PACK], BF16, name="wv_grouped", align_bytes=64)
         wv_codes = keep.tile([P, D], U32, name="wv_codes", align_bytes=64)
         wv_scales = keep.tile([P, D], U8, name="wv_scales", align_bytes=64)
 
-        def prepare_wv(j):
-            h, a = divmod(j * P, 256)
-            cast(WV_ENG[j],
-                 wv_grouped[:, j * P : (j + 1) * P, :].rearrange("p (c i) t -> p c t i", i=4),
-                 wv_raw[h][:, :, a : a + P].rearrange("p t (c i) -> p c t i", i=4))
+        def prepare_wv(h):
+            for a in range(0, HALF, P):
+                nc.scalar.activation(
+                    out=runs_packed(wv_grouped[:, h * HALF + a : h * HALF + a + P, :]),
+                    in_=runs(wv_raw[h][:, :, a : a + P]),
+                    func=COPY,
+                )
             nc.vector.quantize_mx(
-                out=wv_codes[:, j * P : (j + 1) * P].bitcast(E4M3),
-                scales=wv_scales[:, j * P : (j + 1) * P],
-                in_=wv_grouped[:, j * P : (j + 1) * P, :].rearrange("p d t -> p (d t)"),
+                out=wv_codes[:, h * HALF : (h + 1) * HALF].bitcast(E4M3),
+                scales=wv_scales[:, h * HALF : (h + 1) * HALF],
+                in_=wv_grouped[:, h * HALF : (h + 1) * HALF, :].rearrange("p d t -> p (d t)"),
             )
 
-        g_grouped = keep.tile([P, N, PACK], BF16, name="g_grouped", align_bytes=64)
+        diff = {}
+        g_part = {}
 
-        def runs(ap):
-            return ap.rearrange("p t (c i) -> p c t i", i=4)
-
-        def middle(c, i0):
-            c0, n = CHUNKS[c]
-            eng = MID[(c0 + i0) // GROUP]
-            cols = slice(c0 + i0, c0 + i0 + GROUP)
+        def subtract(gi, tile):
+            c0 = gi * GROUP
+            k, y0 = divmod(c0, PIECE)
+            diff[gi] = tile
             a = psum.tile([P, PACK, GROUP], F32, name="a")
             for t in range(PACK):
                 nc.tensor.matmul_mx(
                     out=a[:, t, :],
                     lhsT=wd_codes[:, t * P : (t + 1) * P].bitcast(E4M3),
                     lhsT_scale=wd_scales[:, t * P : (t + 1) * P],
-                    rhs=x_codes[:, cols].bitcast(E4M3),
-                    rhs_scale=x_scales[:, cols],
+                    rhs=x_codes_of(c0, GROUP),
+                    rhs_scale=x_scales[:, c0 : c0 + GROUP],
                     start=True,
                     stop=True,
                 )
-            diff = ring.tile([P, PACK, GROUP], F32, name="diff")
-            if eng[0] == "v":
-                nc.vector.tensor_tensor(out=diff[:], in0=a[:], in1=y_sb[c][:, :, i0 : i0 + GROUP], op=SUB)
+            if MID[gi][0] == "v":
+                nc.vector.tensor_tensor(out=tile, in0=a[:], in1=y_sb[k][:, :, y0 : y0 + GROUP], op=SUB)
             else:
                 a_sb = ring.tile([P, PACK, GROUP], F32, name="a_sb")
                 nc.scalar.activation(out=a_sb[:], in_=a[:], func=COPY)
-                nc.gpsimd.tensor_tensor(out=diff[:], in0=a_sb[:], in1=y_sb[c][:, :, i0 : i0 + GROUP], op=SUB)
+                return lambda: nc.gpsimd.tensor_tensor(out=tile, in0=a_sb[:], in1=y_sb[k][:, :, y0 : y0 + GROUP], op=SUB)
+
+        def weigh(c, i0, dst):
+            gi = (CHUNKS[c][0] + i0) // GROUP
             slope = ring.tile([P, PACK, GROUP], F32, name="slope")
-            nc.scalar.activation(out=slope[:], in_=diff[:], func=TANH)
-            (nc.vector if eng[1] == "v" else nc.gpsimd).tensor_tensor(
-                out=g_grouped[:, cols, :].rearrange("p (c i) t -> p c t i", i=4),
+            nc.scalar.activation(out=slope[:], in_=diff[gi], func=TANH)
+            (nc.vector if MID[gi][1] == "v" else nc.gpsimd).tensor_tensor(
+                out=runs_packed(dst),
                 in0=runs(slope[:]),
                 in1=runs(weight[c][:, :, i0 : i0 + GROUP]),
                 op=MULT,
             )
 
-        def quantize_g(c, i0, n):
-            c0 = CHUNKS[c][0]
+        def quantize_g(c, i0):
+            w = g_part[c, i0].shape[1]
             nc.vector.quantize_mx(
-                out=g_codes[c][:, i0 : i0 + n].bitcast(E5M2),
-                scales=g_scales[c][:, i0 : i0 + n],
-                in_=g_grouped[:, c0 + i0 : c0 + i0 + n, :].rearrange("p n t -> p (n t)"),
+                out=g_codes[c][:, i0 : i0 + w].bitcast(E5M2),
+                scales=g_scales[c][:, i0 : i0 + w],
+                in_=g_part[c, i0][:].rearrange("p n t -> p (n t)"),
             )
 
+        def weigh_chunk(c):
+            n = CHUNKS[c][1]
+            for p0 in range(0, n, PIECE):
+                w = min(PIECE, n - p0)
+                g_part[c, p0] = keep.tile([P, w, PACK], BF16, name="g_part", tag="g_first" if p0 == 0 else "g_rest%d" % c, align_bytes=64)
+                for i0 in range(0, w, GROUP):
+                    weigh(c, p0 + i0, g_part[c, p0][:, i0 : i0 + GROUP, :])
+            for p0 in range(0, n, PIECE):
+                quantize_g(c, p0)
+
+        def subtract_chunk(c, tag):
+            c0, n = CHUNKS[c]
+            diffs = keep.tile([P, n // GROUP, PACK, GROUP], F32, name="diffs", tag=tag, align_bytes=64)
+            return [subtract((c0 + i0) // GROUP, diffs[:, i0 // GROUP, :, :]) for i0 in range(0, n, GROUP)]
+
+        dx_ps = {}
         dx_sb = {}
 
         def second(c, j):
-            c0, n = CHUNKS[c]
-            dx = psum.tile([P, BANK], F32, name="dx")
+            dx_ps[c, j] = psum.tile([P, BANK], F32, name="dx")
             nc.tensor.matmul_mx(
-                out=dx[:],
+                out=dx_ps[c, j][:],
                 lhsT=wv_codes[:, j * P : (j + 1) * P].bitcast(E4M3),
                 lhsT_scale=wv_scales[:, j * P : (j + 1) * P],
                 rhs=g_codes[c][:].bitcast(E5M2),
@@ -234,8 +240,12 @@ def tile_attend_gml_lch_kernel(tc, xT, wd, wv, y, cw, rw, offs, out):
                 start=True,
                 stop=True,
             )
-            dx_sb[c, j] = keep.tile([P, n], F32, name="dx_sb%d_%d" % (c, j))
-            nc.scalar.activation(out=dx_sb[c, j][:], in_=dx[:, :n], func=COPY)
+
+        def evacuate(c, j):
+            n = CHUNKS[c][1]
+            late = j == LATE[c]
+            dx_sb[c, j] = keep.tile([P, n], F32, name="dx_sb", tag=("weight%d" % (c + 1)) if late else "dx_sb%d_%d" % (c, j))
+            nc.scalar.activation(out=dx_sb[c, j][:], in_=dx_ps[c, j][:, :n], func=COPY)
 
         def place(c, j):
             c0, n = CHUNKS[c]
@@ -243,30 +253,42 @@ def tile_attend_gml_lch_kernel(tc, xT, wd, wv, y, cw, rw, offs, out):
             if c == len(CHUNKS) - 1:
                 nc.sync.dma_start(out[j * P : (j + 1) * P, :], placed[j][:])
 
-        def front(c):
-            c0, n = CHUNKS[c]
-            if c > 0:
-                make_weight(c)
-            for i0 in range(0, n, GROUP):
-                middle(c, i0)
-                if c == 0 and i0 == 0:
-                    prepare_wv(0)
-            i0 = 0
-            for w in (512, 256, 128):
-                if n - i0 >= w:
-                    quantize_g(c, i0, w)
-                    i0 += w
-            for j in range(D // P):
-                if c == 0 and j > 0:
-                    prepare_wv(j)
-                second(c, j)
-
-        front(0)
-        for c0 in range(PIECE, N, PIECE):
-            gather(1, c0)
-            quantize_x(c0)
-        for c in range(len(CHUNKS)):
-            if c + 1 < len(CHUNKS):
-                front(c + 1)
-            for j in range(D // P):
+        subtract_chunk(0, "diffs0")
+        prepare_wv(0)
+        weigh_chunk(0)
+        for j in range(2):
+            second(0, j)
+            evacuate(0, j)
+        prepare_wv(1)
+        for j in range(2, 4):
+            second(0, j)
+            if j < LATE[0]:
+                evacuate(0, j)
+        for c0, n in QX[1:]:
+            quantize_x(c0, n)
+        make_weight(1)
+        for f in subtract_chunk(1, "diffs1"):
+            if f:
+                f()
+        weigh_chunk(1)
+        for f in subtract_chunk(2, "g_rest1"):
+            if f:
+                f()
+        for j in range(LATE[0], 4):
+            evacuate(0, j)
+        make_weight(2)
+        for j in range(4):
+            second(1, j)
+            if j < LATE[1]:
+                evacuate(1, j)
+        for j in range(4):
+            place(0, j)
+        weigh_chunk(2)
+        for j in range(LATE[1], 4):
+            evacuate(1, j)
+        for j in range(4):
+            second(2, j)
+            evacuate(2, j)
+        for c in (1, 2):
+            for j in range(4):
                 place(c, j)

@@ -24,12 +24,12 @@ GROUP = 128
 PIECE = 256
 BANK = 512
 HALF = 256
-X_COLS = 512
-X_TAIL_VEC = 320
+X_LOADS = [[(0, 1024, 512), (1024, 1024, 704)], [(0, 1024, 0), (1024, 1024, 704)]]
 CHUNKS = [(0, 256), (256, 384), (640, 384)]
-LATE = [2, 3, 9]
-MID = ["vv"] * 2 + ["vg"] * 3 + ["gg"] * 3
-LATE_LOADS = [("wd", 0), ("wd", 1), ("y", 0), ("rw", 1), ("wv", 0), ("y", 1), ("wv", 1), ("y", 2), ("rw", 2), ("y", 3)]
+LATE = [3, 3, 9]
+WENG = "sss"
+MID = ["vv"] * 2 + ["vg"] * 4 + ["gg"] * 2
+LATE_LOADS = [("wd", 0), ("wd", 1), ("y", 0), ("cw", 0), ("rw", (0, 256)), ("rw", (256, 640)), ("wv", 0), ("y", 1), ("wv", 1), ("y", 2), ("rw", (640, 1024)), ("y", 3)]
 QX = [(0, 256), (256, 256), (512, 512)]
 
 
@@ -53,7 +53,8 @@ def tile_attend_gml_lch_kernel(tc, xT, wd, wv, y, cw, rw, offs, out):
 
         offsets = keep.tile([P, N // 16], U16, name="offsets")
         cw_sb = keep.tile([P, PACK], F32, name="cw_sb")
-        rw_sb = [keep.tile([P, n], F32, name="rw%d" % c) for c, (c0, n) in enumerate(CHUNKS)]
+        rw_all = keep.tile([P, N], F32, name="rw_all")
+        rw_sb = [rw_all[:, c0 : c0 + n] for c0, n in CHUNKS]
         y_sb = [keep.tile([P, PACK, PIECE], F32, name="y%d" % k) for k in range(N // PIECE)]
         wd_raw = [keep.tile([P, PACK, HALF], F32, name="wd_raw%d" % h) for h in range(2)]
         wv_raw = [keep.tile([P, PACK, HALF], F32, name="wv_raw%d" % h) for h in range(2)]
@@ -64,8 +65,7 @@ def tile_attend_gml_lch_kernel(tc, xT, wd, wv, y, cw, rw, offs, out):
 
         def load(kind, k):
             if kind == "rw":
-                c0, n = CHUNKS[k]
-                nc.sync.dma_start(rw_sb[k][:], rw[:, c0 : c0 + n])
+                nc.sync.dma_start(rw_all[:, k[0] : k[1]], rw[:, k[0] : k[1]])
             elif kind == "cw":
                 nc.sync.dma_start(cw_sb[:], cw.rearrange("(p t) o -> p (t o)", t=PACK))
             else:
@@ -74,35 +74,40 @@ def tile_attend_gml_lch_kernel(tc, xT, wd, wv, y, cw, rw, offs, out):
 
         x_raw = {}
         for u in range(2):
-            for n0 in range(0, T, X_COLS):
-                x_raw[u, n0] = keep.tile([P, 2, X_COLS], F32, name="x_raw%d_%d" % (u, n0))
-                nc.sync.dma_start(x_raw[u, n0][:], x_rows[:, u, :, n0 : n0 + X_COLS])
+            for n0, n, nv in X_LOADS[u]:
+                x_raw[u, n0] = keep.tile([P, 2, n], F32, name="x_raw%d_%d" % (u, n0))
+                nc.sync.dma_start(x_raw[u, n0][:], x_rows[:, u, :, n0 : n0 + n])
                 if (u, n0) == (0, 0):
                     nc.sync.dma_start(offsets[:], offs)
-                    load("cw", 0)
-                    load("rw", 0)
+                    pass
         for kind, k in LATE_LOADS:
             load(kind, k)
 
         def listed(c0, n):
             return offsets[:, c0 // 16 : (c0 + n) // 16]
 
-        placed = [keep.tile([P, T], F32, name="placed%d" % j) for j in range(D // P)]
-        for j in range(D // P):
+        placed = [keep.tile([P, T], F32, name="placed%d" % j) for j in range(2)]
+        for j in range(2):
             nc.vector.memset(placed[j][:].bitcast(U32), 0)
+        placed.append(keep.tile([P, T], F32, name="placed2"))
+        nc.vector.memset(placed[2][:].bitcast(U32), 0)
+        placed.append(keep.tile([P, T], F32, name="placed3"))
+        nc.vector.memset(placed[3][:].bitcast(U32), 0)
         g_codes = [keep.tile([P, BANK], U32, name="g_codes%d" % c, align_bytes=64) for c in range(len(CHUNKS))]
         g_scales = [keep.tile([P, BANK], U8, name="g_scales%d" % c, align_bytes=64) for c in range(len(CHUNKS))]
         for c, (c0, n) in enumerate(CHUNKS):
             if n < BANK:
-                nc.gpsimd.memset(g_codes[c][:, n:], 0)
-                nc.gpsimd.memset(g_scales[c][:, n:].bitcast(U32), 0)
+                nc.vector.memset(g_codes[c][:, n:], 0)
+                nc.vector.memset(g_scales[c][:, n:].bitcast(U32), 0)
 
         weight = [keep.tile([P, PACK, n], F32, name="weight%d" % c) for c, (c0, n) in enumerate(CHUNKS)]
 
         def make_weight(c):
             for t in range(PACK):
-                if c == 0 and True:
+                if WENG[c] == "g":
                     nc.gpsimd.tensor_scalar(out=weight[c][:, t, :], in0=rw_sb[c][:], scalar1=cw_sb[:, t : t + 1], scalar2=0.0, op0=MULT, op1=ADD)
+                elif WENG[c] == "v":
+                    nc.vector.tensor_scalar(out=weight[c][:, t, :], in0=rw_sb[c][:], scalar1=cw_sb[:, t : t + 1], scalar2=None, op0=MULT)
                 else:
                     nc.scalar.activation(out=weight[c][:, t, :], in_=rw_sb[c][:], func=COPY, scale=cw_sb[:, t : t + 1])
 
@@ -124,13 +129,14 @@ def tile_attend_gml_lch_kernel(tc, xT, wd, wv, y, cw, rw, offs, out):
             )
 
         for u in range(2):
-            for n0 in range(0, T, X_COLS):
-                cut = X_COLS - (X_TAIL_VEC if (u, n0) == (1, T - X_COLS) else 0)
-                nc.scalar.activation(out=runs_packed(pairs[u][:, n0 : n0 + cut, :]), in_=runs(x_raw[u, n0][:, :, :cut]), func=COPY)
-                if cut < X_COLS:
-                    nc.vector.tensor_copy(out=runs_packed(pairs[u][:, n0 + cut : n0 + X_COLS, :]), in_=runs(x_raw[u, n0][:, :, cut:]))
-            for c0 in range(0, N, 256):
-                nc.vector.tensor_copy(out=x_words[:, c0 : c0 + 256, u], in_=windows[u].indirect(listed(c0, 256)))
+            for n0, n, nv in X_LOADS[u]:
+                cut = n - nv
+                if cut > 0:
+                    nc.scalar.activation(out=pairs[u][:, n0 : n0 + cut, :], in_=x_raw[u, n0][:, :, :cut].rearrange("p e n -> p n e"), func=COPY)
+                if cut < n:
+                    nc.vector.tensor_copy(out=pairs[u][:, n0 + cut : n0 + n, :], in_=x_raw[u, n0][:, :, cut:].rearrange("p e n -> p n e"))
+            for c0 in range(0, N, 512):
+                nc.vector.tensor_copy(out=x_words[:, c0 : c0 + 512, u], in_=windows[u].indirect(listed(c0, 512)))
         quantize_x(*QX[0])
 
         wd_grouped = keep.tile([P, PACK, P, PACK], BF16, name="wd_grouped", align_bytes=64)
@@ -223,8 +229,18 @@ def tile_attend_gml_lch_kernel(tc, xT, wd, wv, y, cw, rw, offs, out):
 
         def subtract_chunk(c, tag):
             c0, n = CHUNKS[c]
-            diffs = keep.tile([P, n // GROUP, PACK, GROUP], F32, name="diffs", tag=tag, align_bytes=64)
-            return [subtract((c0 + i0) // GROUP, diffs[:, i0 // GROUP, :, :]) for i0 in range(0, n, GROUP)]
+            groups = list(range(c0 // GROUP, (c0 + n) // GROUP))
+            late = [gi for gi in groups if MID[gi][0] == "g"]
+            if late:
+                diffs = keep.tile([P, len(late), PACK, GROUP], F32, name="diffs", tag=tag, align_bytes=64)
+            todo = []
+            for gi in groups:
+                if gi in late:
+                    todo.append(subtract(gi, diffs[:, late.index(gi), :, :]))
+                else:
+                    early = keep.tile([P, PACK, GROUP], F32, name="diff%d" % gi)
+                    todo.append(subtract(gi, early[:]))
+            return todo
 
         dx_ps = {}
         dx_sb = {}

@@ -15,8 +15,9 @@ E5M2 = mybir.dt.float8_e5m2_x4
 COPY = mybir.ActivationFunctionType.Copy
 TANH = mybir.ActivationFunctionType.Tanh
 MULT = mybir.AluOpType.mult
-ADD = mybir.AluOpType.add
 SUB = mybir.AluOpType.subtract
+ADD = mybir.AluOpType.add
+EQUAL = mybir.AluOpType.is_equal
 
 P = 128
 PACK = 4
@@ -24,21 +25,21 @@ GROUP = 128
 PIECE = 256
 BANK = 512
 HALF = 256
-X_LOADS = [[(0, 1024, 512), (1024, 1024, 704)], [(0, 1024, 0), (1024, 1024, 704)]]
+RUN = N // P
+QUAD = 32
+X_LOADS = [[(0, 1024, 0), (1024, 1024, 704)], [(0, 1024, 0), (1024, 1024, 704)]]
 CHUNKS = [(0, 256), (256, 384), (640, 384)]
-LATE = [3, 3, 9]
-WENG = "sss"
-MID = ["vv"] * 2 + ["vg"] * 4 + ["gg"] * 2
-LATE_LOADS = [("wd", 0), ("wd", 1), ("y", 0), ("cw", 0), ("rw", (0, 256)), ("rw", (256, 640)), ("wv", 0), ("y", 1), ("wv", 1), ("y", 2), ("rw", (640, 1024)), ("y", 3)]
-QX = [(0, 256), (256, 256), (512, 512)]
+LAP = 16
 
 
 def tile_attend_gml_lch_kernel(tc, xT, wd, wv, y, cw, rw, offs, out):
     nc = tc.nc
     with ExitStack() as ctx:
         keep = ctx.enter_context(tc.tile_pool(name="keep", bufs=1))
-        ring = ctx.enter_context(tc.tile_pool(name="ring", bufs=4))
         psum = ctx.enter_context(tc.psum_pool(name="psum", bufs=4))
+
+        def held(shape, dtype, name, tag=None):
+            return keep.tile(shape, dtype, name=name, tag=tag or name, align_bytes=64)
 
         def runs(ap):
             return ap.rearrange("p t (c i) -> p c t i", i=4)
@@ -46,80 +47,89 @@ def tile_attend_gml_lch_kernel(tc, xT, wd, wv, y, cw, rw, offs, out):
         def runs_packed(ap):
             return ap.rearrange("p (c i) t -> p c t i", i=4)
 
-        warm = keep.tile([P, 8], F32, name="warm")
-        warm_out = keep.tile([P, 8], F32, name="warm_out")
+        warm = held([P, 8], F32, name="warm")
+        warm_out = held([P, 8], F32, name="warm_out")
         nc.vector.memset(warm[:], 0.0)
         nc.scalar.activation(out=warm_out[:], in_=warm[:], func=TANH)
 
-        offsets = keep.tile([P, N // 16], U16, name="offsets")
-        cw_sb = keep.tile([P, PACK], F32, name="cw_sb")
-        rw_all = keep.tile([P, N], F32, name="rw_all")
-        rw_sb = [rw_all[:, c0 : c0 + n] for c0, n in CHUNKS]
-        y_sb = [keep.tile([P, PACK, PIECE], F32, name="y%d" % k) for k in range(N // PIECE)]
-        wd_raw = [keep.tile([P, PACK, HALF], F32, name="wd_raw%d" % h) for h in range(2)]
-        wv_raw = [keep.tile([P, PACK, HALF], F32, name="wv_raw%d" % h) for h in range(2)]
+        offsets = held([P, N // 16], U16, name="offsets")
+        cw_sb = held([P, PACK], F32, name="cw_sb")
+        rw_col = held([P, RUN], F32, name="rw_col")
+        rw_all = held([P, N], F32, name="rw_all")
+        y_sb = [held([P, PACK, n], F32, name="y%d" % c) for c, (c0, n) in enumerate(CHUNKS)]
+        wd_raw = held([P, PACK, V], F32, name="wd_raw")
+        wv_raw = held([P, PACK, D], F32, name="wv_raw")
         x_rows = xT.rearrange("(p u e) n -> p u e n", u=2, e=2)
         y_rows = y.rearrange("(p t) n -> p t n", t=PACK)
-        wd_rows = wd.rearrange("(p j) v -> p j v", j=PACK)
-        wv_rows = wv.rearrange("(p t) d -> p t d", t=PACK)
 
-        def load(kind, k):
-            if kind == "rw":
-                nc.sync.dma_start(rw_all[:, k[0] : k[1]], rw[:, k[0] : k[1]])
-            elif kind == "cw":
-                nc.sync.dma_start(cw_sb[:], cw.rearrange("(p t) o -> p (t o)", t=PACK))
-            else:
-                tiles, rows = {"y": (y_sb, y_rows), "wd": (wd_raw, wd_rows), "wv": (wv_raw, wv_rows)}[kind]
-                nc.sync.dma_start(tiles[k][:], rows[:, :, k * HALF : (k + 1) * HALF])
-
+        nc.sync.dma_start(rw_col[:], rw[0:1, :].rearrange("o (p e) -> p (o e)", e=RUN))
+        nc.sync.dma_start(cw_sb[:], cw.rearrange("(p t) o -> p (t o)", t=PACK))
         x_raw = {}
         for u in range(2):
             for n0, n, nv in X_LOADS[u]:
-                x_raw[u, n0] = keep.tile([P, 2, n], F32, name="x_raw%d_%d" % (u, n0))
+                x_raw[u, n0] = held([P, 2, n], F32, name="x_raw%d_%d" % (u, n0))
                 nc.sync.dma_start(x_raw[u, n0][:], x_rows[:, u, :, n0 : n0 + n])
-                if (u, n0) == (0, 0):
-                    nc.sync.dma_start(offsets[:], offs)
-                    pass
-        for kind, k in LATE_LOADS:
-            load(kind, k)
+            if u == 0:
+                nc.sync.dma_start(offsets[:], offs)
+        nc.sync.dma_start(wd_raw[:], wd.rearrange("(p j) v -> p j v", j=PACK))
+
+        def load_y(c):
+            c0, n = CHUNKS[c]
+            nc.sync.dma_start(y_sb[c][:], y_rows[:, :, c0 : c0 + n])
+
+        load_y(0)
+        nc.sync.dma_start(wv_raw[:], wv.rearrange("(p t) d -> p t d", t=PACK))
+        load_y(1)
+        load_y(2)
 
         def listed(c0, n):
             return offsets[:, c0 // 16 : (c0 + n) // 16]
 
-        placed = [keep.tile([P, T], F32, name="placed%d" % j) for j in range(2)]
-        for j in range(2):
+        ones = held([P, P], F32, name="ones")
+        column = held([P, P], F32, name="column")
+        row = held([P, QUAD], F32, name="row")
+        ident = held([P, P], F32, name="ident")
+        base = held([P, 1], F32, name="base")
+        nc.vector.memset(ones[:], 1.0)
+        for q0 in range(0, P, QUAD):
+            nc.vector.memset(base[q0 : q0 + QUAD, :], float(q0))
+        nc.vector.tensor_tensor_scan(out=column[:], data0=ones[:], data1=ones[:], initial=0.0, op0=MULT, op1=ADD)
+        nc.vector.transpose(out=row[:], in_=column[:, :QUAD])
+        nc.vector.tensor_scalar(out=ident[:], in0=column[:], scalar1=row[:, 0:1], scalar2=base[:], op0=SUB, op1=EQUAL)
+        placed = [held([P, T], F32, name="placed%d" % j, tag=tag) for j, tag in enumerate(["column", "row", "base", "ident"])]
+        lead = BANK - CHUNKS[0][1]
+        g_codes = held([P, lead + N], U32, name="g_codes")
+        g_scales = held([P, lead + N], U8, name="g_scales")
+        nc.vector.memset(g_codes[:, :lead], 0)
+        nc.vector.memset(g_scales[:, :lead].bitcast(U32), 0)
+
+        rw_runs = rw_all[:].rearrange("p (n e) -> p n e", e=RUN)
+        for e0 in range(0, RUN, PACK):
+            spread = psum.tile([P, PACK, P], F32, name="spread", tag="a")
+            for e in range(PACK):
+                nc.tensor.transpose(out=spread[:, e, :], in_=rw_col[:, e0 + e : e0 + e + 1].to_broadcast([P, P]), identity=ident[:])
+            nc.scalar.activation(out=rw_runs[:, :, e0 : e0 + PACK], in_=spread[:].rearrange("p e n -> p n e"), func=COPY)
+
+        for j in range(PACK):
             nc.vector.memset(placed[j][:].bitcast(U32), 0)
-        placed.append(keep.tile([P, T], F32, name="placed2"))
-        nc.vector.memset(placed[2][:].bitcast(U32), 0)
-        placed.append(keep.tile([P, T], F32, name="placed3"))
-        nc.vector.memset(placed[3][:].bitcast(U32), 0)
-        g_codes = [keep.tile([P, BANK], U32, name="g_codes%d" % c, align_bytes=64) for c in range(len(CHUNKS))]
-        g_scales = [keep.tile([P, BANK], U8, name="g_scales%d" % c, align_bytes=64) for c in range(len(CHUNKS))]
-        for c, (c0, n) in enumerate(CHUNKS):
-            if n < BANK:
-                nc.vector.memset(g_codes[c][:, n:], 0)
-                nc.vector.memset(g_scales[c][:, n:].bitcast(U32), 0)
 
-        weight = [keep.tile([P, PACK, n], F32, name="weight%d" % c) for c, (c0, n) in enumerate(CHUNKS)]
+        weight = {}
 
-        def make_weight(c):
+        def make_weight(k, tag):
+            weight[k] = held([P, PACK, PIECE], F32, name="weight%d" % k, tag=tag)
             for t in range(PACK):
-                if WENG[c] == "g":
-                    nc.gpsimd.tensor_scalar(out=weight[c][:, t, :], in0=rw_sb[c][:], scalar1=cw_sb[:, t : t + 1], scalar2=0.0, op0=MULT, op1=ADD)
-                elif WENG[c] == "v":
-                    nc.vector.tensor_scalar(out=weight[c][:, t, :], in0=rw_sb[c][:], scalar1=cw_sb[:, t : t + 1], scalar2=None, op0=MULT)
-                else:
-                    nc.scalar.activation(out=weight[c][:, t, :], in_=rw_sb[c][:], func=COPY, scale=cw_sb[:, t : t + 1])
+                nc.scalar.activation(out=weight[k][:, t, :], in_=rw_all[:, k * PIECE : (k + 1) * PIECE], func=COPY, scale=cw_sb[:, t : t + 1])
 
-        pairs = [keep.tile([P, T, 2], BF16, name="pairs%d" % u, align_bytes=64) for u in range(2)]
+        pairs = [held([P, T, 2], BF16, name="pairs%d" % u) for u in range(2)]
         windows = [pairs[u][:].rearrange("p n e -> p (n e)").bitcast(U32) for u in range(2)]
-        x_grouped = keep.tile([P, N, PACK], BF16, name="x_grouped", align_bytes=64)
+        x_grouped = held([P, N, PACK], BF16, name="x_grouped")
         x_words = x_grouped[:].rearrange("p n j -> p (n j)").bitcast(U32).rearrange("p (n u) -> p n u", u=2)
-        x_codes = [keep.tile([P, PIECE], U32, name="x_codes", align_bytes=64)]
-        x_scales = keep.tile([P, N], U8, name="x_scales", align_bytes=64)
+        x_codes = {0: held([P, PIECE], U32, name="x_codes")}
+        x_scales = held([P, N], U8, name="x_scales")
 
         def x_codes_of(c0, n):
-            return (x_codes[0][:, c0 : c0 + n] if c0 < PIECE else x_codes[1][:, c0 - PIECE : c0 - PIECE + n]).bitcast(E4M3)
+            base = max(b for b in x_codes if b <= c0)
+            return x_codes[base][:, c0 - base : c0 - base + n].bitcast(E4M3)
 
         def quantize_x(c0, n):
             nc.vector.quantize_mx(
@@ -137,15 +147,16 @@ def tile_attend_gml_lch_kernel(tc, xT, wd, wv, y, cw, rw, offs, out):
                     nc.vector.tensor_copy(out=pairs[u][:, n0 + cut : n0 + n, :], in_=x_raw[u, n0][:, :, cut:].rearrange("p e n -> p n e"))
             for c0 in range(0, N, 512):
                 nc.vector.tensor_copy(out=x_words[:, c0 : c0 + 512, u], in_=windows[u].indirect(listed(c0, 512)))
-        quantize_x(*QX[0])
+            make_weight(u, "x_raw%d_%d" % (u, X_LOADS[u][-1][0]))
+        quantize_x(0, PIECE)
 
-        wd_grouped = keep.tile([P, PACK, P, PACK], BF16, name="wd_grouped", align_bytes=64)
-        wd_codes = keep.tile([P, V], U32, name="wd_codes", align_bytes=64)
-        wd_scales = keep.tile([P, V], U8, name="wd_scales", align_bytes=64)
+        wd_grouped = held([P, PACK, P, PACK], BF16, name="wd_grouped")
+        wd_codes = held([P, V], U32, name="wd_codes")
+        wd_scales = held([P, V], U8, name="wd_scales")
         for h in range(2):
             nc.scalar.activation(
                 out=wd_grouped[:, :, 64 * h : 64 * (h + 1), :].rearrange("p t m j -> p m j t"),
-                in_=wd_raw[h][:].rearrange("p j (m t) -> p m j t", t=PACK),
+                in_=wd_raw[:, :, h * HALF : (h + 1) * HALF].rearrange("p j (m t) -> p m j t", t=PACK),
                 func=COPY,
             )
         nc.vector.quantize_mx(
@@ -153,33 +164,27 @@ def tile_attend_gml_lch_kernel(tc, xT, wd, wv, y, cw, rw, offs, out):
             scales=wd_scales[:],
             in_=wd_grouped[:].rearrange("p t m j -> p (t m j)"),
         )
-        x_codes.append(keep.tile([P, N - PIECE], U32, name="x_codes_late", tag="wd_grouped", align_bytes=64))
-        make_weight(0)
+        make_weight(2, "wd_raw")
+        x_codes[PIECE] = held([P, 2 * PIECE], U32, name="x_codes_mid", tag="wd_grouped")
 
-        wv_grouped = keep.tile([P, D, PACK], BF16, name="wv_grouped", align_bytes=64)
-        wv_codes = keep.tile([P, D], U32, name="wv_codes", align_bytes=64)
-        wv_scales = keep.tile([P, D], U8, name="wv_scales", align_bytes=64)
+        wv_codes = held([P, D], U32, name="wv_codes")
+        wv_scales = held([P, D], U8, name="wv_scales")
 
-        def prepare_wv(h):
+        def prepare_wv(h, tag):
+            grouped = held([P, HALF, PACK], BF16, name="wv_grouped", tag=tag)
             for a in range(0, HALF, P):
-                nc.scalar.activation(
-                    out=runs_packed(wv_grouped[:, h * HALF + a : h * HALF + a + P, :]),
-                    in_=runs(wv_raw[h][:, :, a : a + P]),
-                    func=COPY,
-                )
+                nc.scalar.activation(out=runs_packed(grouped[:, a : a + P, :]), in_=runs(wv_raw[:, :, h * HALF + a : h * HALF + a + P]), func=COPY)
             nc.vector.quantize_mx(
                 out=wv_codes[:, h * HALF : (h + 1) * HALF].bitcast(E4M3),
                 scales=wv_scales[:, h * HALF : (h + 1) * HALF],
-                in_=wv_grouped[:, h * HALF : (h + 1) * HALF, :].rearrange("p d t -> p (d t)"),
+                in_=grouped[:].rearrange("p d t -> p (d t)"),
             )
 
         diff = {}
         g_part = {}
 
-        def subtract(gi, tile):
+        def scores(gi):
             c0 = gi * GROUP
-            k, y0 = divmod(c0, PIECE)
-            diff[gi] = tile
             a = psum.tile([P, PACK, GROUP], F32, name="a")
             for t in range(PACK):
                 nc.tensor.matmul_mx(
@@ -191,77 +196,77 @@ def tile_attend_gml_lch_kernel(tc, xT, wd, wv, y, cw, rw, offs, out):
                     start=True,
                     stop=True,
                 )
-            if MID[gi][0] == "v":
-                nc.vector.tensor_tensor(out=tile, in0=a[:], in1=y_sb[k][:, :, y0 : y0 + GROUP], op=SUB)
-            else:
-                a_sb = ring.tile([P, PACK, GROUP], F32, name="a_sb")
-                nc.scalar.activation(out=a_sb[:], in_=a[:], func=COPY)
-                return lambda: nc.gpsimd.tensor_tensor(out=tile, in0=a_sb[:], in1=y_sb[k][:, :, y0 : y0 + GROUP], op=SUB)
+            return a
 
-        def weigh(c, i0, dst):
-            gi = (CHUNKS[c][0] + i0) // GROUP
-            slope = ring.tile([P, PACK, GROUP], F32, name="slope")
-            nc.scalar.activation(out=slope[:], in_=diff[gi], func=TANH)
-            (nc.vector if MID[gi][1] == "v" else nc.gpsimd).tensor_tensor(
-                out=runs_packed(dst),
-                in0=runs(slope[:]),
-                in1=runs(weight[c][:, :, i0 : i0 + GROUP]),
+        def targets(gi):
+            c = max(c for c in range(len(CHUNKS)) if CHUNKS[c][0] <= gi * GROUP)
+            y0 = gi * GROUP - CHUNKS[c][0]
+            return y_sb[c][:, :, y0 : y0 + GROUP]
+
+        def subtract_on_vector(groups, tag):
+            tile = held([P, len(groups), PACK, GROUP], F32, name="diff_v", tag=tag)
+            for k, gi in enumerate(groups):
+                diff[gi] = tile[:, k, :, :]
+                nc.vector.tensor_tensor(out=diff[gi], in0=scores(gi)[:], in1=targets(gi), op=SUB)
+
+        def subtract_on_gpsimd(groups, stage_tag, tag):
+            staged = held([P, len(groups), PACK, GROUP], F32, name="staged", tag=stage_tag)
+            tile = held([P, len(groups), PACK, GROUP], F32, name="diff_g", tag=tag)
+            for k, gi in enumerate(groups):
+                nc.scalar.activation(out=staged[:, k, :, :], in_=scores(gi)[:], func=COPY)
+            for k, gi in enumerate(groups):
+                diff[gi] = tile[:, k, :, :]
+                nc.gpsimd.tensor_tensor(out=diff[gi], in0=staged[:, k, :, :], in1=targets(gi), op=SUB)
+
+        slope = {}
+
+        def bend(gi, tile, k):
+            slope[gi] = (tile, (gi - k) * GROUP)
+            nc.scalar.activation(out=tile[:, :, k * GROUP : (k + 1) * GROUP], in_=diff[gi], func=TANH)
+
+        def weigh(engine, c, lo, hi):
+            tile, base = slope[lo // GROUP]
+            w0 = lo // PIECE * PIECE
+            engine.tensor_tensor(
+                out=runs_packed(g_part[c][:, lo - CHUNKS[c][0] : hi - CHUNKS[c][0], :]),
+                in0=runs(tile[:, :, lo - base : hi - base]),
+                in1=runs(weight[lo // PIECE][:, :, lo - w0 : hi - w0]),
                 op=MULT,
             )
 
-        def quantize_g(c, i0):
-            w = g_part[c, i0].shape[1]
-            nc.vector.quantize_mx(
-                out=g_codes[c][:, i0 : i0 + w].bitcast(E5M2),
-                scales=g_scales[c][:, i0 : i0 + w],
-                in_=g_part[c, i0][:].rearrange("p n t -> p (n t)"),
-            )
-
-        def weigh_chunk(c):
-            n = CHUNKS[c][1]
-            for p0 in range(0, n, PIECE):
-                w = min(PIECE, n - p0)
-                g_part[c, p0] = keep.tile([P, w, PACK], BF16, name="g_part", tag="g_first" if p0 == 0 else "g_rest%d" % c, align_bytes=64)
-                for i0 in range(0, w, GROUP):
-                    weigh(c, p0 + i0, g_part[c, p0][:, i0 : i0 + GROUP, :])
-            for p0 in range(0, n, PIECE):
-                quantize_g(c, p0)
-
-        def subtract_chunk(c, tag):
+        def quantize_g(c, cut):
             c0, n = CHUNKS[c]
-            groups = list(range(c0 // GROUP, (c0 + n) // GROUP))
-            late = [gi for gi in groups if MID[gi][0] == "g"]
-            if late:
-                diffs = keep.tile([P, len(late), PACK, GROUP], F32, name="diffs", tag=tag, align_bytes=64)
-            todo = []
-            for gi in groups:
-                if gi in late:
-                    todo.append(subtract(gi, diffs[:, late.index(gi), :, :]))
-                else:
-                    early = keep.tile([P, PACK, GROUP], F32, name="diff%d" % gi)
-                    todo.append(subtract(gi, early[:]))
-            return todo
+            for lo, hi in ((c0, cut), (cut, c0 + n)):
+                if hi > lo:
+                    nc.vector.quantize_mx(
+                        out=g_codes[:, lead + lo : lead + hi].bitcast(E5M2),
+                        scales=g_scales[:, lead + lo : lead + hi],
+                        in_=g_part[c][:, lo - c0 : hi - c0, :].rearrange("p n t -> p (n t)"),
+                    )
+
+        for c, (c0, n) in enumerate(CHUNKS):
+            g_part[c] = held([P, n, PACK], BF16, name="g_part%d" % c)
 
         dx_ps = {}
         dx_sb = {}
 
         def second(c, j):
+            end = lead + sum(CHUNKS[c])
             dx_ps[c, j] = psum.tile([P, BANK], F32, name="dx")
             nc.tensor.matmul_mx(
                 out=dx_ps[c, j][:],
                 lhsT=wv_codes[:, j * P : (j + 1) * P].bitcast(E4M3),
                 lhsT_scale=wv_scales[:, j * P : (j + 1) * P],
-                rhs=g_codes[c][:].bitcast(E5M2),
-                rhs_scale=g_scales[c][:],
+                rhs=g_codes[:, end - BANK : end].bitcast(E5M2),
+                rhs_scale=g_scales[:, end - BANK : end],
                 start=True,
                 stop=True,
             )
 
-        def evacuate(c, j):
+        def evacuate(c, j, tag=None):
             n = CHUNKS[c][1]
-            late = j == LATE[c]
-            dx_sb[c, j] = keep.tile([P, n], F32, name="dx_sb", tag=("weight%d" % (c + 1)) if late else "dx_sb%d_%d" % (c, j))
-            nc.scalar.activation(out=dx_sb[c, j][:], in_=dx_ps[c, j][:, :n], func=COPY)
+            dx_sb[c, j] = held([P, n], F32, name="dx_sb", tag=tag or "dx_sb%d_%d" % (c, j))
+            nc.scalar.activation(out=dx_sb[c, j][:], in_=dx_ps[c, j][:, BANK - n :], func=COPY)
 
         def place(c, j):
             c0, n = CHUNKS[c]
@@ -269,42 +274,56 @@ def tile_attend_gml_lch_kernel(tc, xT, wd, wv, y, cw, rw, offs, out):
             if c == len(CHUNKS) - 1:
                 nc.sync.dma_start(out[j * P : (j + 1) * P, :], placed[j][:])
 
-        subtract_chunk(0, "diffs0")
-        prepare_wv(0)
-        weigh_chunk(0)
-        for j in range(2):
+        subtract_on_vector([0], "diff0")
+        subtract_on_vector([1], "diff1")
+        for gi in range(2):
+            bend(gi, held([P, PACK, GROUP], F32, name="slope%d" % gi), 0)
+            weigh(nc.vector, 0, gi * GROUP, (gi + 1) * GROUP)
+        quantize_g(0, 0)
+        prepare_wv(0, "wv_low")
+        prepare_wv(1, "diff0")
+        for j in range(4):
             second(0, j)
-            evacuate(0, j)
-        prepare_wv(1)
-        for j in range(2, 4):
-            second(0, j)
-            if j < LATE[0]:
-                evacuate(0, j)
-        for c0, n in QX[1:]:
-            quantize_x(c0, n)
-        make_weight(1)
-        for f in subtract_chunk(1, "diffs1"):
-            if f:
-                f()
-        weigh_chunk(1)
-        for f in subtract_chunk(2, "g_rest1"):
-            if f:
-                f()
-        for j in range(LATE[0], 4):
-            evacuate(0, j)
-        make_weight(2)
+        evacuate(0, 0)
+        quantize_x(PIECE, 2 * PIECE)
+        x_codes[3 * PIECE] = held([P, PIECE], U32, name="x_codes_end", tag="y0")
+        quantize_x(3 * PIECE, PIECE)
+        subtract_on_vector([2, 4], "g_part0")
+        subtract_on_gpsimd([3], "wv_raw", "diff0")
+        both = held([P, PACK, PIECE], F32, name="slope23")
+        bend(2, both, 0)
+        bend(4, held([P, PACK, GROUP], F32, name="slope4"), 0)
+        evacuate(0, 1)
+        bend(3, both, 1)
+        evacuate(0, 2)
+        weigh(nc.gpsimd, 1, 256, 384 - LAP)
+        weigh(nc.gpsimd, 1, 512, 640)
+        weigh(nc.gpsimd, 1, 384 - LAP, 512)
+        for j in range(3):
+            place(0, j)
+        quantize_g(1, 384)
+        make_weight(3, "g_part0")
+        subtract_on_gpsimd([5, 7, 6], "staged_late", "g_part1")
+        evacuate(0, 3, "slope23")
         for j in range(4):
             second(1, j)
-            if j < LATE[1]:
+            if j < 3:
                 evacuate(1, j)
-        for j in range(4):
-            place(0, j)
-        weigh_chunk(2)
-        for j in range(LATE[1], 4):
-            evacuate(1, j)
+        place(0, 3)
+        bend(5, held([P, PACK, GROUP], F32, name="slope5"), 0)
+        both = held([P, PACK, PIECE], F32, name="slope67")
+        bend(7, both, 1)
+        bend(6, both, 0)
+        weigh(nc.gpsimd, 2, 640, 768)
+        weigh(nc.gpsimd, 2, 896 + LAP, 1024)
+        weigh(nc.gpsimd, 2, 768, 896 + LAP)
+        for j in range(3):
+            place(1, j)
+        quantize_g(2, 896)
+        evacuate(1, 3, "slope67")
         for j in range(4):
             second(2, j)
             evacuate(2, j)
-        for c in (1, 2):
-            for j in range(4):
-                place(c, j)
+        place(1, 3)
+        for j in range(4):
+            place(2, j)

@@ -27,7 +27,11 @@ BANK = 512
 HALF = 256
 RUN = N // P
 QUAD = 32
-X_LOADS = [[(0, 1024, 0), (1024, 1024, 704)], [(0, 1024, 0), (1024, 1024, 704)]]
+X_LOADS = [[(0, 1024, 0), (1024, 1024, 704)], [(0, 1024, 0), (1024, 512, 512), (1536, 512, 352)]]
+WD_POOL = 32
+EARLY = 768
+TAIL = N - EARLY
+SPLIT = 2
 CHUNKS = [(0, 256), (256, 384), (640, 384)]
 LAP = 16
 
@@ -58,7 +62,8 @@ def tile_attend_gml_lch_kernel(tc, xT, wd, wv, y, cw, rw, offs, out):
         rw_all = held([P, N], F32, name="rw_all")
         y_sb = [held([P, PACK, n], F32, name="y%d" % c) for c, (c0, n) in enumerate(CHUNKS)]
         wd_raw = held([P, PACK, V], F32, name="wd_raw")
-        wv_raw = held([P, PACK, D], F32, name="wv_raw")
+        tail = held([P, 2, TAIL], U32, name="tail")
+        wv_raw = [held([P, PACK, HALF], F32, name="wv_raw%d" % h) for h in range(2)]
         x_rows = xT.rearrange("(p u e) n -> p u e n", u=2, e=2)
         y_rows = y.rearrange("(p t) n -> p t n", t=PACK)
 
@@ -77,8 +82,10 @@ def tile_attend_gml_lch_kernel(tc, xT, wd, wv, y, cw, rw, offs, out):
             c0, n = CHUNKS[c]
             nc.sync.dma_start(y_sb[c][:], y_rows[:, :, c0 : c0 + n])
 
+        wv_rows = wv.rearrange("(p t) d -> p t d", t=PACK)
+        nc.sync.dma_start(wv_raw[0][:], wv_rows[:, :, :HALF])
         load_y(0)
-        nc.sync.dma_start(wv_raw[:], wv.rearrange("(p t) d -> p t d", t=PACK))
+        nc.sync.dma_start(wv_raw[1][:], wv_rows[:, :, HALF:])
         load_y(1)
         load_y(2)
 
@@ -115,16 +122,18 @@ def tile_attend_gml_lch_kernel(tc, xT, wd, wv, y, cw, rw, offs, out):
 
         weight = {}
 
-        def make_weight(k, tag):
-            weight[k] = held([P, PACK, PIECE], F32, name="weight%d" % k, tag=tag)
+        def make_weight(c, tag):
+            c0, n = CHUNKS[c]
+            weight[c] = held([P, PACK, n], F32, name="weight%d" % c, tag=tag)
             for t in range(PACK):
-                nc.scalar.activation(out=weight[k][:, t, :], in_=rw_all[:, k * PIECE : (k + 1) * PIECE], func=COPY, scale=cw_sb[:, t : t + 1])
+                nc.scalar.activation(out=weight[c][:, t, :], in_=rw_all[:, c0 : c0 + n], func=COPY, scale=cw_sb[:, t : t + 1])
 
         pairs = [held([P, T, 2], BF16, name="pairs%d" % u) for u in range(2)]
         windows = [pairs[u][:].rearrange("p n e -> p (n e)").bitcast(U32) for u in range(2)]
         x_grouped = held([P, N, PACK], BF16, name="x_grouped")
         x_words = x_grouped[:].rearrange("p n j -> p (n j)").bitcast(U32).rearrange("p (n u) -> p n u", u=2)
         x_codes = {0: held([P, PIECE], U32, name="x_codes")}
+
         x_scales = held([P, N], U8, name="x_scales")
 
         def x_codes_of(c0, n):
@@ -145,50 +154,54 @@ def tile_attend_gml_lch_kernel(tc, xT, wd, wv, y, cw, rw, offs, out):
                     nc.scalar.activation(out=pairs[u][:, n0 : n0 + cut, :], in_=x_raw[u, n0][:, :, :cut].rearrange("p e n -> p n e"), func=COPY)
                 if cut < n:
                     nc.vector.tensor_copy(out=pairs[u][:, n0 + cut : n0 + n, :], in_=x_raw[u, n0][:, :, cut:].rearrange("p e n -> p n e"))
-            for c0 in range(0, N, 512):
-                nc.vector.tensor_copy(out=x_words[:, c0 : c0 + 512, u], in_=windows[u].indirect(listed(c0, 512)))
+            for c0, n in ((0, PIECE), (PIECE, EARLY - PIECE)):
+                nc.vector.tensor_copy(out=x_words[:, c0 : c0 + n, u], in_=windows[u].indirect(listed(c0, n)))
+            nc.vector.tensor_copy(out=tail[:, u, :], in_=windows[u].indirect(listed(EARLY, N - EARLY)))
             make_weight(u, "x_raw%d_%d" % (u, X_LOADS[u][-1][0]))
         quantize_x(0, PIECE)
 
         wd_grouped = held([P, PACK, P, PACK], BF16, name="wd_grouped")
         wd_codes = held([P, V], U32, name="wd_codes")
         wd_scales = held([P, V], U8, name="wd_scales")
-        for h in range(2):
-            nc.scalar.activation(
-                out=wd_grouped[:, :, 64 * h : 64 * (h + 1), :].rearrange("p t m j -> p m j t"),
-                in_=wd_raw[:, :, h * HALF : (h + 1) * HALF].rearrange("p j (m t) -> p m j t", t=PACK),
-                func=COPY,
-            )
+        cut = P - WD_POOL
+        nc.scalar.activation(
+            out=wd_grouped[:, :, :cut, :].rearrange("p t m j -> p m j t"),
+            in_=wd_raw[:, :, : PACK * cut].rearrange("p j (m t) -> p m j t", t=PACK),
+            func=COPY,
+        )
+        if WD_POOL:
+            nc.gpsimd.tensor_copy(out=wd_grouped[:, :, cut:, :], in_=wd_raw[:, :, PACK * cut :].rearrange("p j (m t) -> p t m j", t=PACK))
         nc.vector.quantize_mx(
             out=wd_codes[:].bitcast(E4M3),
             scales=wd_scales[:],
             in_=wd_grouped[:].rearrange("p t m j -> p (t m j)"),
         )
-        make_weight(2, "wd_raw")
-        x_codes[PIECE] = held([P, 2 * PIECE], U32, name="x_codes_mid", tag="wd_grouped")
+        x_codes[PIECE] = held([P, N - PIECE], U32, name="x_codes_late", tag="wd_raw")
+        quantize_x(PIECE, EARLY - PIECE)
+        nc.scalar.copy(out=x_words[:, EARLY:, :], in_=tail[:].rearrange("p u n -> p n u"))
 
         wv_codes = held([P, D], U32, name="wv_codes")
         wv_scales = held([P, D], U8, name="wv_scales")
 
-        def prepare_wv(h, tag):
-            grouped = held([P, HALF, PACK], BF16, name="wv_grouped", tag=tag)
-            for a in range(0, HALF, P):
-                nc.scalar.activation(out=runs_packed(grouped[:, a : a + P, :]), in_=runs(wv_raw[:, :, h * HALF + a : h * HALF + a + P]), func=COPY)
+        def prepare_wv(d0, n, tag):
+            grouped = held([P, n, PACK], BF16, name="wv_grouped", tag=tag)
+            for a in range(0, n, P):
+                nc.scalar.activation(out=runs_packed(grouped[:, a : a + P, :]), in_=runs(wv_raw[d0 // HALF][:, :, a : a + P]), func=COPY)
             nc.vector.quantize_mx(
-                out=wv_codes[:, h * HALF : (h + 1) * HALF].bitcast(E4M3),
-                scales=wv_scales[:, h * HALF : (h + 1) * HALF],
+                out=wv_codes[:, d0 : d0 + n].bitcast(E4M3),
+                scales=wv_scales[:, d0 : d0 + n],
                 in_=grouped[:].rearrange("p d t -> p (d t)"),
             )
 
         diff = {}
         g_part = {}
 
-        def scores(gi):
+        def scores(gi, t0=0, count=PACK):
             c0 = gi * GROUP
-            a = psum.tile([P, PACK, GROUP], F32, name="a")
-            for t in range(PACK):
+            a = psum.tile([P, count, GROUP], F32, name="a")
+            for t in range(t0, t0 + count):
                 nc.tensor.matmul_mx(
-                    out=a[:, t, :],
+                    out=a[:, t - t0, :],
                     lhsT=wd_codes[:, t * P : (t + 1) * P].bitcast(E4M3),
                     lhsT_scale=wd_scales[:, t * P : (t + 1) * P],
                     rhs=x_codes_of(c0, GROUP),
@@ -226,11 +239,11 @@ def tile_attend_gml_lch_kernel(tc, xT, wd, wv, y, cw, rw, offs, out):
 
         def weigh(engine, c, lo, hi):
             tile, base = slope[lo // GROUP]
-            w0 = lo // PIECE * PIECE
+            w0 = CHUNKS[c][0]
             engine.tensor_tensor(
                 out=runs_packed(g_part[c][:, lo - CHUNKS[c][0] : hi - CHUNKS[c][0], :]),
                 in0=runs(tile[:, :, lo - base : hi - base]),
-                in1=runs(weight[lo // PIECE][:, :, lo - w0 : hi - w0]),
+                in1=runs(weight[c][:, :, lo - w0 : hi - w0]),
                 op=MULT,
             )
 
@@ -274,22 +287,24 @@ def tile_attend_gml_lch_kernel(tc, xT, wd, wv, y, cw, rw, offs, out):
             if c == len(CHUNKS) - 1:
                 nc.sync.dma_start(out[j * P : (j + 1) * P, :], placed[j][:])
 
-        subtract_on_vector([0], "diff0")
-        subtract_on_vector([1], "diff1")
+        step = PACK // SPLIT
         for gi in range(2):
-            bend(gi, held([P, PACK, GROUP], F32, name="slope%d" % gi), 0)
+            slope[gi] = (held([P, PACK, GROUP], F32, name="slope%d" % gi), gi * GROUP)
+            for t0 in range(0, PACK, step):
+                part = held([P, step, GROUP], F32, name="diff%d_%d" % (gi, t0))
+                nc.vector.tensor_tensor(out=part[:], in0=scores(gi, t0, step)[:], in1=targets(gi)[:, t0 : t0 + step, :], op=SUB)
+                nc.scalar.activation(out=slope[gi][0][:, t0 : t0 + step, :], in_=part[:], func=TANH)
+        for gi in range(2):
             weigh(nc.vector, 0, gi * GROUP, (gi + 1) * GROUP)
         quantize_g(0, 0)
-        prepare_wv(0, "wv_low")
-        prepare_wv(1, "diff0")
+        prepare_wv(0, HALF, "wv_low")
+        prepare_wv(HALF, HALF, "diff1_0")
         for j in range(4):
             second(0, j)
         evacuate(0, 0)
-        quantize_x(PIECE, 2 * PIECE)
-        x_codes[3 * PIECE] = held([P, PIECE], U32, name="x_codes_end", tag="y0")
-        quantize_x(3 * PIECE, PIECE)
+        quantize_x(EARLY, N - EARLY)
         subtract_on_vector([2, 4], "g_part0")
-        subtract_on_gpsimd([3], "wv_raw", "diff0")
+        subtract_on_gpsimd([3], "wv_raw0", "diff1_0")
         both = held([P, PACK, PIECE], F32, name="slope23")
         bend(2, both, 0)
         bend(4, held([P, PACK, GROUP], F32, name="slope4"), 0)
@@ -302,7 +317,7 @@ def tile_attend_gml_lch_kernel(tc, xT, wd, wv, y, cw, rw, offs, out):
         for j in range(3):
             place(0, j)
         quantize_g(1, 384)
-        make_weight(3, "g_part0")
+        make_weight(2, "g_part0")
         subtract_on_gpsimd([5, 7, 6], "staged_late", "g_part1")
         evacuate(0, 3, "slope23")
         for j in range(4):

@@ -28,7 +28,7 @@ HALF = 256
 RUN = N // P
 QUAD = 32
 X_LOADS = [[(0, 1024, 0), (1024, 1024, 704)], [(0, 1024, 0), (1024, 512, 512), (1536, 512, 352)]]
-WD_POOL = 32
+WD_POOL = 64
 EARLY = 768
 TAIL = N - EARLY
 SPLIT = 2
@@ -130,7 +130,7 @@ def tile_attend_gml_lch_kernel(tc, xT, wd, wv, y, cw, rw, offs, out):
 
         pairs = [held([P, T, 2], BF16, name="pairs%d" % u) for u in range(2)]
         windows = [pairs[u][:].rearrange("p n e -> p (n e)").bitcast(U32) for u in range(2)]
-        x_grouped = held([P, N, PACK], BF16, name="x_grouped")
+        x_grouped = held([P, EARLY, PACK], BF16, name="x_grouped")
         x_words = x_grouped[:].rearrange("p n j -> p (n j)").bitcast(U32).rearrange("p (n u) -> p n u", u=2)
         x_codes = {0: held([P, PIECE], U32, name="x_codes")}
 
@@ -140,11 +140,11 @@ def tile_attend_gml_lch_kernel(tc, xT, wd, wv, y, cw, rw, offs, out):
             base = max(b for b in x_codes if b <= c0)
             return x_codes[base][:, c0 - base : c0 - base + n].bitcast(E4M3)
 
-        def quantize_x(c0, n):
+        def quantize_x(c0, n, source=None):
             nc.vector.quantize_mx(
                 out=x_codes_of(c0, n),
                 scales=x_scales[:, c0 : c0 + n],
-                in_=x_grouped[:, c0 : c0 + n, :].rearrange("p n j -> p (n j)"),
+                in_=x_grouped[:, c0 : c0 + n, :].rearrange("p n j -> p (n j)") if source is None else source,
             )
 
         for u in range(2):
@@ -157,28 +157,32 @@ def tile_attend_gml_lch_kernel(tc, xT, wd, wv, y, cw, rw, offs, out):
             for c0, n in ((0, PIECE), (PIECE, EARLY - PIECE)):
                 nc.vector.tensor_copy(out=x_words[:, c0 : c0 + n, u], in_=windows[u].indirect(listed(c0, n)))
             nc.vector.tensor_copy(out=tail[:, u, :], in_=windows[u].indirect(listed(EARLY, N - EARLY)))
-            make_weight(u, "x_raw%d_%d" % (u, X_LOADS[u][-1][0]))
+        make_weight(0, "x_raw0_%d" % X_LOADS[0][-1][0])
         quantize_x(0, PIECE)
 
         wd_grouped = held([P, PACK, P, PACK], BF16, name="wd_grouped")
         wd_codes = held([P, V], U32, name="wd_codes")
         wd_scales = held([P, V], U8, name="wd_scales")
         cut = P - WD_POOL
-        nc.scalar.activation(
-            out=wd_grouped[:, :, :cut, :].rearrange("p t m j -> p m j t"),
-            in_=wd_raw[:, :, : PACK * cut].rearrange("p j (m t) -> p m j t", t=PACK),
-            func=COPY,
-        )
-        if WD_POOL:
-            nc.gpsimd.tensor_copy(out=wd_grouped[:, :, cut:, :], in_=wd_raw[:, :, PACK * cut :].rearrange("p j (m t) -> p t m j", t=PACK))
-        nc.vector.quantize_mx(
-            out=wd_codes[:].bitcast(E4M3),
-            scales=wd_scales[:],
-            in_=wd_grouped[:].rearrange("p t m j -> p (t m j)"),
-        )
-        x_codes[PIECE] = held([P, N - PIECE], U32, name="x_codes_late", tag="wd_raw")
+        wd_columns = wd_raw[:].rearrange("p j (m t) -> p t m j", t=PACK)
+        for t0, width in ((0, P), (2, cut)):
+            nc.scalar.activation(
+                out=wd_grouped[:, t0 : t0 + 2, :width, :].rearrange("p t m j -> p m j t"),
+                in_=wd_columns[:, t0 : t0 + 2, :width, :].rearrange("p t m j -> p m j t"),
+                func=COPY,
+            )
+        nc.gpsimd.tensor_copy(out=wd_grouped[:, 2:, cut:, :], in_=wd_columns[:, 2:, cut:, :])
+        for t0 in (0, 2):
+            nc.vector.quantize_mx(
+                out=wd_codes[:, t0 * P : (t0 + 2) * P].bitcast(E4M3),
+                scales=wd_scales[:, t0 * P : (t0 + 2) * P],
+                in_=wd_grouped[:, t0 : t0 + 2, :, :].rearrange("p t m j -> p (t m j)"),
+            )
+        x_codes[PIECE] = held([P, EARLY - PIECE], U32, name="x_codes_mid", tag="wd_raw")
+        woven = held([P, 2 * TAIL], U32, name="woven", tag="wd_grouped")[:]
         quantize_x(PIECE, EARLY - PIECE)
-        nc.scalar.copy(out=x_words[:, EARLY:, :], in_=tail[:].rearrange("p u n -> p n u"))
+        nc.scalar.copy(out=woven.rearrange("p (n u) -> p n u", u=2), in_=tail[:].rearrange("p u n -> p n u"))
+        make_weight(1, "x_raw1_%d" % X_LOADS[1][-1][0])
 
         wv_codes = held([P, D], U32, name="wv_codes")
         wv_scales = held([P, D], U8, name="wv_scales")
@@ -302,7 +306,8 @@ def tile_attend_gml_lch_kernel(tc, xT, wd, wv, y, cw, rw, offs, out):
         for j in range(4):
             second(0, j)
         evacuate(0, 0)
-        quantize_x(EARLY, N - EARLY)
+        x_codes[EARLY] = held([P, TAIL], U32, name="x_codes_tail", tag="slope0")
+        quantize_x(EARLY, TAIL, woven.bitcast(BF16))
         subtract_on_vector([2, 4], "g_part0")
         subtract_on_gpsimd([3], "wv_raw0", "diff1_0")
         both = held([P, PACK, PIECE], F32, name="slope23")

@@ -171,7 +171,7 @@ def tile_attend_gml_lch_kernel(tc, xT, wd, wv, y, cw, rw, offs, out):
                 in_=wd_columns[:, t0 : t0 + 2, :width, :].rearrange("p t m j -> p m j t"),
                 func=COPY,
             )
-        nc.gpsimd.tensor_copy(out=wd_grouped[:, 2:, cut:, :], in_=wd_columns[:, 2:, cut:, :])
+        nc.gpsimd.tensor_scalar(out=wd_grouped[:, 2:, cut:, :], in0=wd_columns[:, 2:, cut:, :], scalar1=1.0, scalar2=0.0, op0=MULT, op1=ADD)
         for t0 in (0, 2):
             nc.vector.quantize_mx(
                 out=wd_codes[:, t0 * P : (t0 + 2) * P].bitcast(E4M3),

@@ -27,11 +27,9 @@ BANK = 512
 HALF = 256
 RUN = N // P
 QUAD = 32
-X_LOADS = [[(0, 1024, 0), (1024, 1024, 704)], [(0, 1024, 0), (1024, 512, 512), (1536, 512, 352)]]
-WD_POOL = 64
-EARLY = 768
-TAIL = N - EARLY
 SPLIT = 2
+LAST = N - GROUP
+WD_VECTOR = 36
 CHUNKS = [(0, 256), (256, 384), (640, 384)]
 LAP = 16
 
@@ -60,27 +58,23 @@ def tile_attend_gml_lch_kernel(tc, xT, wd, wv, y, cw, rw, offs, out):
         cw_sb = held([P, PACK], F32, name="cw_sb")
         rw_col = held([P, RUN], F32, name="rw_col")
         rw_all = held([P, N], F32, name="rw_all")
-        y_sb = [held([P, PACK, n], F32, name="y%d" % c) for c, (c0, n) in enumerate(CHUNKS)]
+        y_sb = [held([P, PACK, PIECE], F32, name="y%d" % k) for k in range(N // PIECE)]
         wd_raw = held([P, PACK, V], F32, name="wd_raw")
-        tail = held([P, 2, TAIL], U32, name="tail")
         wv_raw = [held([P, PACK, HALF], F32, name="wv_raw%d" % h) for h in range(2)]
-        x_rows = xT.rearrange("(p u e) n -> p u e n", u=2, e=2)
+        x_rows = xT.rearrange("(p t) n -> p t n", t=PACK)
         y_rows = y.rearrange("(p t) n -> p t n", t=PACK)
 
         nc.sync.dma_start(rw_col[:], rw[0:1, :].rearrange("o (p e) -> p (o e)", e=RUN))
         nc.sync.dma_start(cw_sb[:], cw.rearrange("(p t) o -> p (t o)", t=PACK))
-        x_raw = {}
-        for u in range(2):
-            for n0, n, nv in X_LOADS[u]:
-                x_raw[u, n0] = held([P, 2, n], F32, name="x_raw%d_%d" % (u, n0))
-                nc.sync.dma_start(x_raw[u, n0][:], x_rows[:, u, :, n0 : n0 + n])
-            if u == 0:
+        planes = [held([P, T], F32, name="plane%d" % t) for t in range(PACK)]
+        for t in range(PACK):
+            nc.sync.dma_start(planes[t][:], x_rows[:, t, :])
+            if t == 0:
                 nc.sync.dma_start(offsets[:], offs)
         nc.sync.dma_start(wd_raw[:], wd.rearrange("(p j) v -> p j v", j=PACK))
 
-        def load_y(c):
-            c0, n = CHUNKS[c]
-            nc.sync.dma_start(y_sb[c][:], y_rows[:, :, c0 : c0 + n])
+        def load_y(k):
+            nc.sync.dma_start(y_sb[k][:], y_rows[:, :, k * PIECE : (k + 1) * PIECE])
 
         wv_rows = wv.rearrange("(p t) d -> p t d", t=PACK)
         nc.sync.dma_start(wv_raw[0][:], wv_rows[:, :, :HALF])
@@ -88,6 +82,7 @@ def tile_attend_gml_lch_kernel(tc, xT, wd, wv, y, cw, rw, offs, out):
         nc.sync.dma_start(wv_raw[1][:], wv_rows[:, :, HALF:])
         load_y(1)
         load_y(2)
+        load_y(3)
 
         def listed(c0, n):
             return offsets[:, c0 // 16 : (c0 + n) // 16]
@@ -103,7 +98,7 @@ def tile_attend_gml_lch_kernel(tc, xT, wd, wv, y, cw, rw, offs, out):
         nc.vector.tensor_tensor_scan(out=column[:], data0=ones[:], data1=ones[:], initial=0.0, op0=MULT, op1=ADD)
         nc.vector.transpose(out=row[:], in_=column[:, :QUAD])
         nc.vector.tensor_scalar(out=ident[:], in0=column[:], scalar1=row[:, 0:1], scalar2=base[:], op0=SUB, op1=EQUAL)
-        placed = [held([P, T], F32, name="placed%d" % j, tag=tag) for j, tag in enumerate(["column", "row", "base", "ident"])]
+        placed = [held([P, T], F32, name="placed%d" % j, tag=tag) for j, tag in enumerate(["column", "row", "ident", "plane0"])]
         lead = BANK - CHUNKS[0][1]
         g_codes = held([P, lead + N], U32, name="g_codes")
         g_scales = held([P, lead + N], U8, name="g_scales")
@@ -117,8 +112,9 @@ def tile_attend_gml_lch_kernel(tc, xT, wd, wv, y, cw, rw, offs, out):
                 nc.tensor.transpose(out=spread[:, e, :], in_=rw_col[:, e0 + e : e0 + e + 1].to_broadcast([P, P]), identity=ident[:])
             nc.scalar.activation(out=rw_runs[:, :, e0 : e0 + PACK], in_=spread[:].rearrange("p e n -> p n e"), func=COPY)
 
-        for j in range(PACK):
+        for j in range(2):
             nc.vector.memset(placed[j][:].bitcast(U32), 0)
+        nc.gpsimd.memset(placed[2][:].bitcast(U32), 0)
 
         weight = {}
 
@@ -128,61 +124,58 @@ def tile_attend_gml_lch_kernel(tc, xT, wd, wv, y, cw, rw, offs, out):
             for t in range(PACK):
                 nc.scalar.activation(out=weight[c][:, t, :], in_=rw_all[:, c0 : c0 + n], func=COPY, scale=cw_sb[:, t : t + 1])
 
-        pairs = [held([P, T, 2], BF16, name="pairs%d" % u) for u in range(2)]
-        windows = [pairs[u][:].rearrange("p n e -> p (n e)").bitcast(U32) for u in range(2)]
-        x_grouped = held([P, EARLY, PACK], BF16, name="x_grouped")
-        x_words = x_grouped[:].rearrange("p n j -> p (n j)").bitcast(U32).rearrange("p (n u) -> p n u", u=2)
+        picked = held([P, PACK, N], BF16, name="picked")
+        x_grouped = held([P, LAST, PACK], BF16, name="x_grouped")
         x_codes = {0: held([P, PIECE], U32, name="x_codes")}
-
         x_scales = held([P, N], U8, name="x_scales")
 
         def x_codes_of(c0, n):
             base = max(b for b in x_codes if b <= c0)
             return x_codes[base][:, c0 - base : c0 - base + n].bitcast(E4M3)
 
+        def interleave(engine, u, c0, n):
+            target, source = x_grouped[:, c0 : c0 + n, 2 * u : 2 * u + 2], picked[:, 2 * u : 2 * u + 2, c0 : c0 + n].rearrange("p e n -> p n e")
+            if engine == "s":
+                nc.scalar.copy(out=target, in_=source)
+            else:
+                nc.vector.tensor_copy(out=target, in_=source)
+
         def quantize_x(c0, n, source=None):
             nc.vector.quantize_mx(
                 out=x_codes_of(c0, n),
                 scales=x_scales[:, c0 : c0 + n],
-                in_=x_grouped[:, c0 : c0 + n, :].rearrange("p n j -> p (n j)") if source is None else source,
+                in_=(x_grouped[:, c0 : c0 + n, :] if source is None else source).rearrange("p n j -> p (n j)"),
             )
 
-        for u in range(2):
-            for n0, n, nv in X_LOADS[u]:
-                cut = n - nv
-                if cut > 0:
-                    nc.scalar.activation(out=pairs[u][:, n0 : n0 + cut, :], in_=x_raw[u, n0][:, :, :cut].rearrange("p e n -> p n e"), func=COPY)
-                if cut < n:
-                    nc.vector.tensor_copy(out=pairs[u][:, n0 + cut : n0 + n, :], in_=x_raw[u, n0][:, :, cut:].rearrange("p e n -> p n e"))
-            for c0, n in ((0, PIECE), (PIECE, EARLY - PIECE)):
-                nc.vector.tensor_copy(out=x_words[:, c0 : c0 + n, u], in_=windows[u].indirect(listed(c0, n)))
-            nc.vector.tensor_copy(out=tail[:, u, :], in_=windows[u].indirect(listed(EARLY, N - EARLY)))
-        make_weight(0, "x_raw0_%d" % X_LOADS[0][-1][0])
-        quantize_x(0, PIECE)
+        for t in range(PACK):
+            for c0, n in ((0, 256), (256, 512), (768, 256)) if t == PACK - 1 else ((0, N),):
+                nc.vector.tensor_copy(out=picked[:, t, c0 : c0 + n], in_=planes[t][:].indirect(listed(c0, n)))
+            if t == 0:
+                nc.gpsimd.memset(placed[3][:].bitcast(U32), 0)
+        for c in range(3):
+            make_weight(c, None)
+        interleave("s", 0, 0, LAST)
+        interleave("s", 1, 0, PIECE)
+        interleave("v", 1, PIECE, 2 * PIECE)
+        interleave("v", 1, 768, GROUP)
 
         wd_grouped = held([P, PACK, P, PACK], BF16, name="wd_grouped")
         wd_codes = held([P, V], U32, name="wd_codes")
         wd_scales = held([P, V], U8, name="wd_scales")
-        cut = P - WD_POOL
-        wd_columns = wd_raw[:].rearrange("p j (m t) -> p t m j", t=PACK)
-        for t0, width in ((0, P), (2, cut)):
-            nc.scalar.activation(
-                out=wd_grouped[:, t0 : t0 + 2, :width, :].rearrange("p t m j -> p m j t"),
-                in_=wd_columns[:, t0 : t0 + 2, :width, :].rearrange("p t m j -> p m j t"),
-                func=COPY,
-            )
-        nc.gpsimd.tensor_scalar(out=wd_grouped[:, 2:, cut:, :], in0=wd_columns[:, 2:, cut:, :], scalar1=1.0, scalar2=0.0, op0=MULT, op1=ADD)
+        cut = P - WD_VECTOR
+        wd_columns = wd_raw[:].rearrange("p j (m t) -> p m j t", t=PACK)
+        wd_dealt = wd_grouped[:].rearrange("p t m j -> p m j t")
+        nc.scalar.activation(out=wd_dealt[:, :cut], in_=wd_columns[:, :cut], func=COPY)
+        nc.vector.tensor_copy(out=wd_dealt[:, cut:], in_=wd_columns[:, cut:])
+        quantize_x(0, PIECE)
         for t0 in (0, 2):
             nc.vector.quantize_mx(
                 out=wd_codes[:, t0 * P : (t0 + 2) * P].bitcast(E4M3),
                 scales=wd_scales[:, t0 * P : (t0 + 2) * P],
                 in_=wd_grouped[:, t0 : t0 + 2, :, :].rearrange("p t m j -> p (t m j)"),
             )
-        x_codes[PIECE] = held([P, EARLY - PIECE], U32, name="x_codes_mid", tag="wd_raw")
-        woven = held([P, 2 * TAIL], U32, name="woven", tag="wd_grouped")[:]
-        quantize_x(PIECE, EARLY - PIECE)
-        nc.scalar.copy(out=woven.rearrange("p (n u) -> p n u", u=2), in_=tail[:].rearrange("p u n -> p n u"))
-        make_weight(1, "x_raw1_%d" % X_LOADS[1][-1][0])
+        x_codes[PIECE] = held([P, 2 * PIECE], U32, name="x_codes_mid", tag="wd_raw")
+        quantize_x(PIECE, 2 * PIECE)
 
         wv_codes = held([P, D], U32, name="wv_codes")
         wv_scales = held([P, D], U8, name="wv_scales")
@@ -216,9 +209,8 @@ def tile_attend_gml_lch_kernel(tc, xT, wd, wv, y, cw, rw, offs, out):
             return a
 
         def targets(gi):
-            c = max(c for c in range(len(CHUNKS)) if CHUNKS[c][0] <= gi * GROUP)
-            y0 = gi * GROUP - CHUNKS[c][0]
-            return y_sb[c][:, :, y0 : y0 + GROUP]
+            k, y0 = divmod(gi * GROUP, PIECE)
+            return y_sb[k][:, :, y0 : y0 + GROUP]
 
         def subtract_on_vector(groups, tag):
             tile = held([P, len(groups), PACK, GROUP], F32, name="diff_v", tag=tag)
@@ -302,29 +294,31 @@ def tile_attend_gml_lch_kernel(tc, xT, wd, wv, y, cw, rw, offs, out):
             weigh(nc.vector, 0, gi * GROUP, (gi + 1) * GROUP)
         quantize_g(0, 0)
         prepare_wv(0, HALF, "wv_low")
+        x_last = held([P, GROUP, PACK], BF16, name="x_last", tag="wd_grouped")
+        nc.scalar.copy(out=runs_packed(x_last[:]), in_=runs(picked[:, :, LAST:]))
         prepare_wv(HALF, HALF, "diff1_0")
         for j in range(4):
             second(0, j)
         evacuate(0, 0)
-        x_codes[EARLY] = held([P, TAIL], U32, name="x_codes_tail", tag="slope0")
-        quantize_x(EARLY, TAIL, woven.bitcast(BF16))
-        subtract_on_vector([2, 4], "g_part0")
-        subtract_on_gpsimd([3], "wv_raw0", "diff1_0")
-        both = held([P, PACK, PIECE], F32, name="slope23")
-        bend(2, both, 0)
-        bend(4, held([P, PACK, GROUP], F32, name="slope4"), 0)
+        x_codes[768] = held([P, PIECE], U32, name="x_codes_tail", tag="slope0")
+        quantize_x(768, GROUP)
+        quantize_x(LAST, GROUP, x_last[:])
+        subtract_on_vector([2, 3], "g_part0")
+        subtract_on_gpsimd([4], "wv_raw0", "diff1_0")
+        both = held([P, PACK, PIECE], F32, name="slope34")
+        bend(2, held([P, PACK, GROUP], F32, name="slope2"), 0)
+        bend(3, both, 0)
         evacuate(0, 1)
-        bend(3, both, 1)
+        bend(4, both, 1)
         evacuate(0, 2)
-        weigh(nc.gpsimd, 1, 256, 384 - LAP)
-        weigh(nc.gpsimd, 1, 512, 640)
-        weigh(nc.gpsimd, 1, 384 - LAP, 512)
+        weigh(nc.gpsimd, 1, 256, 384)
+        weigh(nc.gpsimd, 1, 384, 512 - LAP)
+        weigh(nc.gpsimd, 1, 512 - LAP, 640)
         for j in range(3):
             place(0, j)
-        quantize_g(1, 384)
-        make_weight(2, "g_part0")
+        quantize_g(1, 512)
         subtract_on_gpsimd([5, 7, 6], "staged_late", "g_part1")
-        evacuate(0, 3, "slope23")
+        evacuate(0, 3, "slope34")
         for j in range(4):
             second(1, j)
             if j < 3:

@@ -8,6 +8,7 @@ FLOPS = 2 * 2 * D * V * N
 F32 = mybir.dt.float32
 BF16 = mybir.dt.bfloat16
 U32 = mybir.dt.uint32
+I32 = mybir.dt.int32
 U16 = mybir.dt.uint16
 U8 = mybir.dt.uint8
 E4M3 = mybir.dt.float8_e4m3fn_x4
@@ -28,8 +29,9 @@ HALF = 256
 RUN = N // P
 QUAD = 32
 SPLIT = 2
-LAST = N - GROUP
-WD_VECTOR = 36
+LAST = 768
+WEAVES = [("s", 0, 256), ("s", 256, 256), ("v", 512, 256)]
+WD_VECTOR = 32
 CHUNKS = [(0, 256), (256, 384), (640, 384)]
 LAP = 16
 
@@ -124,8 +126,11 @@ def tile_attend_gml_lch_kernel(tc, xT, wd, wv, y, cw, rw, offs, out):
             for t in range(PACK):
                 nc.scalar.activation(out=weight[c][:, t, :], in_=rw_all[:, c0 : c0 + n], func=COPY, scale=cw_sb[:, t : t + 1])
 
-        picked = held([P, PACK, N], BF16, name="picked")
-        x_grouped = held([P, LAST, PACK], BF16, name="x_grouped")
+        picked = held([P, PACK * N], BF16, name="picked")
+        picked_halves = picked[:].rearrange("p (u n e) -> p u n e", u=2, e=2)
+        picked_words = picked[:].bitcast(U32).rearrange("p (u n) -> p n u", u=2)
+        early = held([P, 2, N], BF16, name="early")
+        x_grouped = held([P, LAST * PACK], BF16, name="x_grouped")
         x_codes = {0: held([P, PIECE], U32, name="x_codes")}
         x_scales = held([P, N], U8, name="x_scales")
 
@@ -133,31 +138,34 @@ def tile_attend_gml_lch_kernel(tc, xT, wd, wv, y, cw, rw, offs, out):
             base = max(b for b in x_codes if b <= c0)
             return x_codes[base][:, c0 - base : c0 - base + n].bitcast(E4M3)
 
-        def interleave(engine, u, c0, n):
-            target, source = x_grouped[:, c0 : c0 + n, 2 * u : 2 * u + 2], picked[:, 2 * u : 2 * u + 2, c0 : c0 + n].rearrange("p e n -> p n e")
+        def interleave(engine, target, c0, n):
+            words = target.bitcast(U32).rearrange("p (n u) -> p n u", u=2)
             if engine == "s":
-                nc.scalar.copy(out=target, in_=source)
+                nc.scalar.copy(out=words, in_=picked_words[:, c0 : c0 + n, :])
             else:
-                nc.vector.tensor_copy(out=target, in_=source)
+                nc.vector.tensor_copy(out=words.bitcast(I32), in_=picked[:].bitcast(I32).rearrange("p (u n) -> p n u", u=2)[:, c0 : c0 + n, :])
+
+        def grouped_of(c0, n):
+            return x_grouped[:, PACK * c0 : PACK * (c0 + n)]
 
         def quantize_x(c0, n, source=None):
             nc.vector.quantize_mx(
                 out=x_codes_of(c0, n),
                 scales=x_scales[:, c0 : c0 + n],
-                in_=(x_grouped[:, c0 : c0 + n, :] if source is None else source).rearrange("p n j -> p (n j)"),
+                in_=grouped_of(c0, n) if source is None else source,
             )
 
         for t in range(PACK):
-            for c0, n in ((0, 256), (256, 512), (768, 256)) if t == PACK - 1 else ((0, N),):
-                nc.vector.tensor_copy(out=picked[:, t, c0 : c0 + n], in_=planes[t][:].indirect(listed(c0, n)))
+            for c0, n in ((0, 256), (256, 256), (512, 256), (768, 256)) if t == PACK - 1 else ((0, N),):
+                target = early[:, t, c0 : c0 + n] if t < 2 else picked_halves[:, 1, c0 : c0 + n, t - 2]
+                nc.vector.tensor_copy(out=target, in_=planes[t][:].indirect(listed(c0, n)))
             if t == 0:
                 nc.gpsimd.memset(placed[3][:].bitcast(U32), 0)
         for c in range(3):
             make_weight(c, None)
-        interleave("s", 0, 0, LAST)
-        interleave("s", 1, 0, PIECE)
-        interleave("v", 1, PIECE, 2 * PIECE)
-        interleave("v", 1, 768, GROUP)
+        nc.scalar.activation(out=picked_halves[:, 0], in_=early[:].rearrange("p e n -> p n e"), func=COPY)
+        for engine, c0, n in WEAVES:
+            interleave(engine, grouped_of(c0, n), c0, n)
 
         wd_grouped = held([P, PACK, P, PACK], BF16, name="wd_grouped")
         wd_codes = held([P, V], U32, name="wd_codes")
@@ -294,15 +302,14 @@ def tile_attend_gml_lch_kernel(tc, xT, wd, wv, y, cw, rw, offs, out):
             weigh(nc.vector, 0, gi * GROUP, (gi + 1) * GROUP)
         quantize_g(0, 0)
         prepare_wv(0, HALF, "wv_low")
-        x_last = held([P, GROUP, PACK], BF16, name="x_last", tag="wd_grouped")
-        nc.scalar.copy(out=runs_packed(x_last[:]), in_=runs(picked[:, :, LAST:]))
+        x_last = held([P, (N - LAST) * PACK], BF16, name="x_last", tag="wd_grouped")
+        interleave("s", x_last[:], LAST, N - LAST)
         prepare_wv(HALF, HALF, "diff1_0")
         for j in range(4):
             second(0, j)
         evacuate(0, 0)
         x_codes[768] = held([P, PIECE], U32, name="x_codes_tail", tag="slope0")
-        quantize_x(768, GROUP)
-        quantize_x(LAST, GROUP, x_last[:])
+        quantize_x(LAST, N - LAST, x_last[:])
         subtract_on_vector([2, 3], "g_part0")
         subtract_on_gpsimd([4], "wv_raw0", "diff1_0")
         both = held([P, PACK, PIECE], F32, name="slope34")

@@ -29,6 +29,7 @@ HALF = 256
 RUN = N // P
 QUAD = 32
 SPLIT = 2
+Y_LOADS = [(0, 256), (256, 256), (512, 128), (640, 384)]
 LAST = 768
 WEAVES = [("s", 0, 256), ("s", 256, 256), ("v", 512, 256)]
 WD_VECTOR = 32
@@ -51,16 +52,11 @@ def tile_attend_gml_lch_kernel(tc, xT, wd, wv, y, cw, rw, offs, out):
         def runs_packed(ap):
             return ap.rearrange("p (c i) t -> p c t i", i=4)
 
-        warm = held([P, 8], F32, name="warm")
-        warm_out = held([P, 8], F32, name="warm_out")
-        nc.vector.memset(warm[:], 0.0)
-        nc.scalar.activation(out=warm_out[:], in_=warm[:], func=TANH)
-
         offsets = held([P, N // 16], U16, name="offsets")
         cw_sb = held([P, PACK], F32, name="cw_sb")
         rw_col = held([P, RUN], F32, name="rw_col")
         rw_all = held([P, N], F32, name="rw_all")
-        y_sb = [held([P, PACK, PIECE], F32, name="y%d" % k) for k in range(N // PIECE)]
+        y_sb = [held([P, PACK, n], F32, name="y%d" % k) for k, (y0, n) in enumerate(Y_LOADS)]
         wd_raw = held([P, PACK, V], F32, name="wd_raw")
         wv_raw = [held([P, PACK, HALF], F32, name="wv_raw%d" % h) for h in range(2)]
         x_rows = xT.rearrange("(p t) n -> p t n", t=PACK)
@@ -76,7 +72,8 @@ def tile_attend_gml_lch_kernel(tc, xT, wd, wv, y, cw, rw, offs, out):
         nc.sync.dma_start(wd_raw[:], wd.rearrange("(p j) v -> p j v", j=PACK))
 
         def load_y(k):
-            nc.sync.dma_start(y_sb[k][:], y_rows[:, :, k * PIECE : (k + 1) * PIECE])
+            y0, n = Y_LOADS[k]
+            nc.sync.dma_start(y_sb[k][:], y_rows[:, :, y0 : y0 + n])
 
         wv_rows = wv.rearrange("(p t) d -> p t d", t=PACK)
         nc.sync.dma_start(wv_raw[0][:], wv_rows[:, :, :HALF])
@@ -161,7 +158,7 @@ def tile_attend_gml_lch_kernel(tc, xT, wd, wv, y, cw, rw, offs, out):
                 nc.vector.tensor_copy(out=target, in_=planes[t][:].indirect(listed(c0, n)))
             if t == 0:
                 nc.gpsimd.memset(placed[3][:].bitcast(U32), 0)
-        for c in range(3):
+        for c in range(2):
             make_weight(c, None)
         nc.scalar.activation(out=picked_halves[:, 0], in_=early[:].rearrange("p e n -> p n e"), func=COPY)
         for engine, c0, n in WEAVES:
@@ -217,7 +214,8 @@ def tile_attend_gml_lch_kernel(tc, xT, wd, wv, y, cw, rw, offs, out):
             return a
 
         def targets(gi):
-            k, y0 = divmod(gi * GROUP, PIECE)
+            k = max(k for k in range(len(Y_LOADS)) if Y_LOADS[k][0] <= gi * GROUP)
+            y0 = gi * GROUP - Y_LOADS[k][0]
             return y_sb[k][:, :, y0 : y0 + GROUP]
 
         def subtract_on_vector(groups, tag):
@@ -324,6 +322,7 @@ def tile_attend_gml_lch_kernel(tc, xT, wd, wv, y, cw, rw, offs, out):
         for j in range(3):
             place(0, j)
         quantize_g(1, 512)
+        make_weight(2, "g_part0")
         subtract_on_gpsimd([5, 7, 6], "staged_late", "g_part1")
         evacuate(0, 3, "slope34")
         for j in range(4):

@@ -62,8 +62,8 @@ def tile_attend_gml_lch_kernel(tc, xT, wd, wv, y, cw, rw, offs, out):
         x_rows = xT.rearrange("(p t) n -> p t n", t=PACK)
         y_rows = y.rearrange("(p t) n -> p t n", t=PACK)
 
-        nc.sync.dma_start(rw_col[:], rw[0:1, :].rearrange("o (p e) -> p (o e)", e=RUN))
-        nc.sync.dma_start(cw_sb[:], cw.rearrange("(p t) o -> p (t o)", t=PACK))
+        nc.scalar.dma_start(rw_col[:], rw[0:1, :].rearrange("o (p e) -> p (o e)", e=RUN))
+        nc.scalar.dma_start(cw_sb[:], cw.rearrange("(p t) o -> p (t o)", t=PACK))
         planes = [held([P, T], F32, name="plane%d" % t) for t in range(PACK)]
         for t in range(PACK):
             nc.sync.dma_start(planes[t][:], x_rows[:, t, :])

@@ -28,11 +28,11 @@ BANK = 512
 HALF = 256
 RUN = N // P
 QUAD = 32
-SPLIT = 2
+SIDE = 4
+T_HALF = 2
 Y_LOADS = [(0, 256), (256, 256), (512, 128), (640, 384)]
-LAST = 768
-WEAVES = [("s", 0, 256), ("s", 256, 256), ("v", 512, 256)]
-WD_VECTOR = 32
+LAST = N - PIECE
+WD_VECTOR = 88
 CHUNKS = [(0, 256), (256, 384), (640, 384)]
 LAP = 16
 
@@ -47,10 +47,10 @@ def tile_attend_gml_lch_kernel(tc, xT, wd, wv, y, cw, rw, offs, out):
             return keep.tile(shape, dtype, name=name, tag=tag or name, align_bytes=64)
 
         def runs(ap):
-            return ap.rearrange("p t (c i) -> p c t i", i=4)
+            return ap.rearrange("p t (c i) -> p c t i", i=SIDE)
 
         def runs_packed(ap):
-            return ap.rearrange("p (c i) t -> p c t i", i=4)
+            return ap.rearrange("p (c i) t -> p c t i", i=SIDE)
 
         offsets = held([P, N // 16], U16, name="offsets")
         cw_sb = held([P, PACK], F32, name="cw_sb")
@@ -132,28 +132,31 @@ def tile_attend_gml_lch_kernel(tc, xT, wd, wv, y, cw, rw, offs, out):
         x_scales = held([P, N], U8, name="x_scales")
 
         def x_codes_of(c0, n):
-            base = max(b for b in x_codes if b <= c0)
-            return x_codes[base][:, c0 - base : c0 - base + n].bitcast(E4M3)
+            start = max(b for b in x_codes if b <= c0)
+            return x_codes[start][:, c0 - start : c0 - start + n].bitcast(E4M3)
 
-        def interleave(engine, target, c0, n):
-            words = target.bitcast(U32).rearrange("p (n u) -> p n u", u=2)
-            if engine == "s":
-                nc.scalar.copy(out=words, in_=picked_words[:, c0 : c0 + n, :])
-            else:
-                nc.vector.tensor_copy(out=words.bitcast(I32), in_=picked[:].bitcast(I32).rearrange("p (u n) -> p n u", u=2)[:, c0 : c0 + n, :])
+        def weave_on_scalar(target, c0):
+            nc.scalar.copy(out=target.bitcast(U32).rearrange("p (n u) -> p n u", u=2), in_=picked_words[:, c0 : c0 + PIECE, :])
+
+        def weave_on_vector(target, c0):
+            nc.vector.tensor_copy(
+                out=target.bitcast(I32).rearrange("p (n u) -> p n u", u=2),
+                in_=picked[:].bitcast(I32).rearrange("p (u n) -> p n u", u=2)[:, c0 : c0 + PIECE, :],
+            )
 
         def grouped_of(c0, n):
             return x_grouped[:, PACK * c0 : PACK * (c0 + n)]
 
-        def quantize_x(c0, n, source=None):
+        def quantize_x(c0, n, source):
             nc.vector.quantize_mx(
                 out=x_codes_of(c0, n),
                 scales=x_scales[:, c0 : c0 + n],
-                in_=grouped_of(c0, n) if source is None else source,
+                in_=source,
             )
 
         for t in range(PACK):
-            for c0, n in ((0, 256), (256, 256), (512, 256), (768, 256)) if t == PACK - 1 else ((0, N),):
+            n = PIECE if t == PACK - 1 else N
+            for c0 in range(0, N, n):
                 target = early[:, t, c0 : c0 + n] if t < 2 else picked_halves[:, 1, c0 : c0 + n, t - 2]
                 nc.vector.tensor_copy(out=target, in_=planes[t][:].indirect(listed(c0, n)))
             if t == 0:
@@ -161,8 +164,9 @@ def tile_attend_gml_lch_kernel(tc, xT, wd, wv, y, cw, rw, offs, out):
         for c in range(2):
             make_weight(c, None)
         nc.scalar.activation(out=picked_halves[:, 0], in_=early[:].rearrange("p e n -> p n e"), func=COPY)
-        for engine, c0, n in WEAVES:
-            interleave(engine, grouped_of(c0, n), c0, n)
+        weave_on_scalar(grouped_of(0, PIECE), 0)
+        weave_on_scalar(grouped_of(PIECE, PIECE), PIECE)
+        weave_on_vector(grouped_of(2 * PIECE, PIECE), 2 * PIECE)
 
         wd_grouped = held([P, PACK, P, PACK], BF16, name="wd_grouped")
         wd_codes = held([P, V], U32, name="wd_codes")
@@ -170,17 +174,18 @@ def tile_attend_gml_lch_kernel(tc, xT, wd, wv, y, cw, rw, offs, out):
         cut = P - WD_VECTOR
         wd_columns = wd_raw[:].rearrange("p j (m t) -> p m j t", t=PACK)
         wd_dealt = wd_grouped[:].rearrange("p t m j -> p m j t")
-        nc.scalar.activation(out=wd_dealt[:, :cut], in_=wd_columns[:, :cut], func=COPY)
-        nc.vector.tensor_copy(out=wd_dealt[:, cut:], in_=wd_columns[:, cut:])
-        quantize_x(0, PIECE)
-        for t0 in (0, 2):
+        nc.scalar.activation(out=wd_dealt[:, :, :, :T_HALF], in_=wd_columns[:, :, :, :T_HALF], func=COPY)
+        nc.scalar.activation(out=wd_dealt[:, :cut, :, T_HALF:], in_=wd_columns[:, :cut, :, T_HALF:], func=COPY)
+        nc.vector.tensor_copy(out=wd_dealt[:, cut:, :, T_HALF:], in_=wd_columns[:, cut:, :, T_HALF:])
+        quantize_x(0, PIECE, grouped_of(0, PIECE))
+        for t0 in range(0, PACK, T_HALF):
             nc.vector.quantize_mx(
-                out=wd_codes[:, t0 * P : (t0 + 2) * P].bitcast(E4M3),
-                scales=wd_scales[:, t0 * P : (t0 + 2) * P],
-                in_=wd_grouped[:, t0 : t0 + 2, :, :].rearrange("p t m j -> p (t m j)"),
+                out=wd_codes[:, t0 * P : (t0 + T_HALF) * P].bitcast(E4M3),
+                scales=wd_scales[:, t0 * P : (t0 + T_HALF) * P],
+                in_=wd_grouped[:, t0 : t0 + T_HALF, :, :].rearrange("p t m j -> p (t m j)"),
             )
         x_codes[PIECE] = held([P, 2 * PIECE], U32, name="x_codes_mid", tag="wd_raw")
-        quantize_x(PIECE, 2 * PIECE)
+        quantize_x(PIECE, 2 * PIECE, grouped_of(PIECE, 2 * PIECE))
 
         wv_codes = held([P, D], U32, name="wv_codes")
         wv_scales = held([P, D], U8, name="wv_scales")
@@ -240,24 +245,24 @@ def tile_attend_gml_lch_kernel(tc, xT, wd, wv, y, cw, rw, offs, out):
             nc.scalar.activation(out=tile[:, :, k * GROUP : (k + 1) * GROUP], in_=diff[gi], func=TANH)
 
         def weigh(engine, c, lo, hi):
-            tile, base = slope[lo // GROUP]
-            w0 = CHUNKS[c][0]
+            tile, start = slope[lo // GROUP]
+            c0 = CHUNKS[c][0]
             engine.tensor_tensor(
-                out=runs_packed(g_part[c][:, lo - CHUNKS[c][0] : hi - CHUNKS[c][0], :]),
-                in0=runs(tile[:, :, lo - base : hi - base]),
-                in1=runs(weight[c][:, :, lo - w0 : hi - w0]),
+                out=runs_packed(g_part[c][:, lo - c0 : hi - c0, :]),
+                in0=runs(tile[:, :, lo - start : hi - start]),
+                in1=runs(weight[c][:, :, lo - c0 : hi - c0]),
                 op=MULT,
             )
 
-        def quantize_g(c, cut):
+        def quantize_g(c):
             c0, n = CHUNKS[c]
-            for lo, hi in ((c0, cut), (cut, c0 + n)):
-                if hi > lo:
-                    nc.vector.quantize_mx(
-                        out=g_codes[:, lead + lo : lead + hi].bitcast(E5M2),
-                        scales=g_scales[:, lead + lo : lead + hi],
-                        in_=g_part[c][:, lo - c0 : hi - c0, :].rearrange("p n t -> p (n t)"),
-                    )
+            for lo in range(c0, c0 + n, PIECE):
+                hi = min(lo + PIECE, c0 + n)
+                nc.vector.quantize_mx(
+                    out=g_codes[:, lead + lo : lead + hi].bitcast(E5M2),
+                    scales=g_scales[:, lead + lo : lead + hi],
+                    in_=g_part[c][:, lo - c0 : hi - c0, :].rearrange("p n t -> p (n t)"),
+                )
 
         for c, (c0, n) in enumerate(CHUNKS):
             g_part[c] = held([P, n, PACK], BF16, name="g_part%d" % c)
@@ -289,61 +294,62 @@ def tile_attend_gml_lch_kernel(tc, xT, wd, wv, y, cw, rw, offs, out):
             if c == len(CHUNKS) - 1:
                 nc.sync.dma_start(out[j * P : (j + 1) * P, :], placed[j][:])
 
-        step = PACK // SPLIT
         for gi in range(2):
             slope[gi] = (held([P, PACK, GROUP], F32, name="slope%d" % gi), gi * GROUP)
-            for t0 in range(0, PACK, step):
-                part = held([P, step, GROUP], F32, name="diff%d_%d" % (gi, t0))
-                nc.vector.tensor_tensor(out=part[:], in0=scores(gi, t0, step)[:], in1=targets(gi)[:, t0 : t0 + step, :], op=SUB)
-                nc.scalar.activation(out=slope[gi][0][:, t0 : t0 + step, :], in_=part[:], func=TANH)
+            for t0 in range(0, PACK, T_HALF):
+                part = held([P, T_HALF, GROUP], F32, name="diff%d_%d" % (gi, t0))
+                nc.vector.tensor_tensor(out=part[:], in0=scores(gi, t0, T_HALF)[:], in1=targets(gi)[:, t0 : t0 + T_HALF, :], op=SUB)
+                nc.scalar.activation(out=slope[gi][0][:, t0 : t0 + T_HALF, :], in_=part[:], func=TANH)
         for gi in range(2):
             weigh(nc.vector, 0, gi * GROUP, (gi + 1) * GROUP)
-        quantize_g(0, 0)
+        quantize_g(0)
         prepare_wv(0, HALF, "wv_low")
-        x_last = held([P, (N - LAST) * PACK], BF16, name="x_last", tag="wd_grouped")
-        interleave("s", x_last[:], LAST, N - LAST)
+        x_last = held([P, PIECE * PACK], BF16, name="x_last", tag="wd_grouped")
+        weave_on_scalar(x_last[:], LAST)
         prepare_wv(HALF, HALF, "diff1_0")
-        for j in range(4):
+        for j in range(PACK):
             second(0, j)
         evacuate(0, 0)
-        x_codes[768] = held([P, PIECE], U32, name="x_codes_tail", tag="slope0")
-        quantize_x(LAST, N - LAST, x_last[:])
+        x_codes[LAST] = held([P, PIECE], U32, name="x_codes_tail", tag="slope0")
+        quantize_x(LAST, PIECE, x_last[:])
+
         subtract_on_vector([2, 3], "g_part0")
         subtract_on_gpsimd([4], "wv_raw0", "diff1_0")
-        both = held([P, PACK, PIECE], F32, name="slope34")
+        slope34 = held([P, PACK, PIECE], F32, name="slope34")
         bend(2, held([P, PACK, GROUP], F32, name="slope2"), 0)
-        bend(3, both, 0)
+        bend(3, slope34, 0)
         evacuate(0, 1)
-        bend(4, both, 1)
+        bend(4, slope34, 1)
         evacuate(0, 2)
-        weigh(nc.gpsimd, 1, 256, 384)
-        weigh(nc.gpsimd, 1, 384, 512 - LAP)
-        weigh(nc.gpsimd, 1, 512 - LAP, 640)
-        for j in range(3):
+        weigh(nc.gpsimd, 1, 2 * GROUP, 3 * GROUP)
+        weigh(nc.gpsimd, 1, 3 * GROUP, 4 * GROUP - LAP)
+        weigh(nc.gpsimd, 1, 4 * GROUP - LAP, 5 * GROUP)
+        for j in range(PACK - 1):
             place(0, j)
-        quantize_g(1, 512)
+        quantize_g(1)
+
         make_weight(2, "g_part0")
         subtract_on_gpsimd([5, 7, 6], "staged_late", "g_part1")
-        evacuate(0, 3, "slope34")
-        for j in range(4):
+        evacuate(0, PACK - 1, "slope34")
+        for j in range(PACK):
             second(1, j)
-            if j < 3:
+            if j < PACK - 1:
                 evacuate(1, j)
-        place(0, 3)
+        place(0, PACK - 1)
         bend(5, held([P, PACK, GROUP], F32, name="slope5"), 0)
-        both = held([P, PACK, PIECE], F32, name="slope67")
-        bend(7, both, 1)
-        bend(6, both, 0)
-        weigh(nc.gpsimd, 2, 640, 768)
-        weigh(nc.gpsimd, 2, 896 + LAP, 1024)
-        weigh(nc.gpsimd, 2, 768, 896 + LAP)
-        for j in range(3):
+        slope67 = held([P, PACK, PIECE], F32, name="slope67")
+        bend(7, slope67, 1)
+        bend(6, slope67, 0)
+        weigh(nc.gpsimd, 2, 5 * GROUP, 6 * GROUP)
+        weigh(nc.gpsimd, 2, 7 * GROUP + LAP, 8 * GROUP)
+        weigh(nc.gpsimd, 2, 6 * GROUP, 7 * GROUP + LAP)
+        for j in range(PACK - 1):
             place(1, j)
-        quantize_g(2, 896)
-        evacuate(1, 3, "slope67")
-        for j in range(4):
+        quantize_g(2)
+        evacuate(1, PACK - 1, "slope67")
+        for j in range(PACK):
             second(2, j)
             evacuate(2, j)
-        place(1, 3)
-        for j in range(4):
+        place(1, PACK - 1)
+        for j in range(PACK):
             place(2, j)

@@ -29,6 +29,7 @@ HALF = 256
 RUN = N // P
 QUAD = 32
 SIDE = 4
+GPSIMD_SIDE = 2
 T_HALF = 2
 Y_LOADS = [(0, 256), (256, 256), (512, 128), (640, 384)]
 LAST = N - PIECE
@@ -46,11 +47,11 @@ def tile_attend_gml_lch_kernel(tc, xT, wd, wv, y, cw, rw, offs, out):
         def held(shape, dtype, name, tag=None):
             return keep.tile(shape, dtype, name=name, tag=tag or name, align_bytes=64)
 
-        def runs(ap):
-            return ap.rearrange("p t (c i) -> p c t i", i=SIDE)
+        def runs(ap, side=SIDE):
+            return ap.rearrange("p t (c i) -> p c t i", i=side)
 
-        def runs_packed(ap):
-            return ap.rearrange("p (c i) t -> p c t i", i=SIDE)
+        def runs_packed(ap, side=SIDE):
+            return ap.rearrange("p (c i) t -> p c t i", i=side)
 
         offsets = held([P, N // 16], U16, name="offsets")
         cw_sb = held([P, PACK], F32, name="cw_sb")
@@ -247,10 +248,11 @@ def tile_attend_gml_lch_kernel(tc, xT, wd, wv, y, cw, rw, offs, out):
         def weigh(engine, c, lo, hi):
             tile, start = slope[lo // GROUP]
             c0 = CHUNKS[c][0]
+            side = SIDE if c == 0 else GPSIMD_SIDE
             engine.tensor_tensor(
-                out=runs_packed(g_part[c][:, lo - c0 : hi - c0, :]),
-                in0=runs(tile[:, :, lo - start : hi - start]),
-                in1=runs(weight[c][:, :, lo - c0 : hi - c0]),
+                out=runs_packed(g_part[c][:, lo - c0 : hi - c0, :], side),
+                in0=runs(tile[:, :, lo - start : hi - start], side),
+                in1=runs(weight[c][:, :, lo - c0 : hi - c0], side),
                 op=MULT,
             )
 

@@ -29,7 +29,7 @@ HALF = 256
 RUN = N // P
 QUAD = 32
 SIDE = 4
-GPSIMD_SIDE = 2
+GPSIMD_SIDE = 8
 T_HALF = 2
 Y_LOADS = [(0, 256), (256, 256), (512, 128), (640, 384)]
 LAST = N - PIECE

@@ -272,8 +272,16 @@ def tile_attend_gml_lch_kernel(tc, xT, wd, wv, y, cw, rw, offs, out):
         dx_ps = {}
         dx_sb = {}
 
+        def span(c, j):
+            c0, n = CHUNKS[c]
+            if j == 0 and c == 1:
+                return c0, PIECE
+            if j == 0 and c == 2:
+                return 2 * PIECE, 2 * PIECE
+            return c0, n
+
         def second(c, j):
-            end = lead + sum(CHUNKS[c])
+            end = lead + sum(span(c, j))
             dx_ps[c, j] = psum.tile([P, BANK], F32, name="dx")
             nc.tensor.matmul_mx(
                 out=dx_ps[c, j][:],
@@ -286,12 +294,12 @@ def tile_attend_gml_lch_kernel(tc, xT, wd, wv, y, cw, rw, offs, out):
             )
 
         def evacuate(c, j, tag=None):
-            n = CHUNKS[c][1]
+            n = span(c, j)[1]
             dx_sb[c, j] = held([P, n], F32, name="dx_sb", tag=tag or "dx_sb%d_%d" % (c, j))
             nc.scalar.activation(out=dx_sb[c, j][:], in_=dx_ps[c, j][:, BANK - n :], func=COPY)
 
         def place(c, j):
-            c0, n = CHUNKS[c]
+            c0, n = span(c, j)
             nc.vector.tensor_copy(out=placed[j][:].indirect(listed(c0, n)), in_=dx_sb[c, j][:])
             if c == len(CHUNKS) - 1:
                 nc.sync.dma_start(out[j * P : (j + 1) * P, :], placed[j][:])

@@ -351,8 +351,7 @@ def tile_attend_gml_lch_kernel(tc, xT, wd, wv, y, cw, rw, offs, out):
         bend(7, slope67, 1)
         bend(6, slope67, 0)
         weigh(nc.gpsimd, 2, 5 * GROUP, 6 * GROUP)
-        weigh(nc.gpsimd, 2, 7 * GROUP + LAP, 8 * GROUP)
-        weigh(nc.gpsimd, 2, 6 * GROUP, 7 * GROUP + LAP)
+        weigh(nc.gpsimd, 2, 6 * GROUP, 8 * GROUP)
         for j in range(PACK - 1):
             place(1, j)
         quantize_g(2)

@@ -35,6 +35,7 @@ Y_LOADS = [(0, 256), (256, 256), (512, 128), (640, 384)]
 LAST = N - PIECE
 WD_VECTOR = 88
 CHUNKS = [(0, 256), (256, 384), (640, 384)]
+FIRST_ROWS_SPANS = [(0, 256), (256, 256), (512, 512)]
 LAP = 16
 
 
@@ -219,10 +220,10 @@ def tile_attend_gml_lch_kernel(tc, xT, wd, wv, y, cw, rw, offs, out):
                 )
             return a
 
-        def targets(gi):
+        def targets(gi, count=1):
             k = max(k for k in range(len(Y_LOADS)) if Y_LOADS[k][0] <= gi * GROUP)
             y0 = gi * GROUP - Y_LOADS[k][0]
-            return y_sb[k][:, :, y0 : y0 + GROUP]
+            return y_sb[k][:, :, y0 : y0 + count * GROUP]
 
         def subtract_on_vector(groups, tag):
             tile = held([P, len(groups), PACK, GROUP], F32, name="diff_v", tag=tag)
@@ -230,14 +231,17 @@ def tile_attend_gml_lch_kernel(tc, xT, wd, wv, y, cw, rw, offs, out):
                 diff[gi] = tile[:, k, :, :]
                 nc.vector.tensor_tensor(out=diff[gi], in0=scores(gi)[:], in1=targets(gi), op=SUB)
 
-        def subtract_on_gpsimd(groups, stage_tag, tag):
-            staged = held([P, len(groups), PACK, GROUP], F32, name="staged", tag=stage_tag)
-            tile = held([P, len(groups), PACK, GROUP], F32, name="diff_g", tag=tag)
-            for k, gi in enumerate(groups):
-                nc.scalar.activation(out=staged[:, k, :, :], in_=scores(gi)[:], func=COPY)
-            for k, gi in enumerate(groups):
-                diff[gi] = tile[:, k, :, :]
-                nc.gpsimd.tensor_tensor(out=diff[gi], in0=staged[:, k, :, :], in1=targets(gi), op=SUB)
+        def subtract_on_gpsimd(parts, stage_tag, tag):
+            first, total = parts[0][0], sum(count for gi, count in parts)
+            staged = held([P, total, PACK, GROUP], F32, name="staged", tag=stage_tag)
+            tile = held([P, total, PACK, GROUP], F32, name="diff_g", tag=tag)
+            for k in range(total):
+                nc.scalar.activation(out=staged[:, k, :, :], in_=scores(first + k)[:], func=COPY)
+                diff[first + k] = tile[:, k, :, :]
+            for gi, count in parts:
+                ks = slice(gi - first, gi - first + count)
+                part_targets = targets(gi, count).rearrange("p t (k n) -> p k t n", n=GROUP)
+                nc.gpsimd.tensor_tensor(out=tile[:, ks, :, :], in0=staged[:, ks, :, :], in1=part_targets, op=SUB)
 
         slope = {}
 
@@ -273,12 +277,7 @@ def tile_attend_gml_lch_kernel(tc, xT, wd, wv, y, cw, rw, offs, out):
         dx_sb = {}
 
         def span(c, j):
-            c0, n = CHUNKS[c]
-            if j == 0 and c == 1:
-                return c0, PIECE
-            if j == 0 and c == 2:
-                return 2 * PIECE, 2 * PIECE
-            return c0, n
+            return FIRST_ROWS_SPANS[c] if j == 0 else CHUNKS[c]
 
         def second(c, j):
             end = lead + sum(span(c, j))
@@ -324,7 +323,7 @@ def tile_attend_gml_lch_kernel(tc, xT, wd, wv, y, cw, rw, offs, out):
         quantize_x(LAST, PIECE, x_last[:])
 
         subtract_on_vector([2, 3], "g_part0")
-        subtract_on_gpsimd([4], "wv_raw0", "diff1_0")
+        subtract_on_gpsimd([(4, 1)], "wv_raw0", "diff1_0")
         slope34 = held([P, PACK, PIECE], F32, name="slope34")
         bend(2, held([P, PACK, GROUP], F32, name="slope2"), 0)
         bend(3, slope34, 0)
@@ -339,7 +338,7 @@ def tile_attend_gml_lch_kernel(tc, xT, wd, wv, y, cw, rw, offs, out):
         quantize_g(1)
 
         make_weight(2, "g_part0")
-        subtract_on_gpsimd([5, 7, 6], "staged_late", "g_part1")
+        subtract_on_gpsimd([(5, 2), (7, 1)], "staged_late", "g_part1")
         evacuate(0, PACK - 1, "slope34")
         for j in range(PACK):
             second(1, j)
@@ -348,8 +347,8 @@ def tile_attend_gml_lch_kernel(tc, xT, wd, wv, y, cw, rw, offs, out):
         place(0, PACK - 1)
         bend(5, held([P, PACK, GROUP], F32, name="slope5"), 0)
         slope67 = held([P, PACK, PIECE], F32, name="slope67")
-        bend(7, slope67, 1)
         bend(6, slope67, 0)
+        bend(7, slope67, 1)
         weigh(nc.gpsimd, 2, 5 * GROUP, 6 * GROUP)
         weigh(nc.gpsimd, 2, 6 * GROUP, 8 * GROUP)
         for j in range(PACK - 1):

@@ -8,7 +8,6 @@ FLOPS = 2 * 2 * D * V * N
 F32 = mybir.dt.float32
 BF16 = mybir.dt.bfloat16
 U32 = mybir.dt.uint32
-I32 = mybir.dt.int32
 U16 = mybir.dt.uint16
 U8 = mybir.dt.uint8
 E4M3 = mybir.dt.float8_e4m3fn_x4
@@ -23,30 +22,32 @@ EQUAL = mybir.AluOpType.is_equal
 P = 128
 PACK = 4
 GROUP = 128
-PIECE = 256
-BANK = 512
-HALF = 256
+CHUNK = 256
 RUN = N // P
 QUAD = 32
 SIDE = 4
 GPSIMD_SIDE = 8
-T_HALF = 2
-Y_LOADS = [(0, 256), (256, 256), (512, 128), (640, 384)]
-LAST = N - PIECE
-WD_VECTOR = 88
-CHUNKS = [(0, 256), (256, 384), (640, 384)]
-FIRST_ROWS_SPANS = [(0, 256), (256, 256), (512, 512)]
-LAP = 16
+PAIRED = 3 * CHUNK
+WD_VECTOR = 84
+KIB = 1024
+AT_WD, AT_G, AT_R = 0, 8 * KIB, 11 * KIB
 
 
 def tile_attend_gml_lch_kernel(tc, xT, wd, wv, y, cw, rw, offs, out):
     nc = tc.nc
     with ExitStack() as ctx:
         keep = ctx.enter_context(tc.tile_pool(name="keep", bufs=1))
-        psum = ctx.enter_context(tc.psum_pool(name="psum", bufs=4))
+        shared = ctx.enter_context(tc.tile_pool(name="shared", bufs=1))
+        psum = ctx.enter_context(tc.psum_pool(name="psum", bufs=1))
 
         def held(shape, dtype, name, tag=None):
             return keep.tile(shape, dtype, name=name, tag=tag or name, align_bytes=64)
+
+        def over(offset, shape, dtype, name):
+            return shared.tile(shape, dtype, name=name, align_bytes=64, offset=offset)
+
+        def bank(b, shape, name):
+            return psum.tile(shape, F32, name=name, tag="bank%d" % b)
 
         def runs(ap, side=SIDE):
             return ap.rearrange("p t (c i) -> p c t i", i=side)
@@ -57,33 +58,24 @@ def tile_attend_gml_lch_kernel(tc, xT, wd, wv, y, cw, rw, offs, out):
         offsets = held([P, N // 16], U16, name="offsets")
         cw_sb = held([P, PACK], F32, name="cw_sb")
         rw_col = held([P, RUN], F32, name="rw_col")
-        rw_all = held([P, N], F32, name="rw_all")
-        y_sb = [held([P, PACK, n], F32, name="y%d" % k) for k, (y0, n) in enumerate(Y_LOADS)]
-        wd_raw = held([P, PACK, V], F32, name="wd_raw")
-        wv_raw = [held([P, PACK, HALF], F32, name="wv_raw%d" % h) for h in range(2)]
+        y_sb = [held([P, PACK, CHUNK], F32, name="y%d" % c) for c in range(N // CHUNK)]
+        wd_raw = over(AT_WD, [P, PACK, V], F32, "wd_raw")
+        wv_raw = [held([P, PACK, CHUNK], F32, name="wv_raw%d" % h) for h in range(2)]
+        planes = [held([P, T], F32, name="plane%d" % t) for t in range(PACK)]
         x_rows = xT.rearrange("(p t) n -> p t n", t=PACK)
         y_rows = y.rearrange("(p t) n -> p t n", t=PACK)
-
+        wv_rows = wv.rearrange("(p t) d -> p t d", t=PACK)
         nc.scalar.dma_start(rw_col[:], rw[0:1, :].rearrange("o (p e) -> p (o e)", e=RUN))
         nc.scalar.dma_start(cw_sb[:], cw.rearrange("(p t) o -> p (t o)", t=PACK))
-        planes = [held([P, T], F32, name="plane%d" % t) for t in range(PACK)]
         for t in range(PACK):
             nc.sync.dma_start(planes[t][:], x_rows[:, t, :])
             if t == 0:
                 nc.sync.dma_start(offsets[:], offs)
         nc.sync.dma_start(wd_raw[:], wd.rearrange("(p j) v -> p j v", j=PACK))
-
-        def load_y(k):
-            y0, n = Y_LOADS[k]
-            nc.sync.dma_start(y_sb[k][:], y_rows[:, :, y0 : y0 + n])
-
-        wv_rows = wv.rearrange("(p t) d -> p t d", t=PACK)
-        nc.sync.dma_start(wv_raw[0][:], wv_rows[:, :, :HALF])
-        load_y(0)
-        nc.sync.dma_start(wv_raw[1][:], wv_rows[:, :, HALF:])
-        load_y(1)
-        load_y(2)
-        load_y(3)
+        for c in range(N // CHUNK):
+            nc.sync.dma_start(y_sb[c][:], y_rows[:, :, c * CHUNK : (c + 1) * CHUNK])
+            if c < 2:
+                nc.sync.dma_start(wv_raw[c][:], wv_rows[:, :, c * CHUNK : (c + 1) * CHUNK])
 
         def listed(c0, n):
             return offsets[:, c0 // 16 : (c0 + n) // 16]
@@ -100,264 +92,278 @@ def tile_attend_gml_lch_kernel(tc, xT, wd, wv, y, cw, rw, offs, out):
         nc.vector.transpose(out=row[:], in_=column[:, :QUAD])
         nc.vector.tensor_scalar(out=ident[:], in0=column[:], scalar1=row[:, 0:1], scalar2=base[:], op0=SUB, op1=EQUAL)
         placed = [held([P, T], F32, name="placed%d" % j, tag=tag) for j, tag in enumerate(["column", "row", "ident", "plane0"])]
-        lead = BANK - CHUNKS[0][1]
-        g_codes = held([P, lead + N], U32, name="g_codes")
-        g_scales = held([P, lead + N], U8, name="g_scales")
-        nc.vector.memset(g_codes[:, :lead], 0)
-        nc.vector.memset(g_scales[:, :lead].bitcast(U32), 0)
 
-        rw_runs = rw_all[:].rearrange("p (n e) -> p n e", e=RUN)
+        weight = held([P, PACK, N], F32, name="weight")
+        weight_runs = weight[:].rearrange("p t (n e) -> p t n e", e=RUN)
         for e0 in range(0, RUN, PACK):
-            spread = psum.tile([P, PACK, P], F32, name="spread", tag="a")
+            spread = bank(e0 // PACK, [P, PACK, P], "spread")
             for e in range(PACK):
                 nc.tensor.transpose(out=spread[:, e, :], in_=rw_col[:, e0 + e : e0 + e + 1].to_broadcast([P, P]), identity=ident[:])
-            nc.scalar.activation(out=rw_runs[:, :, e0 : e0 + PACK], in_=spread[:].rearrange("p e n -> p n e"), func=COPY)
-
+            for t in range(PACK):
+                nc.scalar.activation(
+                    out=weight_runs[:, t, :, e0 : e0 + PACK], in_=spread[:].rearrange("p e n -> p n e"), func=COPY, scale=cw_sb[:, t : t + 1]
+                )
         for j in range(2):
             nc.vector.memset(placed[j][:].bitcast(U32), 0)
         nc.gpsimd.memset(placed[2][:].bitcast(U32), 0)
 
-        weight = {}
-
-        def make_weight(c, tag):
-            c0, n = CHUNKS[c]
-            weight[c] = held([P, PACK, n], F32, name="weight%d" % c, tag=tag)
-            for t in range(PACK):
-                nc.scalar.activation(out=weight[c][:, t, :], in_=rw_all[:, c0 : c0 + n], func=COPY, scale=cw_sb[:, t : t + 1])
-
-        picked = held([P, PACK * N], BF16, name="picked")
+        picked = held([P, PACK * PAIRED], BF16, name="picked")
         picked_halves = picked[:].rearrange("p (u n e) -> p u n e", u=2, e=2)
         picked_words = picked[:].bitcast(U32).rearrange("p (u n) -> p n u", u=2)
-        early = held([P, 2, N], BF16, name="early")
-        x_grouped = held([P, LAST * PACK], BF16, name="x_grouped")
-        x_codes = {0: held([P, PIECE], U32, name="x_codes")}
-        x_scales = held([P, N], U8, name="x_scales")
-
-        def x_codes_of(c0, n):
-            start = max(b for b in x_codes if b <= c0)
-            return x_codes[start][:, c0 - start : c0 - start + n].bitcast(E4M3)
-
-        def weave_on_scalar(target, c0):
-            nc.scalar.copy(out=target.bitcast(U32).rearrange("p (n u) -> p n u", u=2), in_=picked_words[:, c0 : c0 + PIECE, :])
-
-        def weave_on_vector(target, c0):
-            nc.vector.tensor_copy(
-                out=target.bitcast(I32).rearrange("p (n u) -> p n u", u=2),
-                in_=picked[:].bitcast(I32).rearrange("p (u n) -> p n u", u=2)[:, c0 : c0 + PIECE, :],
-            )
-
-        def grouped_of(c0, n):
-            return x_grouped[:, PACK * c0 : PACK * (c0 + n)]
-
-        def quantize_x(c0, n, source):
-            nc.vector.quantize_mx(
-                out=x_codes_of(c0, n),
-                scales=x_scales[:, c0 : c0 + n],
-                in_=source,
-            )
-
+        rest = held([P, PACK, CHUNK], BF16, name="rest")
         for t in range(PACK):
-            n = PIECE if t == PACK - 1 else N
-            for c0 in range(0, N, n):
-                target = early[:, t, c0 : c0 + n] if t < 2 else picked_halves[:, 1, c0 : c0 + n, t - 2]
-                nc.vector.tensor_copy(out=target, in_=planes[t][:].indirect(listed(c0, n)))
+            n = CHUNK if t == PACK - 1 else PAIRED
+            for c0 in range(0, PAIRED, n):
+                nc.vector.tensor_copy(out=picked_halves[:, t // 2, c0 : c0 + n, t % 2], in_=planes[t][:].indirect(listed(c0, n)))
+            nc.scalar.activation(out=rest[:, t, :], in_=planes[t][:].indirect(listed(PAIRED, CHUNK)), func=COPY)
             if t == 0:
                 nc.gpsimd.memset(placed[3][:].bitcast(U32), 0)
-        for c in range(2):
-            make_weight(c, None)
-        nc.scalar.activation(out=picked_halves[:, 0], in_=early[:].rearrange("p e n -> p n e"), func=COPY)
-        weave_on_scalar(grouped_of(0, PIECE), 0)
-        weave_on_scalar(grouped_of(PIECE, PIECE), PIECE)
-        weave_on_vector(grouped_of(2 * PIECE, PIECE), 2 * PIECE)
 
-        wd_grouped = held([P, PACK, P, PACK], BF16, name="wd_grouped")
+        def weave(target, c0):
+            nc.scalar.copy(out=target.bitcast(U32).rearrange("p (n u) -> p n u", u=2), in_=picked_words[:, c0 : c0 + CHUNK, :])
+
+        def quantize(codes, scales, packed, fmt):
+            nc.vector.quantize_mx(out=codes.bitcast(fmt), scales=scales, in_=packed)
+
+        x_codes = {}
+        x_scales = held([P, N], U8, name="x_scales")
+        x_packed = {}
+
+        def pack_x(c, tile):
+            x_packed[c] = tile
+            if c * CHUNK < PAIRED:
+                weave(tile[:], c * CHUNK)
+            else:
+                nc.scalar.activation(out=runs_packed(tile[:].rearrange("p (n t) -> p n t", t=PACK)), in_=runs(rest[:]), func=COPY)
+
+        def quantize_x(c, tile):
+            x_codes[c] = tile
+            quantize(tile[:], x_scales[:, c * CHUNK : (c + 1) * CHUNK], x_packed[c][:], E4M3)
+
+        for c in range(2):
+            pack_x(c, held([P, CHUNK * PACK], BF16, name="x_packed%d" % c))
+        quantize_x(0, held([P, CHUNK], U32, name="x_codes0"))
+
+        wd_packed = held([P, PACK, P, PACK], BF16, name="wd_packed")
         wd_codes = held([P, V], U32, name="wd_codes")
         wd_scales = held([P, V], U8, name="wd_scales")
         cut = P - WD_VECTOR
         wd_columns = wd_raw[:].rearrange("p j (m t) -> p m j t", t=PACK)
-        wd_dealt = wd_grouped[:].rearrange("p t m j -> p m j t")
-        nc.scalar.activation(out=wd_dealt[:, :, :, :T_HALF], in_=wd_columns[:, :, :, :T_HALF], func=COPY)
-        nc.scalar.activation(out=wd_dealt[:, :cut, :, T_HALF:], in_=wd_columns[:, :cut, :, T_HALF:], func=COPY)
-        nc.vector.tensor_copy(out=wd_dealt[:, cut:, :, T_HALF:], in_=wd_columns[:, cut:, :, T_HALF:])
-        quantize_x(0, PIECE, grouped_of(0, PIECE))
-        for t0 in range(0, PACK, T_HALF):
-            nc.vector.quantize_mx(
-                out=wd_codes[:, t0 * P : (t0 + T_HALF) * P].bitcast(E4M3),
-                scales=wd_scales[:, t0 * P : (t0 + T_HALF) * P],
-                in_=wd_grouped[:, t0 : t0 + T_HALF, :, :].rearrange("p t m j -> p (t m j)"),
-            )
-        x_codes[PIECE] = held([P, 2 * PIECE], U32, name="x_codes_mid", tag="wd_raw")
-        quantize_x(PIECE, 2 * PIECE, grouped_of(PIECE, 2 * PIECE))
+        wd_dealt = wd_packed[:].rearrange("p t m j -> p m j t")
 
-        wv_codes = held([P, D], U32, name="wv_codes")
-        wv_scales = held([P, D], U8, name="wv_scales")
-
-        def prepare_wv(d0, n, tag):
-            grouped = held([P, n, PACK], BF16, name="wv_grouped", tag=tag)
-            for a in range(0, n, P):
-                nc.scalar.activation(out=runs_packed(grouped[:, a : a + P, :]), in_=runs(wv_raw[d0 // HALF][:, :, a : a + P]), func=COPY)
-            nc.vector.quantize_mx(
-                out=wv_codes[:, d0 : d0 + n].bitcast(E4M3),
-                scales=wv_scales[:, d0 : d0 + n],
-                in_=grouped[:].rearrange("p d t -> p (d t)"),
+        def quantize_wd(t0):
+            quantize(
+                wd_codes[:, t0 * P : (t0 + 2) * P],
+                wd_scales[:, t0 * P : (t0 + 2) * P],
+                wd_packed[:, t0 : t0 + 2, :, :].rearrange("p t m j -> p (t m j)"),
+                E4M3,
             )
 
-        diff = {}
-        g_part = {}
+        for t0 in (0, 2):
+            nc.scalar.activation(out=wd_dealt[:, :cut, :, t0 : t0 + 2], in_=wd_columns[:, :cut, :, t0 : t0 + 2], func=COPY)
+            nc.vector.tensor_copy(out=wd_dealt[:, cut:, :, t0 : t0 + 2], in_=wd_columns[:, cut:, :, t0 : t0 + 2])
+        quantize_wd(0)
+        quantize_wd(2)
+        quantize_x(1, over(AT_WD, [P, CHUNK], U32, "x_codes1"))
+        for c in (2, 3):
+            pack_x(c, over(AT_WD + c * 2 * KIB, [P, CHUNK * PACK], BF16, "x_packed%d" % c))
 
-        def scores(gi, t0=0, count=PACK):
+        wv_packed = {}
+        wv_mx = {}
+
+        def cast_wv(j, tile):
+            wv_packed[j] = tile[:, (j % 2) * P : (j % 2 + 1) * P, :]
+            nc.scalar.activation(out=runs_packed(wv_packed[j]), in_=runs(wv_raw[j // 2][:, :, (j % 2) * P : (j % 2 + 1) * P]), func=COPY)
+
+        def quantize_wv(j, packed, codes, scales):
+            quantize(codes, scales, packed.rearrange("p d t -> p (d t)"), E4M3)
+            for k in range(packed.shape[1] // P):
+                wv_mx[j + k] = (codes[:, k * P : (k + 1) * P], scales[:, k * P : (k + 1) * P])
+
+        def scores(gi, b, t0=0, count=PACK):
             c0 = gi * GROUP
-            a = psum.tile([P, count, GROUP], F32, name="a")
+            a = bank(b, [P, count, GROUP], "a%d" % gi)
+            codes = x_codes[c0 // CHUNK]
             for t in range(t0, t0 + count):
                 nc.tensor.matmul_mx(
                     out=a[:, t - t0, :],
                     lhsT=wd_codes[:, t * P : (t + 1) * P].bitcast(E4M3),
                     lhsT_scale=wd_scales[:, t * P : (t + 1) * P],
-                    rhs=x_codes_of(c0, GROUP),
+                    rhs=codes[:, c0 % CHUNK : c0 % CHUNK + GROUP].bitcast(E4M3),
                     rhs_scale=x_scales[:, c0 : c0 + GROUP],
                     start=True,
                     stop=True,
                 )
             return a
 
-        def targets(gi, count=1):
-            k = max(k for k in range(len(Y_LOADS)) if Y_LOADS[k][0] <= gi * GROUP)
-            y0 = gi * GROUP - Y_LOADS[k][0]
-            return y_sb[k][:, :, y0 : y0 + count * GROUP]
+        def targets(gi):
+            return y_sb[gi // 2][:, :, (gi % 2) * GROUP : (gi % 2 + 1) * GROUP]
 
-        def subtract_on_vector(groups, tag):
-            tile = held([P, len(groups), PACK, GROUP], F32, name="diff_v", tag=tag)
-            for k, gi in enumerate(groups):
-                diff[gi] = tile[:, k, :, :]
-                nc.vector.tensor_tensor(out=diff[gi], in0=scores(gi)[:], in1=targets(gi), op=SUB)
-
-        def subtract_on_gpsimd(parts, stage_tag, tag):
-            first, total = parts[0][0], sum(count for gi, count in parts)
-            staged = held([P, total, PACK, GROUP], F32, name="staged", tag=stage_tag)
-            tile = held([P, total, PACK, GROUP], F32, name="diff_g", tag=tag)
-            for k in range(total):
-                nc.scalar.activation(out=staged[:, k, :, :], in_=scores(first + k)[:], func=COPY)
-                diff[first + k] = tile[:, k, :, :]
-            for gi, count in parts:
-                ks = slice(gi - first, gi - first + count)
-                part_targets = targets(gi, count).rearrange("p t (k n) -> p k t n", n=GROUP)
-                nc.gpsimd.tensor_tensor(out=tile[:, ks, :, :], in0=staged[:, ks, :, :], in1=part_targets, op=SUB)
-
+        diff = {}
         slope = {}
+        g_packed = {}
+        g_mx = {}
+        dx = {}
 
-        def bend(gi, tile, k):
-            slope[gi] = (tile, (gi - k) * GROUP)
-            nc.scalar.activation(out=tile[:, :, k * GROUP : (k + 1) * GROUP], in_=diff[gi], func=TANH)
+        def group(name, tag=None):
+            return held([P, PACK, GROUP], F32, name=name, tag=tag)
 
-        def weigh(engine, c, lo, hi):
-            tile, start = slope[lo // GROUP]
-            c0 = CHUNKS[c][0]
-            side = SIDE if c == 0 else GPSIMD_SIDE
-            engine.tensor_tensor(
-                out=runs_packed(g_part[c][:, lo - c0 : hi - c0, :], side),
-                in0=runs(tile[:, :, lo - start : hi - start], side),
-                in1=runs(weight[c][:, :, lo - c0 : hi - c0], side),
-                op=MULT,
-            )
+        def subtract(gi, b, tile):
+            diff[gi] = tile
+            nc.vector.tensor_tensor(out=tile[:], in0=scores(gi, b)[:], in1=targets(gi), op=SUB)
 
-        def quantize_g(c):
-            c0, n = CHUNKS[c]
-            for lo in range(c0, c0 + n, PIECE):
-                hi = min(lo + PIECE, c0 + n)
-                nc.vector.quantize_mx(
-                    out=g_codes[:, lead + lo : lead + hi].bitcast(E5M2),
-                    scales=g_scales[:, lead + lo : lead + hi],
-                    in_=g_part[c][:, lo - c0 : hi - c0, :].rearrange("p n t -> p (n t)"),
+        def bend(gi, tile):
+            slope[gi] = tile
+            nc.scalar.activation(out=tile[:], in_=diff[gi][:], func=TANH)
+
+        def weigh(engine, c, tile, side):
+            g_packed[c] = tile
+            for k in range(2):
+                gi = 2 * c + k
+                engine.tensor_tensor(
+                    out=runs_packed(tile[:, k * GROUP : (k + 1) * GROUP, :], side),
+                    in0=runs(slope[gi][:], side),
+                    in1=runs(weight[:, :, gi * GROUP : (gi + 1) * GROUP], side),
+                    op=MULT,
                 )
 
-        for c, (c0, n) in enumerate(CHUNKS):
-            g_part[c] = held([P, n, PACK], BF16, name="g_part%d" % c)
+        def weigh_late(c):
+            weigh(nc.gpsimd, c, held([P, CHUNK, PACK], BF16, name="g_packed%d" % c, tag="g_late"), GPSIMD_SIDE)
 
-        dx_ps = {}
-        dx_sb = {}
+        def quantize_g(c, codes, scales):
+            g_mx[c] = (codes, scales)
+            quantize(codes[:], scales[:], g_packed[c][:].rearrange("p n t -> p (n t)"), E5M2)
 
-        def span(c, j):
-            return FIRST_ROWS_SPANS[c] if j == 0 else CHUNKS[c]
-
-        def second(c, j):
-            end = lead + sum(span(c, j))
-            dx_ps[c, j] = psum.tile([P, BANK], F32, name="dx")
+        def second(target, c, j):
             nc.tensor.matmul_mx(
-                out=dx_ps[c, j][:],
-                lhsT=wv_codes[:, j * P : (j + 1) * P].bitcast(E4M3),
-                lhsT_scale=wv_scales[:, j * P : (j + 1) * P],
-                rhs=g_codes[:, end - BANK : end].bitcast(E5M2),
-                rhs_scale=g_scales[:, end - BANK : end],
+                out=target,
+                lhsT=wv_mx[j][0].bitcast(E4M3),
+                lhsT_scale=wv_mx[j][1],
+                rhs=g_mx[c][0][:].bitcast(E5M2),
+                rhs_scale=g_mx[c][1][:],
                 start=True,
                 stop=True,
             )
 
-        def evacuate(c, j, tag=None):
-            n = span(c, j)[1]
-            dx_sb[c, j] = held([P, n], F32, name="dx_sb", tag=tag or "dx_sb%d_%d" % (c, j))
-            nc.scalar.activation(out=dx_sb[c, j][:], in_=dx_ps[c, j][:, BANK - n :], func=COPY)
+        def results(b, name):
+            return bank(b, [P, 2, CHUNK], name)
 
-        def place(c, j):
-            c0, n = span(c, j)
-            nc.vector.tensor_copy(out=placed[j][:].indirect(listed(c0, n)), in_=dx_sb[c, j][:])
-            if c == len(CHUNKS) - 1:
-                nc.sync.dma_start(out[j * P : (j + 1) * P, :], placed[j][:])
+        def copy_out(engine, target, source):
+            if engine is nc.vector:
+                nc.vector.tensor_copy(out=target, in_=source)
+            else:
+                nc.scalar.activation(out=target, in_=source, func=COPY)
+
+        def evacuate(engine, c, j, source, tile):
+            dx[c, j] = tile
+            copy_out(engine, tile[:], source)
+
+        def piece(name, tag=None):
+            return held([P, CHUNK], F32, name=name, tag=tag)
+
+        def place(engine, j, c0, source):
+            window = placed[j][:].indirect(listed(c0, source.shape[1]))
+            if engine is nc.vector:
+                nc.vector.tensor_copy(out=window, in_=source)
+            else:
+                nc.scalar.activation(out=window, in_=source, func=COPY)
+
+        def place_chunk(engine, c, j):
+            place(engine, j, c * CHUNK, dx[c, j][:])
+
+        def store(j):
+            nc.sync.dma_start(out[j * P : (j + 1) * P, :], placed[j][:])
 
         for gi in range(2):
-            slope[gi] = (held([P, PACK, GROUP], F32, name="slope%d" % gi), gi * GROUP)
-            for t0 in range(0, PACK, T_HALF):
-                part = held([P, T_HALF, GROUP], F32, name="diff%d_%d" % (gi, t0))
-                nc.vector.tensor_tensor(out=part[:], in0=scores(gi, t0, T_HALF)[:], in1=targets(gi)[:, t0 : t0 + T_HALF, :], op=SUB)
-                nc.scalar.activation(out=slope[gi][0][:, t0 : t0 + T_HALF, :], in_=part[:], func=TANH)
-        for gi in range(2):
-            weigh(nc.vector, 0, gi * GROUP, (gi + 1) * GROUP)
-        quantize_g(0)
-        prepare_wv(0, HALF, "wv_low")
-        x_last = held([P, PIECE * PACK], BF16, name="x_last", tag="wd_grouped")
-        weave_on_scalar(x_last[:], LAST)
-        prepare_wv(HALF, HALF, "diff1_0")
-        for j in range(PACK):
-            second(0, j)
-        evacuate(0, 0)
-        x_codes[LAST] = held([P, PIECE], U32, name="x_codes_tail", tag="slope0")
-        quantize_x(LAST, PIECE, x_last[:])
-
-        subtract_on_vector([2, 3], "g_part0")
-        subtract_on_gpsimd([(4, 1)], "wv_raw0", "diff1_0")
-        slope34 = held([P, PACK, PIECE], F32, name="slope34")
-        bend(2, held([P, PACK, GROUP], F32, name="slope2"), 0)
-        bend(3, slope34, 0)
-        evacuate(0, 1)
-        bend(4, slope34, 1)
-        evacuate(0, 2)
-        weigh(nc.gpsimd, 1, 2 * GROUP, 3 * GROUP)
-        weigh(nc.gpsimd, 1, 3 * GROUP, 4 * GROUP - LAP)
-        weigh(nc.gpsimd, 1, 4 * GROUP - LAP, 5 * GROUP)
-        for j in range(PACK - 1):
-            place(0, j)
-        quantize_g(1)
-
-        make_weight(2, "g_part0")
-        subtract_on_gpsimd([(5, 2), (7, 1)], "staged_late", "g_part1")
-        evacuate(0, PACK - 1, "slope34")
-        for j in range(PACK):
-            second(1, j)
-            if j < PACK - 1:
-                evacuate(1, j)
-        place(0, PACK - 1)
-        bend(5, held([P, PACK, GROUP], F32, name="slope5"), 0)
-        slope67 = held([P, PACK, PIECE], F32, name="slope67")
-        bend(6, slope67, 0)
-        bend(7, slope67, 1)
-        weigh(nc.gpsimd, 2, 5 * GROUP, 6 * GROUP)
-        weigh(nc.gpsimd, 2, 6 * GROUP, 8 * GROUP)
-        for j in range(PACK - 1):
-            place(1, j)
-        quantize_g(2)
-        evacuate(1, PACK - 1, "slope67")
-        for j in range(PACK):
-            second(2, j)
-            evacuate(2, j)
-        place(1, PACK - 1)
-        for j in range(PACK):
-            place(2, j)
+            slope[gi] = group("slope%d" % gi)
+        for t0 in (0, 2):
+            for gi in range(2):
+                part = held([P, 2, GROUP], F32, name="part%d_%d" % (gi, t0))
+                nc.vector.tensor_tensor(out=part[:], in0=scores(gi, t0 + gi, t0, 2)[:], in1=targets(gi)[:, t0 : t0 + 2, :], op=SUB)
+                nc.scalar.activation(out=slope[gi][:, t0 : t0 + 2, :], in_=part[:], func=TANH)
+        quantize_x(2, held([P, CHUNK], U32, name="x_codes2", tag="part0_0"))
+        weigh(nc.vector, 0, over(AT_G, [P, CHUNK, PACK], BF16, "g_packed0"), SIDE)
+        wv_low = held([P, 2 * P, PACK], BF16, name="wv_low", tag="y0")
+        wv_codes = held([P, 2 * P], U32, name="wv_codes")
+        wv_scales = held([P, 2 * P], U8, name="wv_scales")
+        cast_wv(0, wv_low)
+        quantize_wv(0, wv_packed[0], wv_codes[:, :P], wv_scales[:, :P])
+        quantize_g(0, held([P, CHUNK], U32, name="g_codes0"), held([P, CHUNK], U8, name="g_scales0"))
+        cast_wv(1, wv_low)
+        quantize_wv(1, wv_packed[1], wv_codes[:, P:], wv_scales[:, P:])
+        quantize_x(3, held([P, CHUNK], U32, name="x_codes3", tag="slope1"))
+        first = [bank(4 + j, [P, CHUNK], "first%d" % j) for j in range(2)]
+        for j in range(2):
+            second(first[j][:], 0, j)
+        wv_high = held([P, 2 * P, PACK], BF16, name="wv_high", tag="g_late")
+        cast_wv(2, wv_high)
+        cast_wv(3, wv_high)
+        subtract(2, 6, over(AT_G, [P, PACK, GROUP], F32, "diff2"))
+        subtract(3, 7, group("diff3", "y0"))
+        evacuate(nc.vector, 0, 0, first[0][:], piece("dx0_0", "wv_raw1"))
+        quantize_wv(2, wv_high[:], held([P, 2 * P], U32, name="wv_codes_high")[:], held([P, 2 * P], U8, name="wv_scales_high")[:])
+        bend(2, group("slope2"))
+        evacuate(nc.scalar, 0, 1, first[1][:], piece("dx0_1", "y1"))
+        bend(3, group("slope3"))
+        weigh_late(1)
+        place_chunk(nc.vector, 0, 0)
+        place_chunk(nc.scalar, 0, 1)
+        subtract(4, 0, over(AT_R + 2 * KIB, [P, PACK, GROUP], F32, "diff4"))
+        subtract(5, 1, group("diff5"))
+        bend(4, group("slope4"))
+        bend(5, over(AT_R, [P, PACK, GROUP], F32, "slope5"))
+        quantize_g(1, held([P, CHUNK], U32, name="g_codes1", tag="y2"), held([P, CHUNK], U8, name="g_scales1", tag="wv_raw1"))
+        weigh_late(2)
+        pair = results(7, "pair1")
+        for j in range(2):
+            second(pair[:, j, :], 1, j)
+        subtract(6, 2, over(AT_R + 2 * KIB, [P, PACK, GROUP], F32, "diff6"))
+        subtract(7, 3, group("diff7", "diff5"))
+        late = {2: results(4, "late2"), 3: results(0, "late3")}
+        for j in (2, 3):
+            second(late[j][:, 0, :], 1, j)
+        late0 = results(6, "late0")
+        for j in (2, 3):
+            second(late0[:, j - 2, :], 0, j)
+        both = held([P, 2, CHUNK], F32, name="dx1")
+        copy_out(nc.scalar, both[:], pair[:])
+        bend(6, group("slope6", "y2"))
+        place(nc.vector, 0, CHUNK, both[:, 0, :])
+        place(nc.scalar, 1, CHUNK, both[:, 1, :])
+        bend(7, over(AT_R - KIB // 2, [P, PACK, GROUP], F32, "slope7"))
+        evacuate(nc.vector, 0, 2, late0[:, 0, :], over(AT_R + 3 * KIB // 2, [P, CHUNK], F32, "dx0_2"))
+        quantize_g(2, over(AT_R + 3 * KIB, [P, CHUNK], U32, "g_codes2"), held([P, CHUNK], U8, name="g_scales2"))
+        weigh_late(3)
+        pair = results(5, "pair2")
+        for j in range(2):
+            second(pair[:, j, :], 2, j)
+        for j in (2, 3):
+            second(late[j][:, 1, :], 2, j)
+        place_chunk(nc.vector, 0, 2)
+        evacuate(nc.scalar, 2, 0, pair[:, 0, :], piece("dx2_0"))
+        place_chunk(nc.scalar, 2, 0)
+        tail = {2: held([P, 3 * CHUNK], F32, name="tail2"), 3: held([P, 3 * CHUNK], F32, name="tail3", tag="dx2_0")}
+        copy_out(nc.vector, tail[2][:, : 2 * CHUNK], late[2][:].rearrange("p c n -> p (c n)"))
+        evacuate(nc.vector, 2, 1, pair[:, 1, :], over(AT_R + KIB, [P, CHUNK], F32, "dx2_1"))
+        quantize_g(3, held([P, CHUNK], U32, name="g_codes3"), over(AT_R + 2 * KIB, [P, CHUNK], U8, "g_scales3"))
+        place_chunk(nc.vector, 2, 1)
+        copy_out(nc.scalar, tail[3][:, : 2 * CHUNK], late[3][:].rearrange("p c n -> p (c n)"))
+        last = [results(1 + k, "last%d" % k) for k in range(2)]
+        for k, js in enumerate([(0, 3), (1, 2)]):
+            for a, j in enumerate(js):
+                second(last[k][:, a, :], 3, j)
+        evacuate(nc.scalar, 3, 0, last[0][:, 0, :], piece("dx3_0"))
+        evacuate(nc.scalar, 0, 3, late0[:, 1, :], piece("dx0_3", "g_codes3"))
+        evacuate(nc.vector, 3, 1, last[1][:, 0, :], piece("dx3_1"))
+        copy_out(nc.vector, tail[2][:, 2 * CHUNK :], last[1][:, 1, :])
+        place_chunk(nc.scalar, 3, 0)
+        store(0)
+        place_chunk(nc.vector, 3, 1)
+        store(1)
+        place(nc.vector, 2, CHUNK, tail[2][:])
+        store(2)
+        place_chunk(nc.scalar, 0, 3)
+        copy_out(nc.scalar, tail[3][:, 2 * CHUNK :], last[0][:, 1, :])
+        place(nc.scalar, 3, CHUNK, tail[3][:, :384])
+        place(nc.scalar, 3, CHUNK + 384, tail[3][:, 384:])
+        store(3)

@@ -30,7 +30,7 @@ GPSIMD_SIDE = 8
 PAIRED = 3 * CHUNK
 WD_VECTOR = 84
 KIB = 1024
-AT_WD, AT_G, AT_R = 0, 8 * KIB, 11 * KIB
+AT_WD, AT_G, AT_R, AT_S, AT_U = 0, 8 * KIB, 10 * KIB, 16 * KIB, 22 * KIB
 
 
 def tile_attend_gml_lch_kernel(tc, xT, wd, wv, y, cw, rw, offs, out):
@@ -93,19 +93,23 @@ def tile_attend_gml_lch_kernel(tc, xT, wd, wv, y, cw, rw, offs, out):
         nc.vector.tensor_scalar(out=ident[:], in0=column[:], scalar1=row[:, 0:1], scalar2=base[:], op0=SUB, op1=EQUAL)
         placed = [held([P, T], F32, name="placed%d" % j, tag=tag) for j, tag in enumerate(["column", "row", "ident", "plane0"])]
 
-        weight = held([P, PACK, N], F32, name="weight")
-        weight_runs = weight[:].rearrange("p t (n e) -> p t n e", e=RUN)
+        rw_all = held([P, N], F32, name="rw_all")
+        rw_runs = rw_all[:].rearrange("p (n e) -> p n e", e=RUN)
         for e0 in range(0, RUN, PACK):
             spread = bank(e0 // PACK, [P, PACK, P], "spread")
             for e in range(PACK):
                 nc.tensor.transpose(out=spread[:, e, :], in_=rw_col[:, e0 + e : e0 + e + 1].to_broadcast([P, P]), identity=ident[:])
-            for t in range(PACK):
-                nc.scalar.activation(
-                    out=weight_runs[:, t, :, e0 : e0 + PACK], in_=spread[:].rearrange("p e n -> p n e"), func=COPY, scale=cw_sb[:, t : t + 1]
-                )
+            nc.scalar.activation(out=rw_runs[:, :, e0 : e0 + PACK], in_=spread[:].rearrange("p e n -> p n e"), func=COPY)
+        weight = held([P, PACK, N], F32, name="weight")
+        for t in range(PACK):
+            nc.scalar.activation(out=weight[:, t, :CHUNK], in_=rw_all[:, :CHUNK], func=COPY, scale=cw_sb[:, t : t + 1])
         for j in range(2):
             nc.vector.memset(placed[j][:].bitcast(U32), 0)
         nc.gpsimd.memset(placed[2][:].bitcast(U32), 0)
+        for t in range(PACK):
+            nc.gpsimd.tensor_scalar(
+                out=weight[:, t, CHUNK:], in0=rw_all[:, CHUNK:], scalar1=cw_sb[:, t : t + 1], scalar2=0.0, op0=MULT, op1=ADD
+            )
 
         picked = held([P, PACK * PAIRED], BF16, name="picked")
         picked_halves = picked[:].rearrange("p (u n e) -> p u n e", u=2, e=2)
@@ -308,62 +312,61 @@ def tile_attend_gml_lch_kernel(tc, xT, wd, wv, y, cw, rw, offs, out):
         weigh_late(1)
         place_chunk(nc.vector, 0, 0)
         place_chunk(nc.scalar, 0, 1)
-        subtract(4, 0, over(AT_R + 2 * KIB, [P, PACK, GROUP], F32, "diff4"))
-        subtract(5, 1, group("diff5"))
+        subtract(4, 0, over(AT_S + KIB, [P, PACK, GROUP], F32, "diff4"))
+        subtract(5, 1, over(AT_R + 2 * KIB, [P, PACK, GROUP], F32, "diff5"))
         bend(4, group("slope4"))
-        bend(5, over(AT_R, [P, PACK, GROUP], F32, "slope5"))
+        bend(5, group("slope5"))
         quantize_g(1, held([P, CHUNK], U32, name="g_codes1", tag="y2"), held([P, CHUNK], U8, name="g_scales1", tag="wv_raw1"))
         weigh_late(2)
         pair = results(7, "pair1")
         for j in range(2):
             second(pair[:, j, :], 1, j)
-        subtract(6, 2, over(AT_R + 2 * KIB, [P, PACK, GROUP], F32, "diff6"))
-        subtract(7, 3, group("diff7", "diff5"))
+        subtract(6, 2, over(AT_S + KIB, [P, PACK, GROUP], F32, "diff6"))
+        subtract(7, 3, over(AT_R + KIB // 2, [P, PACK, GROUP], F32, "diff7"))
         late = {2: results(4, "late2"), 3: results(0, "late3")}
         for j in (2, 3):
             second(late[j][:, 0, :], 1, j)
         late0 = results(6, "late0")
         for j in (2, 3):
             second(late0[:, j - 2, :], 0, j)
-        both = held([P, 2, CHUNK], F32, name="dx1")
+        evacuate(nc.scalar, 0, 2, late0[:, 0, :], over(AT_R + 5 * KIB // 2, [P, CHUNK], F32, "dx0_2"))
+        bend(6, over(AT_R + 7 * KIB // 2, [P, PACK, GROUP], F32, "slope6"))
+        bend(7, over(AT_U + 3 * KIB, [P, PACK, GROUP], F32, "slope7"))
+        place_chunk(nc.vector, 0, 2)
+        both = over(AT_S + 2 * KIB, [P, 2, CHUNK], F32, "dx1")
         copy_out(nc.scalar, both[:], pair[:])
-        bend(6, group("slope6", "y2"))
+        quantize_g(2, over(AT_S + KIB, [P, CHUNK], U32, "g_codes2"), held([P, CHUNK], U8, name="g_scales2"))
+        weigh_late(3)
         place(nc.vector, 0, CHUNK, both[:, 0, :])
         place(nc.scalar, 1, CHUNK, both[:, 1, :])
-        bend(7, over(AT_R - KIB // 2, [P, PACK, GROUP], F32, "slope7"))
-        evacuate(nc.vector, 0, 2, late0[:, 0, :], over(AT_R + 3 * KIB // 2, [P, CHUNK], F32, "dx0_2"))
-        quantize_g(2, over(AT_R + 3 * KIB, [P, CHUNK], U32, "g_codes2"), held([P, CHUNK], U8, name="g_scales2"))
-        weigh_late(3)
-        pair = results(5, "pair2")
+        pair = results(7, "pair2")
         for j in range(2):
             second(pair[:, j, :], 2, j)
         for j in (2, 3):
             second(late[j][:, 1, :], 2, j)
-        place_chunk(nc.vector, 0, 2)
+        closing = {3: over(AT_S + 3 * KIB, [P, 4 * CHUNK], F32, "closing3"), 2: over(AT_U + 4 * KIB, [P, 4 * CHUNK], F32, "closing2")}
         evacuate(nc.scalar, 2, 0, pair[:, 0, :], piece("dx2_0"))
+        evacuate(nc.scalar, 0, 3, late0[:, 1, :], piece("dx0_3"))
+        copy_out(nc.vector, closing[3][:, : 2 * CHUNK], late[3][:].rearrange("p c n -> p (c n)"))
         place_chunk(nc.scalar, 2, 0)
-        tail = {2: held([P, 3 * CHUNK], F32, name="tail2"), 3: held([P, 3 * CHUNK], F32, name="tail3", tag="dx2_0")}
-        copy_out(nc.vector, tail[2][:, : 2 * CHUNK], late[2][:].rearrange("p c n -> p (c n)"))
-        evacuate(nc.vector, 2, 1, pair[:, 1, :], over(AT_R + KIB, [P, CHUNK], F32, "dx2_1"))
-        quantize_g(3, held([P, CHUNK], U32, name="g_codes3"), over(AT_R + 2 * KIB, [P, CHUNK], U8, "g_scales3"))
-        place_chunk(nc.vector, 2, 1)
-        copy_out(nc.scalar, tail[3][:, : 2 * CHUNK], late[3][:].rearrange("p c n -> p (c n)"))
+        quantize_g(3, held([P, CHUNK], U32, name="g_codes3"), held([P, CHUNK], U8, name="g_scales3"))
+        evacuate(nc.vector, 2, 1, pair[:, 1, :], over(AT_U + 3 * KIB, [P, CHUNK], F32, "dx2_1"))
+        copy_out(nc.vector, closing[2][:, : 2 * CHUNK], late[2][:].rearrange("p c n -> p (c n)"))
         last = [results(1 + k, "last%d" % k) for k in range(2)]
-        for k, js in enumerate([(0, 3), (1, 2)]):
+        for k, js in enumerate([(3, 0), (2, 1)]):
             for a, j in enumerate(js):
                 second(last[k][:, a, :], 3, j)
-        evacuate(nc.scalar, 3, 0, last[0][:, 0, :], piece("dx3_0"))
-        evacuate(nc.scalar, 0, 3, late0[:, 1, :], piece("dx0_3", "g_codes3"))
-        evacuate(nc.vector, 3, 1, last[1][:, 0, :], piece("dx3_1"))
-        copy_out(nc.vector, tail[2][:, 2 * CHUNK :], last[1][:, 1, :])
-        place_chunk(nc.scalar, 3, 0)
+        copy_out(nc.scalar, closing[3][:, 2 * CHUNK :], last[0][:].rearrange("p c n -> p (c n)"))
+        copy_out(nc.scalar, closing[2][:, 2 * CHUNK :], last[1][:].rearrange("p c n -> p (c n)"))
+        place_chunk(nc.vector, 2, 1)
+        place(nc.vector, 2, CHUNK, closing[2][:, :CHUNK])
+        place(nc.scalar, 0, 3 * CHUNK, closing[3][:, 3 * CHUNK :])
         store(0)
-        place_chunk(nc.vector, 3, 1)
+        place(nc.vector, 1, 3 * CHUNK, closing[2][:, 3 * CHUNK :])
         store(1)
-        place(nc.vector, 2, CHUNK, tail[2][:])
+        place(nc.vector, 2, 2 * CHUNK, closing[2][:, CHUNK : 3 * CHUNK])
         store(2)
+        for a in (384, 0):
+            place(nc.scalar, 3, CHUNK + a, closing[3][:, a : a + 384])
         place_chunk(nc.scalar, 0, 3)
-        copy_out(nc.scalar, tail[3][:, 2 * CHUNK :], last[0][:, 1, :])
-        place(nc.scalar, 3, CHUNK, tail[3][:, :384])
-        place(nc.scalar, 3, CHUNK + 384, tail[3][:, 384:])
         store(3)

@@ -30,7 +30,8 @@ GPSIMD_SIDE = 8
 PAIRED = 3 * CHUNK
 WD_VECTOR = 84
 KIB = 1024
-AT_WD, AT_G, AT_R, AT_S, AT_U = 0, 8 * KIB, 10 * KIB, 16 * KIB, 22 * KIB
+AT_WD, AT_G, AT_R, AT_S = 0, 8 * KIB, 20 * KIB, 22 * KIB
+AT_Y3 = AT_G + 13 * KIB // 2
 
 
 def tile_attend_gml_lch_kernel(tc, xT, wd, wv, y, cw, rw, offs, out):
@@ -58,13 +59,12 @@ def tile_attend_gml_lch_kernel(tc, xT, wd, wv, y, cw, rw, offs, out):
         offsets = held([P, N // 16], U16, name="offsets")
         cw_sb = held([P, PACK], F32, name="cw_sb")
         rw_col = held([P, RUN], F32, name="rw_col")
-        y_sb = [held([P, PACK, CHUNK], F32, name="y%d" % c) for c in range(N // CHUNK)]
+        y_sb = [held([P, PACK, CHUNK], F32, name="y%d" % c) if c != 3 else over(AT_Y3, [P, PACK, CHUNK], F32, "y3") for c in range(N // CHUNK)]
         wd_raw = over(AT_WD, [P, PACK, V], F32, "wd_raw")
-        wv_raw = [held([P, PACK, CHUNK], F32, name="wv_raw%d" % h) for h in range(2)]
+        wv_raw = held([P, PACK, D], F32, name="wv_raw")
         planes = [held([P, T], F32, name="plane%d" % t) for t in range(PACK)]
         x_rows = xT.rearrange("(p t) n -> p t n", t=PACK)
         y_rows = y.rearrange("(p t) n -> p t n", t=PACK)
-        wv_rows = wv.rearrange("(p t) d -> p t d", t=PACK)
         nc.scalar.dma_start(rw_col[:], rw[0:1, :].rearrange("o (p e) -> p (o e)", e=RUN))
         nc.scalar.dma_start(cw_sb[:], cw.rearrange("(p t) o -> p (t o)", t=PACK))
         for t in range(PACK):
@@ -74,8 +74,8 @@ def tile_attend_gml_lch_kernel(tc, xT, wd, wv, y, cw, rw, offs, out):
         nc.sync.dma_start(wd_raw[:], wd.rearrange("(p j) v -> p j v", j=PACK))
         for c in range(N // CHUNK):
             nc.sync.dma_start(y_sb[c][:], y_rows[:, :, c * CHUNK : (c + 1) * CHUNK])
-            if c < 2:
-                nc.sync.dma_start(wv_raw[c][:], wv_rows[:, :, c * CHUNK : (c + 1) * CHUNK])
+            if c == 1:
+                nc.sync.dma_start(wv_raw[:], wv.rearrange("(p t) d -> p t d", t=PACK))
 
         def listed(c0, n):
             return offsets[:, c0 // 16 : (c0 + n) // 16]
@@ -171,13 +171,14 @@ def tile_attend_gml_lch_kernel(tc, xT, wd, wv, y, cw, rw, offs, out):
         quantize_x(1, over(AT_WD, [P, CHUNK], U32, "x_codes1"))
         for c in (2, 3):
             pack_x(c, over(AT_WD + c * 2 * KIB, [P, CHUNK * PACK], BF16, "x_packed%d" % c))
+        quantize_x(2, held([P, CHUNK], U32, name="x_codes2"))
 
         wv_packed = {}
         wv_mx = {}
 
         def cast_wv(j, tile):
             wv_packed[j] = tile[:, (j % 2) * P : (j % 2 + 1) * P, :]
-            nc.scalar.activation(out=runs_packed(wv_packed[j]), in_=runs(wv_raw[j // 2][:, :, (j % 2) * P : (j % 2 + 1) * P]), func=COPY)
+            nc.scalar.activation(out=runs_packed(wv_packed[j]), in_=runs(wv_raw[:, :, j * P : (j + 1) * P]), func=COPY)
 
         def quantize_wv(j, packed, codes, scales):
             quantize(codes, scales, packed.rearrange("p d t -> p (d t)"), E4M3)
@@ -232,7 +233,7 @@ def tile_attend_gml_lch_kernel(tc, xT, wd, wv, y, cw, rw, offs, out):
                 )
 
         def weigh_late(c):
-            weigh(nc.gpsimd, c, held([P, CHUNK, PACK], BF16, name="g_packed%d" % c, tag="g_late"), GPSIMD_SIDE)
+            weigh(nc.gpsimd, c, over(AT_G + (5 if c == 1 else 3) * KIB // 2, [P, CHUNK, PACK], BF16, "g_packed%d" % c), GPSIMD_SIDE)
 
         def quantize_g(c, codes, scales):
             g_mx[c] = (codes, scales)
@@ -285,88 +286,77 @@ def tile_attend_gml_lch_kernel(tc, xT, wd, wv, y, cw, rw, offs, out):
                 part = held([P, 2, GROUP], F32, name="part%d_%d" % (gi, t0))
                 nc.vector.tensor_tensor(out=part[:], in0=scores(gi, t0 + gi, t0, 2)[:], in1=targets(gi)[:, t0 : t0 + 2, :], op=SUB)
                 nc.scalar.activation(out=slope[gi][:, t0 : t0 + 2, :], in_=part[:], func=TANH)
-        quantize_x(2, held([P, CHUNK], U32, name="x_codes2", tag="part0_0"))
-        weigh(nc.vector, 0, over(AT_G, [P, CHUNK, PACK], BF16, "g_packed0"), SIDE)
-        wv_low = held([P, 2 * P, PACK], BF16, name="wv_low", tag="y0")
-        wv_codes = held([P, 2 * P], U32, name="wv_codes")
-        wv_scales = held([P, 2 * P], U8, name="wv_scales")
-        cast_wv(0, wv_low)
-        quantize_wv(0, wv_packed[0], wv_codes[:, :P], wv_scales[:, :P])
+        quantize_x(3, held([P, CHUNK], U32, name="x_codes3", tag="part0_0"))
+        subtract(2, 6, group("diff2", "part1_0"))
+        bend(2, group("slope2"))
+        weigh(nc.vector, 0, held([P, CHUNK, PACK], BF16, name="g_packed0"), SIDE)
+        subtract(3, 7, group("diff3", "slope0"))
         quantize_g(0, held([P, CHUNK], U32, name="g_codes0"), held([P, CHUNK], U8, name="g_scales0"))
-        cast_wv(1, wv_low)
-        quantize_wv(1, wv_packed[1], wv_codes[:, P:], wv_scales[:, P:])
-        quantize_x(3, held([P, CHUNK], U32, name="x_codes3", tag="slope1"))
+        wv_low = over(AT_G + 7 * KIB // 2, [P, 2 * P, PACK], BF16, "wv_low")
+        wv_high = over(AT_G, [P, 2 * P, PACK], BF16, "wv_high")
+        for j in range(PACK):
+            cast_wv(j, wv_low if j < 2 else wv_high)
+        quantize_wv(0, wv_low[:], held([P, 2 * P], U32, name="wv_codes")[:], held([P, 2 * P], U8, name="wv_scales")[:])
+        bend(3, over(AT_G + 9 * KIB // 2, [P, PACK, GROUP], F32, "slope3"))
+        weigh_late(1)
         first = [bank(4 + j, [P, CHUNK], "first%d" % j) for j in range(2)]
         for j in range(2):
             second(first[j][:], 0, j)
-        wv_high = held([P, 2 * P, PACK], BF16, name="wv_high", tag="g_late")
-        cast_wv(2, wv_high)
-        cast_wv(3, wv_high)
-        subtract(2, 6, over(AT_G, [P, PACK, GROUP], F32, "diff2"))
-        subtract(3, 7, group("diff3", "y0"))
-        evacuate(nc.vector, 0, 0, first[0][:], piece("dx0_0", "wv_raw1"))
-        quantize_wv(2, wv_high[:], held([P, 2 * P], U32, name="wv_codes_high")[:], held([P, 2 * P], U8, name="wv_scales_high")[:])
-        bend(2, group("slope2"))
-        evacuate(nc.scalar, 0, 1, first[1][:], piece("dx0_1", "y1"))
-        bend(3, group("slope3"))
-        weigh_late(1)
+        for gi in (4, 5):
+            subtract(gi, gi - 4, group("diff%d" % gi))
+            bend(gi, over(AT_R, [P, PACK, GROUP], F32, "slope4") if gi == 4 else group("slope5"))
+        subtract(6, 2, group("diff6", "part1_0"))
+        subtract(7, 3, group("diff7", "slope0"))
+        bend(6, over(AT_S, [P, PACK, GROUP], F32, "slope6"))
+        evacuate(nc.scalar, 0, 1, first[1][:], over(AT_Y3 + 3 * KIB, [P, CHUNK], F32, "dx0_1"))
+        bend(7, group("slope7"))
+        evacuate(nc.vector, 0, 0, first[0][:], over(AT_Y3, [P, CHUNK], F32, "dx0_0"))
+        quantize_g(1, over(AT_Y3 + KIB, [P, CHUNK], U32, "g_codes1"), held([P, CHUNK], U8, name="g_scales1"))
+        quantize_wv(2, wv_high[:], over(AT_Y3 + 2 * KIB, [P, 2 * P], U32, "wv_codes_high")[:], over(AT_Y3 - KIB, [P, 2 * P], U8, "wv_scales_high")[:])
+        weigh_late(2)
         place_chunk(nc.vector, 0, 0)
         place_chunk(nc.scalar, 0, 1)
-        subtract(4, 0, over(AT_S + KIB, [P, PACK, GROUP], F32, "diff4"))
-        subtract(5, 1, over(AT_R + 2 * KIB, [P, PACK, GROUP], F32, "diff5"))
-        bend(4, group("slope4"))
-        bend(5, group("slope5"))
-        quantize_g(1, held([P, CHUNK], U32, name="g_codes1", tag="y2"), held([P, CHUNK], U8, name="g_scales1", tag="wv_raw1"))
-        weigh_late(2)
-        pair = results(7, "pair1")
-        for j in range(2):
-            second(pair[:, j, :], 1, j)
-        subtract(6, 2, over(AT_S + KIB, [P, PACK, GROUP], F32, "diff6"))
-        subtract(7, 3, over(AT_R + KIB // 2, [P, PACK, GROUP], F32, "diff7"))
-        late = {2: results(4, "late2"), 3: results(0, "late3")}
-        for j in (2, 3):
-            second(late[j][:, 0, :], 1, j)
-        late0 = results(6, "late0")
-        for j in (2, 3):
-            second(late0[:, j - 2, :], 0, j)
-        evacuate(nc.scalar, 0, 2, late0[:, 0, :], over(AT_R + 5 * KIB // 2, [P, CHUNK], F32, "dx0_2"))
-        bend(6, over(AT_R + 7 * KIB // 2, [P, PACK, GROUP], F32, "slope6"))
-        bend(7, over(AT_U + 3 * KIB, [P, PACK, GROUP], F32, "slope7"))
-        place_chunk(nc.vector, 0, 2)
-        both = over(AT_S + 2 * KIB, [P, 2, CHUNK], F32, "dx1")
-        copy_out(nc.scalar, both[:], pair[:])
-        quantize_g(2, over(AT_S + KIB, [P, CHUNK], U32, "g_codes2"), held([P, CHUNK], U8, name="g_scales2"))
+        closing = held([P, 2, 5 * CHUNK], F32, name="closing")
+
+        def products(b, c, js):
+            tile = results(b, "dx%d_%d" % (c, js[0]))
+            for k, j in enumerate(js):
+                second(tile[:, k, :], c, j)
+            return tile
+
+        def close(engine, c, source):
+            copy_out(engine, closing[:, :, c * CHUNK : (c + 1) * CHUNK], source[:])
+
+        early1 = products(6, 1, (0, 1))
+        late0 = products(7, 0, (2, 3))
+        late1 = products(0, 1, (2, 3))
+        both = over(AT_R, [P, 2, CHUNK], F32, "dx1")
+        copy_out(nc.vector, both[:], early1[:])
+        close(nc.scalar, 0, late0)
+        close(nc.vector, 1, late1)
+        quantize_g(2, held([P, CHUNK], U32, name="g_codes2"), over(AT_Y3, [P, CHUNK], U8, "g_scales2"))
         weigh_late(3)
         place(nc.vector, 0, CHUNK, both[:, 0, :])
         place(nc.scalar, 1, CHUNK, both[:, 1, :])
-        pair = results(7, "pair2")
-        for j in range(2):
-            second(pair[:, j, :], 2, j)
-        for j in (2, 3):
-            second(late[j][:, 1, :], 2, j)
-        closing = {3: over(AT_S + 3 * KIB, [P, 4 * CHUNK], F32, "closing3"), 2: over(AT_U + 4 * KIB, [P, 4 * CHUNK], F32, "closing2")}
-        evacuate(nc.scalar, 2, 0, pair[:, 0, :], piece("dx2_0"))
-        evacuate(nc.scalar, 0, 3, late0[:, 1, :], piece("dx0_3"))
-        copy_out(nc.vector, closing[3][:, : 2 * CHUNK], late[3][:].rearrange("p c n -> p (c n)"))
-        place_chunk(nc.scalar, 2, 0)
-        quantize_g(3, held([P, CHUNK], U32, name="g_codes3"), held([P, CHUNK], U8, name="g_scales3"))
-        evacuate(nc.vector, 2, 1, pair[:, 1, :], over(AT_U + 3 * KIB, [P, CHUNK], F32, "dx2_1"))
-        copy_out(nc.vector, closing[2][:, : 2 * CHUNK], late[2][:].rearrange("p c n -> p (c n)"))
-        last = [results(1 + k, "last%d" % k) for k in range(2)]
-        for k, js in enumerate([(3, 0), (2, 1)]):
-            for a, j in enumerate(js):
-                second(last[k][:, a, :], 3, j)
-        copy_out(nc.scalar, closing[3][:, 2 * CHUNK :], last[0][:].rearrange("p c n -> p (c n)"))
-        copy_out(nc.scalar, closing[2][:, 2 * CHUNK :], last[1][:].rearrange("p c n -> p (c n)"))
-        place_chunk(nc.vector, 2, 1)
-        place(nc.vector, 2, CHUNK, closing[2][:, :CHUNK])
-        place(nc.scalar, 0, 3 * CHUNK, closing[3][:, 3 * CHUNK :])
+        place(nc.scalar, 3, 0, closing[:, 1, :CHUNK])
+        early2 = products(1, 2, (0, 1))
+        late2 = products(2, 2, (2, 3))
+        both = over(AT_S, [P, 2, CHUNK], F32, "dx2")
+        copy_out(nc.vector, both[:], early2[:])
+        close(nc.vector, 2, late2)
+        quantize_g(3, held([P, CHUNK], U32, name="g_codes3"), over(AT_R, [P, CHUNK], U8, "g_scales3"))
+        place(nc.scalar, 0, 2 * CHUNK, both[:, 0, :])
+        place(nc.vector, 1, 2 * CHUNK, both[:, 1, :])
+        for k, js in ((1, (3, 0)), (0, (2, 1))):
+            last = products(3 + k, 3, js)
+            copy_out(nc.scalar if k == 1 else nc.vector, closing[:, k, 3 * CHUNK :], last[:].rearrange("p c n -> p (c n)"))
+        place(nc.scalar, 0, 3 * CHUNK, closing[:, 1, 4 * CHUNK :])
         store(0)
-        place(nc.vector, 1, 3 * CHUNK, closing[2][:, 3 * CHUNK :])
+        place(nc.vector, 2, 3 * CHUNK, closing[:, 0, 3 * CHUNK : 4 * CHUNK])
+        place(nc.vector, 1, 3 * CHUNK, closing[:, 0, 4 * CHUNK :])
         store(1)
-        place(nc.vector, 2, 2 * CHUNK, closing[2][:, CHUNK : 3 * CHUNK])
-        store(2)
-        for a in (384, 0):
-            place(nc.scalar, 3, CHUNK + a, closing[3][:, a : a + 384])
-        place_chunk(nc.scalar, 0, 3)
+        for a in (640, 256):
+            place(nc.scalar, 3, a, closing[:, 1, a : a + 384])
         store(3)
+        place(nc.vector, 2, 0, closing[:, 0, : 3 * CHUNK])
+        store(2)

@@ -30,8 +30,7 @@ GPSIMD_SIDE = 8
 PAIRED = 3 * CHUNK
 WD_VECTOR = 84
 KIB = 1024
-AT_WD, AT_G, AT_R, AT_S = 0, 8 * KIB, 20 * KIB, 22 * KIB
-AT_Y3 = AT_G + 13 * KIB // 2
+AT_WD, AT_G = 0, 10 * KIB
 
 
 def tile_attend_gml_lch_kernel(tc, xT, wd, wv, y, cw, rw, offs, out):
@@ -59,7 +58,7 @@ def tile_attend_gml_lch_kernel(tc, xT, wd, wv, y, cw, rw, offs, out):
         offsets = held([P, N // 16], U16, name="offsets")
         cw_sb = held([P, PACK], F32, name="cw_sb")
         rw_col = held([P, RUN], F32, name="rw_col")
-        y_sb = [held([P, PACK, CHUNK], F32, name="y%d" % c) if c != 3 else over(AT_Y3, [P, PACK, CHUNK], F32, "y3") for c in range(N // CHUNK)]
+        y_sb = [held([P, PACK, CHUNK], F32, name="y%d" % c) for c in range(N // CHUNK)]
         wd_raw = over(AT_WD, [P, PACK, V], F32, "wd_raw")
         wv_raw = held([P, PACK, D], F32, name="wv_raw")
         planes = [held([P, T], F32, name="plane%d" % t) for t in range(PACK)]
@@ -74,7 +73,7 @@ def tile_attend_gml_lch_kernel(tc, xT, wd, wv, y, cw, rw, offs, out):
         nc.sync.dma_start(wd_raw[:], wd.rearrange("(p j) v -> p j v", j=PACK))
         for c in range(N // CHUNK):
             nc.sync.dma_start(y_sb[c][:], y_rows[:, :, c * CHUNK : (c + 1) * CHUNK])
-            if c == 1:
+            if c == 0:
                 nc.sync.dma_start(wv_raw[:], wv.rearrange("(p t) d -> p t d", t=PACK))
 
         def listed(c0, n):
@@ -102,13 +101,13 @@ def tile_attend_gml_lch_kernel(tc, xT, wd, wv, y, cw, rw, offs, out):
             nc.scalar.activation(out=rw_runs[:, :, e0 : e0 + PACK], in_=spread[:].rearrange("p e n -> p n e"), func=COPY)
         weight = held([P, PACK, N], F32, name="weight")
         for t in range(PACK):
-            nc.scalar.activation(out=weight[:, t, :CHUNK], in_=rw_all[:, :CHUNK], func=COPY, scale=cw_sb[:, t : t + 1])
+            nc.scalar.activation(out=weight[:, t, : 2 * CHUNK], in_=rw_all[:, : 2 * CHUNK], func=COPY, scale=cw_sb[:, t : t + 1])
         for j in range(2):
             nc.vector.memset(placed[j][:].bitcast(U32), 0)
         nc.gpsimd.memset(placed[2][:].bitcast(U32), 0)
         for t in range(PACK):
             nc.gpsimd.tensor_scalar(
-                out=weight[:, t, CHUNK:], in0=rw_all[:, CHUNK:], scalar1=cw_sb[:, t : t + 1], scalar2=0.0, op0=MULT, op1=ADD
+                out=weight[:, t, 2 * CHUNK :], in0=rw_all[:, 2 * CHUNK :], scalar1=cw_sb[:, t : t + 1], scalar2=0.0, op0=MULT, op1=ADD
             )
 
         picked = held([P, PACK * PAIRED], BF16, name="picked")
@@ -131,22 +130,17 @@ def tile_attend_gml_lch_kernel(tc, xT, wd, wv, y, cw, rw, offs, out):
 
         x_codes = {}
         x_scales = held([P, N], U8, name="x_scales")
-        x_packed = {}
 
-        def pack_x(c, tile):
-            x_packed[c] = tile
-            if c * CHUNK < PAIRED:
-                weave(tile[:], c * CHUNK)
-            else:
-                nc.scalar.activation(out=runs_packed(tile[:].rearrange("p (n t) -> p n t", t=PACK)), in_=runs(rest[:]), func=COPY)
+        def quantize_x(c0, packed, codes):
+            n = codes.shape[1]
+            for a in range(0, n, CHUNK):
+                x_codes[(c0 + a) // CHUNK] = codes[:, a : a + CHUNK]
+            quantize(codes[:], x_scales[:, c0 : c0 + n], packed[:], E4M3)
 
-        def quantize_x(c, tile):
-            x_codes[c] = tile
-            quantize(tile[:], x_scales[:, c * CHUNK : (c + 1) * CHUNK], x_packed[c][:], E4M3)
-
+        x_packed = [held([P, CHUNK * PACK], BF16, name="x_packed%d" % c) for c in range(2)]
         for c in range(2):
-            pack_x(c, held([P, CHUNK * PACK], BF16, name="x_packed%d" % c))
-        quantize_x(0, held([P, CHUNK], U32, name="x_codes0"))
+            weave(x_packed[c][:], c * CHUNK)
+        quantize_x(0, x_packed[0], held([P, CHUNK], U32, name="x_codes0"))
 
         wd_packed = held([P, PACK, P, PACK], BF16, name="wd_packed")
         wd_codes = held([P, V], U32, name="wd_codes")
@@ -168,22 +162,10 @@ def tile_attend_gml_lch_kernel(tc, xT, wd, wv, y, cw, rw, offs, out):
             nc.vector.tensor_copy(out=wd_dealt[:, cut:, :, t0 : t0 + 2], in_=wd_columns[:, cut:, :, t0 : t0 + 2])
         quantize_wd(0)
         quantize_wd(2)
-        quantize_x(1, over(AT_WD, [P, CHUNK], U32, "x_codes1"))
-        for c in (2, 3):
-            pack_x(c, over(AT_WD + c * 2 * KIB, [P, CHUNK * PACK], BF16, "x_packed%d" % c))
-        quantize_x(2, held([P, CHUNK], U32, name="x_codes2"))
-
-        wv_packed = {}
-        wv_mx = {}
-
-        def cast_wv(j, tile):
-            wv_packed[j] = tile[:, (j % 2) * P : (j % 2 + 1) * P, :]
-            nc.scalar.activation(out=runs_packed(wv_packed[j]), in_=runs(wv_raw[:, :, j * P : (j + 1) * P]), func=COPY)
-
-        def quantize_wv(j, packed, codes, scales):
-            quantize(codes, scales, packed.rearrange("p d t -> p (d t)"), E4M3)
-            for k in range(packed.shape[1] // P):
-                wv_mx[j + k] = (codes[:, k * P : (k + 1) * P], scales[:, k * P : (k + 1) * P])
+        quantize_x(CHUNK, x_packed[1], over(AT_WD, [P, CHUNK], U32, "x_codes1"))
+        x_high = over(AT_WD + 4 * KIB, [P, 2 * CHUNK * PACK], BF16, "x_high")
+        weave(x_high[:, : CHUNK * PACK], 2 * CHUNK)
+        nc.scalar.activation(out=runs_packed(x_high[:, CHUNK * PACK :].rearrange("p (n t) -> p n t", t=PACK)), in_=runs(rest[:]), func=COPY)
 
         def scores(gi, b, t0=0, count=PACK):
             c0 = gi * GROUP
@@ -208,7 +190,6 @@ def tile_attend_gml_lch_kernel(tc, xT, wd, wv, y, cw, rw, offs, out):
         slope = {}
         g_packed = {}
         g_mx = {}
-        dx = {}
 
         def group(name, tag=None):
             return held([P, PACK, GROUP], F32, name=name, tag=tag)
@@ -217,41 +198,21 @@ def tile_attend_gml_lch_kernel(tc, xT, wd, wv, y, cw, rw, offs, out):
             diff[gi] = tile
             nc.vector.tensor_tensor(out=tile[:], in0=scores(gi, b)[:], in1=targets(gi), op=SUB)
 
-        def bend(gi, tile):
-            slope[gi] = tile
-            nc.scalar.activation(out=tile[:], in_=diff[gi][:], func=TANH)
+        def bend(gi, target):
+            slope[gi] = target
+            nc.scalar.activation(out=target, in_=diff[gi][:], func=TANH)
 
-        def weigh(engine, c, tile, side):
-            g_packed[c] = tile
-            for k in range(2):
-                gi = 2 * c + k
-                engine.tensor_tensor(
-                    out=runs_packed(tile[:, k * GROUP : (k + 1) * GROUP, :], side),
-                    in0=runs(slope[gi][:], side),
-                    in1=runs(weight[:, :, gi * GROUP : (gi + 1) * GROUP], side),
-                    op=MULT,
-                )
-
-        def weigh_late(c):
-            weigh(nc.gpsimd, c, over(AT_G + (5 if c == 1 else 3) * KIB // 2, [P, CHUNK, PACK], BF16, "g_packed%d" % c), GPSIMD_SIDE)
-
-        def quantize_g(c, codes, scales):
-            g_mx[c] = (codes, scales)
-            quantize(codes[:], scales[:], g_packed[c][:].rearrange("p n t -> p (n t)"), E5M2)
-
-        def second(target, c, j):
-            nc.tensor.matmul_mx(
-                out=target,
-                lhsT=wv_mx[j][0].bitcast(E4M3),
-                lhsT_scale=wv_mx[j][1],
-                rhs=g_mx[c][0][:].bitcast(E5M2),
-                rhs_scale=g_mx[c][1][:],
-                start=True,
-                stop=True,
+        def weigh(engine, c0, source, target, side):
+            engine.tensor_tensor(
+                out=runs_packed(target, side),
+                in0=runs(source, side),
+                in1=runs(weight[:, :, c0 : c0 + source.shape[2]], side),
+                op=MULT,
             )
 
-        def results(b, name):
-            return bank(b, [P, 2, CHUNK], name)
+        def quantize_g(c0, codes, scales):
+            g_mx[c0] = (codes, scales)
+            quantize(codes[:], scales[:], g_packed[c0][:].rearrange("p n t -> p (n t)"), E5M2)
 
         def copy_out(engine, target, source):
             if engine is nc.vector:
@@ -259,22 +220,12 @@ def tile_attend_gml_lch_kernel(tc, xT, wd, wv, y, cw, rw, offs, out):
             else:
                 nc.scalar.activation(out=target, in_=source, func=COPY)
 
-        def evacuate(engine, c, j, source, tile):
-            dx[c, j] = tile
-            copy_out(engine, tile[:], source)
-
-        def piece(name, tag=None):
-            return held([P, CHUNK], F32, name=name, tag=tag)
-
         def place(engine, j, c0, source):
             window = placed[j][:].indirect(listed(c0, source.shape[1]))
             if engine is nc.vector:
                 nc.vector.tensor_copy(out=window, in_=source)
             else:
                 nc.scalar.activation(out=window, in_=source, func=COPY)
-
-        def place_chunk(engine, c, j):
-            place(engine, j, c * CHUNK, dx[c, j][:])
 
         def store(j):
             nc.sync.dma_start(out[j * P : (j + 1) * P, :], placed[j][:])
@@ -286,77 +237,78 @@ def tile_attend_gml_lch_kernel(tc, xT, wd, wv, y, cw, rw, offs, out):
                 part = held([P, 2, GROUP], F32, name="part%d_%d" % (gi, t0))
                 nc.vector.tensor_tensor(out=part[:], in0=scores(gi, t0 + gi, t0, 2)[:], in1=targets(gi)[:, t0 : t0 + 2, :], op=SUB)
                 nc.scalar.activation(out=slope[gi][:, t0 : t0 + 2, :], in_=part[:], func=TANH)
-        quantize_x(3, held([P, CHUNK], U32, name="x_codes3", tag="part0_0"))
-        subtract(2, 6, group("diff2", "part1_0"))
-        bend(2, group("slope2"))
-        weigh(nc.vector, 0, held([P, CHUNK, PACK], BF16, name="g_packed0"), SIDE)
-        subtract(3, 7, group("diff3", "slope0"))
+        quantize_x(2 * CHUNK, x_high, held([P, 2 * CHUNK], U32, name="x_codes_high", tag="part0_0"))
+        g_packed[0] = held([P, CHUNK, PACK], BF16, name="g_packed0")
+        for gi in range(2):
+            weigh(nc.vector, gi * GROUP, slope[gi][:], g_packed[0][:, gi * GROUP : (gi + 1) * GROUP, :], SIDE)
+        subtract(2, 6, group("diff2", "slope0"))
         quantize_g(0, held([P, CHUNK], U32, name="g_codes0"), held([P, CHUNK], U8, name="g_scales0"))
-        wv_low = over(AT_G + 7 * KIB // 2, [P, 2 * P, PACK], BF16, "wv_low")
-        wv_high = over(AT_G, [P, 2 * P, PACK], BF16, "wv_high")
+        wv_packed = held([P, D, PACK], BF16, name="wv_packed", tag="g_late")
         for j in range(PACK):
-            cast_wv(j, wv_low if j < 2 else wv_high)
-        quantize_wv(0, wv_low[:], held([P, 2 * P], U32, name="wv_codes")[:], held([P, 2 * P], U8, name="wv_scales")[:])
-        bend(3, over(AT_G + 9 * KIB // 2, [P, PACK, GROUP], F32, "slope3"))
-        weigh_late(1)
-        first = [bank(4 + j, [P, CHUNK], "first%d" % j) for j in range(2)]
-        for j in range(2):
-            second(first[j][:], 0, j)
-        for gi in (4, 5):
-            subtract(gi, gi - 4, group("diff%d" % gi))
-            bend(gi, over(AT_R, [P, PACK, GROUP], F32, "slope4") if gi == 4 else group("slope5"))
-        subtract(6, 2, group("diff6", "part1_0"))
-        subtract(7, 3, group("diff7", "slope0"))
-        bend(6, over(AT_S, [P, PACK, GROUP], F32, "slope6"))
-        evacuate(nc.scalar, 0, 1, first[1][:], over(AT_Y3 + 3 * KIB, [P, CHUNK], F32, "dx0_1"))
-        bend(7, group("slope7"))
-        evacuate(nc.vector, 0, 0, first[0][:], over(AT_Y3, [P, CHUNK], F32, "dx0_0"))
-        quantize_g(1, over(AT_Y3 + KIB, [P, CHUNK], U32, "g_codes1"), held([P, CHUNK], U8, name="g_scales1"))
-        quantize_wv(2, wv_high[:], over(AT_Y3 + 2 * KIB, [P, 2 * P], U32, "wv_codes_high")[:], over(AT_Y3 - KIB, [P, 2 * P], U8, "wv_scales_high")[:])
-        weigh_late(2)
-        place_chunk(nc.vector, 0, 0)
-        place_chunk(nc.scalar, 0, 1)
-        closing = held([P, 2, 5 * CHUNK], F32, name="closing")
-
-        def products(b, c, js):
-            tile = results(b, "dx%d_%d" % (c, js[0]))
+            nc.scalar.activation(out=runs_packed(wv_packed[:, j * P : (j + 1) * P, :]), in_=runs(wv_raw[:, :, j * P : (j + 1) * P]), func=COPY)
+        subtract(3, 7, group("diff3", "slope1"))
+        wv_codes = held([P, D], U32, name="wv_codes")
+        wv_scales = held([P, D], U8, name="wv_scales")
+        quantize(wv_codes[:], wv_scales[:], wv_packed[:].rearrange("p d t -> p (d t)"), E4M3)
+        for gi in (2, 3):
+            bend(gi, group("slope%d" % gi)[:])
+        def products(b, c0, js):
+            codes, scales = g_mx[c0]
+            tile = bank(b, [P, len(js), codes.shape[1]], "dx%d_%d" % (c0, js[0]))
             for k, j in enumerate(js):
-                second(tile[:, k, :], c, j)
+                nc.tensor.matmul_mx(
+                    out=tile[:, k, :],
+                    lhsT=wv_codes[:, j * P : (j + 1) * P].bitcast(E4M3),
+                    lhsT_scale=wv_scales[:, j * P : (j + 1) * P],
+                    rhs=codes[:].bitcast(E5M2),
+                    rhs_scale=scales[:],
+                    start=True,
+                    stop=True,
+                )
             return tile
 
-        def close(engine, c, source):
-            copy_out(engine, closing[:, :, c * CHUNK : (c + 1) * CHUNK], source[:])
-
-        early1 = products(6, 1, (0, 1))
-        late0 = products(7, 0, (2, 3))
-        late1 = products(0, 1, (2, 3))
-        both = over(AT_R, [P, 2, CHUNK], F32, "dx1")
-        copy_out(nc.vector, both[:], early1[:])
-        close(nc.scalar, 0, late0)
-        close(nc.vector, 1, late1)
-        quantize_g(2, held([P, CHUNK], U32, name="g_codes2"), over(AT_Y3, [P, CHUNK], U8, "g_scales2"))
-        weigh_late(3)
-        place(nc.vector, 0, CHUNK, both[:, 0, :])
-        place(nc.scalar, 1, CHUNK, both[:, 1, :])
-        place(nc.scalar, 3, 0, closing[:, 1, :CHUNK])
-        early2 = products(1, 2, (0, 1))
-        late2 = products(2, 2, (2, 3))
-        both = over(AT_S, [P, 2, CHUNK], F32, "dx2")
-        copy_out(nc.vector, both[:], early2[:])
-        close(nc.vector, 2, late2)
-        quantize_g(3, held([P, CHUNK], U32, name="g_codes3"), over(AT_R, [P, CHUNK], U8, "g_scales3"))
-        place(nc.scalar, 0, 2 * CHUNK, both[:, 0, :])
-        place(nc.vector, 1, 2 * CHUNK, both[:, 1, :])
-        for k, js in ((1, (3, 0)), (0, (2, 1))):
-            last = products(3 + k, 3, js)
-            copy_out(nc.scalar if k == 1 else nc.vector, closing[:, k, 3 * CHUNK :], last[:].rearrange("p c n -> p (c n)"))
-        place(nc.scalar, 0, 3 * CHUNK, closing[:, 1, 4 * CHUNK :])
+        first = [products(4 + e, 0, (e, 2 + e)) for e in range(2)]
+        opening0 = over(AT_G + 2 * KIB, [P, CHUNK], F32, "opening0")
+        opening2 = held([P, CHUNK], F32, name="opening2")
+        opening_odd = held([P, 2, CHUNK], F32, name="opening_odd")
+        opening = [opening0[:], opening_odd[:, 0, :], opening2[:], opening_odd[:, 1, :]]
+        slope_pair = over(AT_G - 2 * KIB, [P, PACK, CHUNK], F32, "slope_pair")
+        for gi in range(4, 8):
+            subtract(gi, gi - 4, group("diff%d" % gi))
+            bend(gi, slope_pair[:, :, (gi - 4) * GROUP : (gi - 3) * GROUP] if gi < 6 else group("slope%d" % gi)[:])
+            if gi == 4:
+                copy_out(nc.scalar, opening0[:], first[0][:, 0, :])
+                copy_out(nc.scalar, opening2[:], first[0][:, 1, :])
+            if gi == 6:
+                copy_out(nc.scalar, opening_odd[:], first[1][:])
+        g_packed[CHUNK] = held([P, 2 * CHUNK, PACK], BF16, name="g_packed1", tag="g_late")
+        for gi in (2, 3):
+            weigh(nc.gpsimd, gi * GROUP, slope[gi], g_packed[CHUNK][:, (gi - 2) * GROUP : (gi - 1) * GROUP, :], GPSIMD_SIDE)
+        weigh(nc.gpsimd, 2 * CHUNK, slope_pair[:], g_packed[CHUNK][:, CHUNK:, :], GPSIMD_SIDE)
+        for j in range(PACK):
+            place(nc.vector if j % 2 == 0 else nc.scalar, j, 0, opening[j])
+        quantize_g(CHUNK, held([P, 2 * CHUNK], U32, name="g_codes1"), over(AT_G + 5 * KIB // 2, [P, 2 * CHUNK], U8, "g_scales1"))
+        g_packed[3 * CHUNK] = over(AT_G + KIB // 2, [P, CHUNK, PACK], BF16, "g_packed3")
+        for gi in (6, 7):
+            weigh(nc.vector, gi * GROUP, slope[gi], g_packed[3 * CHUNK][:, (gi - 6) * GROUP : (gi - 5) * GROUP, :], SIDE)
+        closing = [held([P, 2, 3 * CHUNK], F32, name="closing%d" % e) for e in range(2)]
+        middle = {j: products(b, CHUNK, (j,)) for j, b in ((0, 6), (1, 7), (3, 0), (2, 1))}
+        copy_out(nc.vector, closing[0][:, 0, : 2 * CHUNK], middle[0][:, 0, :])
+        quantize_g(3 * CHUNK, held([P, CHUNK], U32, name="g_codes3"), held([P, CHUNK], U8, name="g_scales3"))
+        for j in (1, 3):
+            copy_out(nc.scalar, closing[1][:, j // 2, : 2 * CHUNK], middle[j][:, 0, :])
+        last = [products(2 + e, 3 * CHUNK, (e, 2 + e)) for e in range(2)]
+        place(nc.vector, 0, CHUNK, closing[0][:, 0, : 2 * CHUNK])
+        copy_out(nc.vector, closing[0][:, :, 2 * CHUNK :], last[0][:])
+        place(nc.vector, 0, 3 * CHUNK, closing[0][:, 0, 2 * CHUNK :])
         store(0)
-        place(nc.vector, 2, 3 * CHUNK, closing[:, 0, 3 * CHUNK : 4 * CHUNK])
-        place(nc.vector, 1, 3 * CHUNK, closing[:, 0, 4 * CHUNK :])
+        place(nc.scalar, 1, CHUNK, closing[1][:, 0, :384])
+        copy_out(nc.scalar, closing[1][:, :, 2 * CHUNK :], last[1][:])
+        copy_out(nc.scalar, closing[0][:, 1, : 2 * CHUNK], middle[2][:, 0, :])
+        place(nc.scalar, 1, CHUNK + 384, closing[1][:, 0, 384:])
         store(1)
-        for a in (640, 256):
-            place(nc.scalar, 3, a, closing[:, 1, a : a + 384])
-        store(3)
-        place(nc.vector, 2, 0, closing[:, 0, : 3 * CHUNK])
+        place(nc.vector, 2, CHUNK, closing[0][:, 1, :])
         store(2)
+        for a in (384, 0):
+            place(nc.scalar, 3, CHUNK + a, closing[1][:, 1, a : a + 384])
+        store(3)

@@ -8,6 +8,7 @@ FLOPS = 2 * 2 * D * V * N
 F32 = mybir.dt.float32
 BF16 = mybir.dt.bfloat16
 U32 = mybir.dt.uint32
+I32 = mybir.dt.int32
 U16 = mybir.dt.uint16
 U8 = mybir.dt.uint8
 E4M3 = mybir.dt.float8_e4m3fn_x4
@@ -28,7 +29,7 @@ QUAD = 32
 SIDE = 4
 GPSIMD_SIDE = 8
 PAIRED = 3 * CHUNK
-WD_VECTOR = 84
+WD_VECTOR = (76, 64)
 KIB = 1024
 AT_WD, AT_G = 0, 10 * KIB
 
@@ -114,16 +115,24 @@ def tile_attend_gml_lch_kernel(tc, xT, wd, wv, y, cw, rw, offs, out):
         picked_halves = picked[:].rearrange("p (u n e) -> p u n e", u=2, e=2)
         picked_words = picked[:].bitcast(U32).rearrange("p (u n) -> p n u", u=2)
         rest = held([P, PACK, CHUNK], BF16, name="rest")
+        x_packed = {c: held([P, CHUNK * PACK], BF16, name="x_packed%d" % c) for c in (0, 3)}
         for t in range(PACK):
             n = CHUNK if t == PACK - 1 else PAIRED
             for c0 in range(0, PAIRED, n):
                 nc.vector.tensor_copy(out=picked_halves[:, t // 2, c0 : c0 + n, t % 2], in_=planes[t][:].indirect(listed(c0, n)))
+                if t == PACK - 1 and c0 == CHUNK:
+                    nc.vector.tensor_copy(
+                        out=x_packed[0][:].bitcast(I32).rearrange("p (n u) -> p n u", u=2),
+                        in_=picked[:].bitcast(I32).rearrange("p (u n) -> p n u", u=2)[:, :CHUNK, :],
+                    )
             nc.scalar.activation(out=rest[:, t, :], in_=planes[t][:].indirect(listed(PAIRED, CHUNK)), func=COPY)
             if t == 0:
                 nc.gpsimd.memset(placed[3][:].bitcast(U32), 0)
 
         def weave(target, c0):
             nc.scalar.copy(out=target.bitcast(U32).rearrange("p (n u) -> p n u", u=2), in_=picked_words[:, c0 : c0 + CHUNK, :])
+
+        nc.scalar.activation(out=runs_packed(x_packed[3][:].rearrange("p (n t) -> p n t", t=PACK)), in_=runs(rest[:]), func=COPY)
 
         def quantize(codes, scales, packed, fmt):
             nc.vector.quantize_mx(out=codes.bitcast(fmt), scales=scales, in_=packed)
@@ -137,15 +146,11 @@ def tile_attend_gml_lch_kernel(tc, xT, wd, wv, y, cw, rw, offs, out):
                 x_codes[(c0 + a) // CHUNK] = codes[:, a : a + CHUNK]
             quantize(codes[:], x_scales[:, c0 : c0 + n], packed[:], E4M3)
 
-        x_packed = [held([P, CHUNK * PACK], BF16, name="x_packed%d" % c) for c in range(2)]
-        for c in range(2):
-            weave(x_packed[c][:], c * CHUNK)
         quantize_x(0, x_packed[0], held([P, CHUNK], U32, name="x_codes0"))
 
         wd_packed = held([P, PACK, P, PACK], BF16, name="wd_packed")
         wd_codes = held([P, V], U32, name="wd_codes")
         wd_scales = held([P, V], U8, name="wd_scales")
-        cut = P - WD_VECTOR
         wd_columns = wd_raw[:].rearrange("p j (m t) -> p m j t", t=PACK)
         wd_dealt = wd_packed[:].rearrange("p t m j -> p m j t")
 
@@ -158,14 +163,15 @@ def tile_attend_gml_lch_kernel(tc, xT, wd, wv, y, cw, rw, offs, out):
             )
 
         for t0 in (0, 2):
+            cut = P - WD_VECTOR[t0 // 2]
             nc.scalar.activation(out=wd_dealt[:, :cut, :, t0 : t0 + 2], in_=wd_columns[:, :cut, :, t0 : t0 + 2], func=COPY)
             nc.vector.tensor_copy(out=wd_dealt[:, cut:, :, t0 : t0 + 2], in_=wd_columns[:, cut:, :, t0 : t0 + 2])
         quantize_wd(0)
         quantize_wd(2)
-        quantize_x(CHUNK, x_packed[1], over(AT_WD, [P, CHUNK], U32, "x_codes1"))
-        x_high = over(AT_WD + 4 * KIB, [P, 2 * CHUNK * PACK], BF16, "x_high")
-        weave(x_high[:, : CHUNK * PACK], 2 * CHUNK)
-        nc.scalar.activation(out=runs_packed(x_high[:, CHUNK * PACK :].rearrange("p (n t) -> p n t", t=PACK)), in_=runs(rest[:]), func=COPY)
+        quantize_x(3 * CHUNK, x_packed[3], over(AT_WD, [P, CHUNK], U32, "x_codes3"))
+        x_middle = over(AT_WD + 4 * KIB, [P, 2 * CHUNK * PACK], BF16, "x_middle")
+        for c in range(2):
+            weave(x_middle[:, c * CHUNK * PACK : (c + 1) * CHUNK * PACK], (c + 1) * CHUNK)
 
         def scores(gi, b, t0=0, count=PACK):
             c0 = gi * GROUP
@@ -237,12 +243,14 @@ def tile_attend_gml_lch_kernel(tc, xT, wd, wv, y, cw, rw, offs, out):
                 part = held([P, 2, GROUP], F32, name="part%d_%d" % (gi, t0))
                 nc.vector.tensor_tensor(out=part[:], in0=scores(gi, t0 + gi, t0, 2)[:], in1=targets(gi)[:, t0 : t0 + 2, :], op=SUB)
                 nc.scalar.activation(out=slope[gi][:, t0 : t0 + 2, :], in_=part[:], func=TANH)
-        quantize_x(2 * CHUNK, x_high, held([P, 2 * CHUNK], U32, name="x_codes_high", tag="part0_0"))
+        quantize_x(CHUNK, x_middle, held([P, 2 * CHUNK], U32, name="x_codes_middle", tag="part0_0"))
         g_packed[0] = held([P, CHUNK, PACK], BF16, name="g_packed0")
         for gi in range(2):
             weigh(nc.vector, gi * GROUP, slope[gi][:], g_packed[0][:, gi * GROUP : (gi + 1) * GROUP, :], SIDE)
         subtract(2, 6, group("diff2", "slope0"))
-        quantize_g(0, held([P, CHUNK], U32, name="g_codes0"), held([P, CHUNK], U8, name="g_scales0"))
+        g_mx[0] = (held([P, CHUNK], U32, name="g_codes0"), held([P, CHUNK], U8, name="g_scales0"))
+        for a in (0, GROUP):
+            quantize(g_mx[0][0][:, a : a + GROUP], g_mx[0][1][:, a : a + GROUP], g_packed[0][:, a : a + GROUP, :].rearrange("p n t -> p (n t)"), E5M2)
         wv_packed = held([P, D, PACK], BF16, name="wv_packed", tag="g_late")
         for j in range(PACK):
             nc.scalar.activation(out=runs_packed(wv_packed[:, j * P : (j + 1) * P, :]), in_=runs(wv_raw[:, :, j * P : (j + 1) * P]), func=COPY)
@@ -291,24 +299,27 @@ def tile_attend_gml_lch_kernel(tc, xT, wd, wv, y, cw, rw, offs, out):
         g_packed[3 * CHUNK] = over(AT_G + KIB // 2, [P, CHUNK, PACK], BF16, "g_packed3")
         for gi in (6, 7):
             weigh(nc.vector, gi * GROUP, slope[gi], g_packed[3 * CHUNK][:, (gi - 6) * GROUP : (gi - 5) * GROUP, :], SIDE)
-        closing = [held([P, 2, 3 * CHUNK], F32, name="closing%d" % e) for e in range(2)]
+        closing0 = held([P, 3 * CHUNK], F32, name="closing0")
+        closing_odd = held([P, 2, 3 * CHUNK], F32, name="closing_odd")
         middle = {j: products(b, CHUNK, (j,)) for j, b in ((0, 6), (1, 7), (3, 0), (2, 1))}
-        copy_out(nc.vector, closing[0][:, 0, : 2 * CHUNK], middle[0][:, 0, :])
+        copy_out(nc.vector, closing0[:, : 2 * CHUNK], middle[0][:, 0, :])
         quantize_g(3 * CHUNK, held([P, CHUNK], U32, name="g_codes3"), held([P, CHUNK], U8, name="g_scales3"))
         for j in (1, 3):
-            copy_out(nc.scalar, closing[1][:, j // 2, : 2 * CHUNK], middle[j][:, 0, :])
+            copy_out(nc.scalar, closing_odd[:, j // 2, : 2 * CHUNK], middle[j][:, 0, :])
         last = [products(2 + e, 3 * CHUNK, (e, 2 + e)) for e in range(2)]
-        place(nc.vector, 0, CHUNK, closing[0][:, 0, : 2 * CHUNK])
-        copy_out(nc.vector, closing[0][:, :, 2 * CHUNK :], last[0][:])
-        place(nc.vector, 0, 3 * CHUNK, closing[0][:, 0, 2 * CHUNK :])
+        closing2 = held([P, 3 * CHUNK], F32, name="closing2", tag="g_codes3")
+        place(nc.vector, 0, CHUNK, closing0[:, : 2 * CHUNK])
+        copy_out(nc.vector, closing0[:, 2 * CHUNK :], last[0][:, 0, :])
+        copy_out(nc.vector, closing2[:, 2 * CHUNK :], last[0][:, 1, :])
+        place(nc.vector, 0, 3 * CHUNK, closing0[:, 2 * CHUNK :])
         store(0)
-        place(nc.scalar, 1, CHUNK, closing[1][:, 0, :384])
-        copy_out(nc.scalar, closing[1][:, :, 2 * CHUNK :], last[1][:])
-        copy_out(nc.scalar, closing[0][:, 1, : 2 * CHUNK], middle[2][:, 0, :])
-        place(nc.scalar, 1, CHUNK + 384, closing[1][:, 0, 384:])
+        place(nc.scalar, 1, CHUNK, closing_odd[:, 0, :384])
+        copy_out(nc.scalar, closing_odd[:, :, 2 * CHUNK :], last[1][:])
+        copy_out(nc.scalar, closing2[:, : 2 * CHUNK], middle[2][:, 0, :])
+        place(nc.scalar, 1, CHUNK + 384, closing_odd[:, 0, 384:])
         store(1)
-        place(nc.vector, 2, CHUNK, closing[0][:, 1, :])
+        place(nc.vector, 2, CHUNK, closing2[:])
         store(2)
         for a in (384, 0):
-            place(nc.scalar, 3, CHUNK + a, closing[1][:, 1, a : a + 384])
+            place(nc.scalar, 3, CHUNK + a, closing_odd[:, 1, a : a + 384])
         store(3)

@@ -8,7 +8,6 @@ FLOPS = 2 * 2 * D * V * N
 F32 = mybir.dt.float32
 BF16 = mybir.dt.bfloat16
 U32 = mybir.dt.uint32
-I32 = mybir.dt.int32
 U16 = mybir.dt.uint16
 U8 = mybir.dt.uint8
 E4M3 = mybir.dt.float8_e4m3fn_x4
@@ -29,7 +28,7 @@ QUAD = 32
 SIDE = 4
 GPSIMD_SIDE = 8
 PAIRED = 3 * CHUNK
-WD_VECTOR = (76, 64)
+WD_VECTOR = 84
 KIB = 1024
 AT_WD, AT_G = 0, 10 * KIB
 
@@ -115,24 +114,16 @@ def tile_attend_gml_lch_kernel(tc, xT, wd, wv, y, cw, rw, offs, out):
         picked_halves = picked[:].rearrange("p (u n e) -> p u n e", u=2, e=2)
         picked_words = picked[:].bitcast(U32).rearrange("p (u n) -> p n u", u=2)
         rest = held([P, PACK, CHUNK], BF16, name="rest")
-        x_packed = {c: held([P, CHUNK * PACK], BF16, name="x_packed%d" % c) for c in (0, 3)}
         for t in range(PACK):
             n = CHUNK if t == PACK - 1 else PAIRED
             for c0 in range(0, PAIRED, n):
                 nc.vector.tensor_copy(out=picked_halves[:, t // 2, c0 : c0 + n, t % 2], in_=planes[t][:].indirect(listed(c0, n)))
-                if t == PACK - 1 and c0 == CHUNK:
-                    nc.vector.tensor_copy(
-                        out=x_packed[0][:].bitcast(I32).rearrange("p (n u) -> p n u", u=2),
-                        in_=picked[:].bitcast(I32).rearrange("p (u n) -> p n u", u=2)[:, :CHUNK, :],
-                    )
             nc.scalar.activation(out=rest[:, t, :], in_=planes[t][:].indirect(listed(PAIRED, CHUNK)), func=COPY)
             if t == 0:
                 nc.gpsimd.memset(placed[3][:].bitcast(U32), 0)
 
         def weave(target, c0):
             nc.scalar.copy(out=target.bitcast(U32).rearrange("p (n u) -> p n u", u=2), in_=picked_words[:, c0 : c0 + CHUNK, :])
-
-        nc.scalar.activation(out=runs_packed(x_packed[3][:].rearrange("p (n t) -> p n t", t=PACK)), in_=runs(rest[:]), func=COPY)
 
         def quantize(codes, scales, packed, fmt):
             nc.vector.quantize_mx(out=codes.bitcast(fmt), scales=scales, in_=packed)
@@ -146,11 +137,15 @@ def tile_attend_gml_lch_kernel(tc, xT, wd, wv, y, cw, rw, offs, out):
                 x_codes[(c0 + a) // CHUNK] = codes[:, a : a + CHUNK]
             quantize(codes[:], x_scales[:, c0 : c0 + n], packed[:], E4M3)
 
+        x_packed = [held([P, CHUNK * PACK], BF16, name="x_packed%d" % c) for c in range(2)]
+        for c in range(2):
+            weave(x_packed[c][:], c * CHUNK)
         quantize_x(0, x_packed[0], held([P, CHUNK], U32, name="x_codes0"))
 
         wd_packed = held([P, PACK, P, PACK], BF16, name="wd_packed")
         wd_codes = held([P, V], U32, name="wd_codes")
         wd_scales = held([P, V], U8, name="wd_scales")
+        cut = P - WD_VECTOR
         wd_columns = wd_raw[:].rearrange("p j (m t) -> p m j t", t=PACK)
         wd_dealt = wd_packed[:].rearrange("p t m j -> p m j t")
 
@@ -163,15 +158,14 @@ def tile_attend_gml_lch_kernel(tc, xT, wd, wv, y, cw, rw, offs, out):
             )
 
         for t0 in (0, 2):
-            cut = P - WD_VECTOR[t0 // 2]
             nc.scalar.activation(out=wd_dealt[:, :cut, :, t0 : t0 + 2], in_=wd_columns[:, :cut, :, t0 : t0 + 2], func=COPY)
             nc.vector.tensor_copy(out=wd_dealt[:, cut:, :, t0 : t0 + 2], in_=wd_columns[:, cut:, :, t0 : t0 + 2])
         quantize_wd(0)
         quantize_wd(2)
-        quantize_x(3 * CHUNK, x_packed[3], over(AT_WD, [P, CHUNK], U32, "x_codes3"))
-        x_middle = over(AT_WD + 4 * KIB, [P, 2 * CHUNK * PACK], BF16, "x_middle")
-        for c in range(2):
-            weave(x_middle[:, c * CHUNK * PACK : (c + 1) * CHUNK * PACK], (c + 1) * CHUNK)
+        quantize_x(CHUNK, x_packed[1], over(AT_WD, [P, CHUNK], U32, "x_codes1"))
+        x_high = over(AT_WD + 4 * KIB, [P, 2 * CHUNK * PACK], BF16, "x_high")
+        weave(x_high[:, : CHUNK * PACK], 2 * CHUNK)
+        nc.scalar.activation(out=runs_packed(x_high[:, CHUNK * PACK :].rearrange("p (n t) -> p n t", t=PACK)), in_=runs(rest[:]), func=COPY)
 
         def scores(gi, b, t0=0, count=PACK):
             c0 = gi * GROUP
@@ -243,7 +237,7 @@ def tile_attend_gml_lch_kernel(tc, xT, wd, wv, y, cw, rw, offs, out):
                 part = held([P, 2, GROUP], F32, name="part%d_%d" % (gi, t0))
                 nc.vector.tensor_tensor(out=part[:], in0=scores(gi, t0 + gi, t0, 2)[:], in1=targets(gi)[:, t0 : t0 + 2, :], op=SUB)
                 nc.scalar.activation(out=slope[gi][:, t0 : t0 + 2, :], in_=part[:], func=TANH)
-        quantize_x(CHUNK, x_middle, held([P, 2 * CHUNK], U32, name="x_codes_middle", tag="part0_0"))
+        quantize_x(2 * CHUNK, x_high, held([P, 2 * CHUNK], U32, name="x_codes_high", tag="part0_0"))
         g_packed[0] = held([P, CHUNK, PACK], BF16, name="g_packed0")
         for gi in range(2):
             weigh(nc.vector, gi * GROUP, slope[gi][:], g_packed[0][:, gi * GROUP : (gi + 1) * GROUP, :], SIDE)

@@ -165,7 +165,9 @@ def tile_attend_gml_lch_kernel(tc, xT, wd, wv, y, cw, rw, offs, out):
         quantize_x(CHUNK, x_packed[1], over(AT_WD, [P, CHUNK], U32, "x_codes1"))
         x_high = over(AT_WD + 4 * KIB, [P, 2 * CHUNK * PACK], BF16, "x_high")
         weave(x_high[:, : CHUNK * PACK], 2 * CHUNK)
-        nc.scalar.activation(out=runs_packed(x_high[:, CHUNK * PACK :].rearrange("p (n t) -> p n t", t=PACK)), in_=runs(rest[:]), func=COPY)
+        rest_packed = x_high[:, CHUNK * PACK :].rearrange("p (n t) -> p n t", t=PACK)
+        nc.vector.tensor_copy(out=runs_packed(rest_packed[:, :GROUP, :]), in_=runs(rest[:, :, :GROUP]))
+        nc.scalar.activation(out=runs_packed(rest_packed[:, GROUP:, :]), in_=runs(rest[:, :, GROUP:]), func=COPY)
 
         def scores(gi, b, t0=0, count=PACK):
             c0 = gi * GROUP

@@ -30,6 +30,7 @@ GPSIMD_SIDE = 8
 PAIRED = 3 * CHUNK
 WD_VECTOR = 84
 KIB = 1024
+Y_LOADS = [(0, 384), (384, 384), (768, 256)]
 AT_WD, AT_G = 0, 10 * KIB
 
 
@@ -58,7 +59,7 @@ def tile_attend_gml_lch_kernel(tc, xT, wd, wv, y, cw, rw, offs, out):
         offsets = held([P, N // 16], U16, name="offsets")
         cw_sb = held([P, PACK], F32, name="cw_sb")
         rw_col = held([P, RUN], F32, name="rw_col")
-        y_sb = [held([P, PACK, CHUNK], F32, name="y%d" % c) for c in range(N // CHUNK)]
+        y_sb = [held([P, PACK, n], F32, name="y%d" % k) for k, (y0, n) in enumerate(Y_LOADS)]
         wd_raw = over(AT_WD, [P, PACK, V], F32, "wd_raw")
         wv_raw = held([P, PACK, D], F32, name="wv_raw")
         planes = [held([P, T], F32, name="plane%d" % t) for t in range(PACK)]
@@ -71,9 +72,9 @@ def tile_attend_gml_lch_kernel(tc, xT, wd, wv, y, cw, rw, offs, out):
             if t == 0:
                 nc.sync.dma_start(offsets[:], offs)
         nc.sync.dma_start(wd_raw[:], wd.rearrange("(p j) v -> p j v", j=PACK))
-        for c in range(N // CHUNK):
-            nc.sync.dma_start(y_sb[c][:], y_rows[:, :, c * CHUNK : (c + 1) * CHUNK])
-            if c == 0:
+        for k, (y0, n) in enumerate(Y_LOADS):
+            nc.sync.dma_start(y_sb[k][:], y_rows[:, :, y0 : y0 + n])
+            if k == 0:
                 nc.sync.dma_start(wv_raw[:], wv.rearrange("(p t) d -> p t d", t=PACK))
 
         def listed(c0, n):
@@ -186,7 +187,9 @@ def tile_attend_gml_lch_kernel(tc, xT, wd, wv, y, cw, rw, offs, out):
             return a
 
         def targets(gi):
-            return y_sb[gi // 2][:, :, (gi % 2) * GROUP : (gi % 2 + 1) * GROUP]
+            k = max(k for k in range(len(Y_LOADS)) if Y_LOADS[k][0] <= gi * GROUP)
+            y0 = gi * GROUP - Y_LOADS[k][0]
+            return y_sb[k][:, :, y0 : y0 + GROUP]
 
         diff = {}
         slope = {}

@@ -294,13 +294,33 @@ def tile_attend_gml_lch_kernel(tc, xT, wd, wv, y, cw, rw, offs, out):
         weigh(nc.gpsimd, 2 * CHUNK, slope_pair[:], g_packed[CHUNK][:, CHUNK:, :], GPSIMD_SIDE)
         for j in range(PACK):
             place(nc.vector if j % 2 == 0 else nc.scalar, j, 0, opening[j])
-        quantize_g(CHUNK, held([P, 2 * CHUNK], U32, name="g_codes1"), over(AT_G + 5 * KIB // 2, [P, 2 * CHUNK], U8, "g_scales1"))
+        g_mx[CHUNK] = (held([P, 2 * CHUNK], U32, name="g_codes1"), over(AT_G + 5 * KIB // 2, [P, 2 * CHUNK], U8, "g_scales1"))
+        for a in (0, CHUNK):
+            quantize(
+                g_mx[CHUNK][0][:, a : a + CHUNK],
+                g_mx[CHUNK][1][:, a : a + CHUNK],
+                g_packed[CHUNK][:, a : a + CHUNK, :].rearrange("p n t -> p (n t)"),
+                E5M2,
+            )
         g_packed[3 * CHUNK] = over(AT_G + KIB // 2, [P, CHUNK, PACK], BF16, "g_packed3")
         for gi in (6, 7):
             weigh(nc.vector, gi * GROUP, slope[gi], g_packed[3 * CHUNK][:, (gi - 6) * GROUP : (gi - 5) * GROUP, :], SIDE)
         closing0 = held([P, 3 * CHUNK], F32, name="closing0")
         closing_odd = held([P, 2, 3 * CHUNK], F32, name="closing_odd")
-        middle = {j: products(b, CHUNK, (j,)) for j, b in ((0, 6), (1, 7), (3, 0), (2, 1))}
+        middle = {j: bank(6 + j, [P, 1, 2 * CHUNK], "middle%d" % j) for j in range(2)}
+        for a in (0, CHUNK):
+            for j in range(2):
+                nc.tensor.matmul_mx(
+                    out=middle[j][:, 0, a : a + CHUNK],
+                    lhsT=wv_codes[:, j * P : (j + 1) * P].bitcast(E4M3),
+                    lhsT_scale=wv_scales[:, j * P : (j + 1) * P],
+                    rhs=g_mx[CHUNK][0][:, a : a + CHUNK].bitcast(E5M2),
+                    rhs_scale=g_mx[CHUNK][1][:, a : a + CHUNK],
+                    start=True,
+                    stop=True,
+                )
+        for j, b in ((3, 0), (2, 1)):
+            middle[j] = products(b, CHUNK, (j,))
         copy_out(nc.vector, closing0[:, : 2 * CHUNK], middle[0][:, 0, :])
         quantize_g(3 * CHUNK, held([P, CHUNK], U32, name="g_codes3"), held([P, CHUNK], U8, name="g_scales3"))
         for j in (1, 3):

@@ -323,19 +323,20 @@ def tile_attend_gml_lch_kernel(tc, xT, wd, wv, y, cw, rw, offs, out):
             middle[j] = products(b, CHUNK, (j,))
         copy_out(nc.vector, closing0[:, : 2 * CHUNK], middle[0][:, 0, :])
         quantize_g(3 * CHUNK, held([P, CHUNK], U32, name="g_codes3"), held([P, CHUNK], U8, name="g_scales3"))
+        closing2 = held([P, 3 * CHUNK], F32, name="closing2")
         for j in (1, 3):
             copy_out(nc.scalar, closing_odd[:, j // 2, : 2 * CHUNK], middle[j][:, 0, :])
-        last = [products(2 + e, 3 * CHUNK, (e, 2 + e)) for e in range(2)]
-        closing2 = held([P, 3 * CHUNK], F32, name="closing2", tag="g_codes3")
+        copy_out(nc.scalar, closing2[:, : 2 * CHUNK], middle[2][:, 0, :])
+        last = [products(2 + h, 3 * CHUNK, js) for h, js in enumerate([(1, 0), (2, 3)])]
+        copy_out(nc.scalar, closing_odd[:, 0, 2 * CHUNK :], last[0][:, 0, :])
+        copy_out(nc.scalar, closing0[:, 2 * CHUNK :], last[0][:, 1, :])
         place(nc.vector, 0, CHUNK, closing0[:, : 2 * CHUNK])
-        copy_out(nc.vector, closing0[:, 2 * CHUNK :], last[0][:, 0, :])
-        copy_out(nc.vector, closing2[:, 2 * CHUNK :], last[0][:, 1, :])
+        copy_out(nc.vector, closing2[:, 2 * CHUNK :], last[1][:, 0, :])
         place(nc.vector, 0, 3 * CHUNK, closing0[:, 2 * CHUNK :])
         store(0)
-        place(nc.scalar, 1, CHUNK, closing_odd[:, 0, :384])
-        copy_out(nc.scalar, closing_odd[:, :, 2 * CHUNK :], last[1][:])
-        copy_out(nc.scalar, closing2[:, : 2 * CHUNK], middle[2][:, 0, :])
         place(nc.scalar, 1, CHUNK + 384, closing_odd[:, 0, 384:])
+        copy_out(nc.scalar, closing_odd[:, 1, 2 * CHUNK :], last[1][:, 1, :])
+        place(nc.scalar, 1, CHUNK, closing_odd[:, 0, :384])
         store(1)
         place(nc.vector, 2, CHUNK, closing2[:])
         store(2)

from contextlib import ExitStack

import concourse.mybir as mybir

N, T, D, V = 1024, 2048, 512, 512
FLOPS = 2 * 2 * D * V * N

F32 = mybir.dt.float32
BF16 = mybir.dt.bfloat16
U32 = mybir.dt.uint32
U16 = mybir.dt.uint16
U8 = mybir.dt.uint8
E4M3 = mybir.dt.float8_e4m3fn_x4
E5M2 = mybir.dt.float8_e5m2_x4
COPY = mybir.ActivationFunctionType.Copy
TANH = mybir.ActivationFunctionType.Tanh
MULT = mybir.AluOpType.mult
SUB = mybir.AluOpType.subtract
ADD = mybir.AluOpType.add
EQUAL = mybir.AluOpType.is_equal

P = 128
PACK = 4
GROUP = 128
CHUNK = 256
RUN = N // P
QUAD = 32
SIDE = 4
GPSIMD_SIDE = 8
PAIRED = 3 * CHUNK
WD_VECTOR = 84
KIB = 1024
Y_LOADS = [(0, 384), (384, 384), (768, 256)]
AT_WD, AT_G = 0, 10 * KIB


def tile_attend_gml_lch_kernel(tc, xT, wd, wv, y, cw, rw, offs, out):
    nc = tc.nc
    with ExitStack() as ctx:
        keep = ctx.enter_context(tc.tile_pool(name="keep", bufs=1))
        shared = ctx.enter_context(tc.tile_pool(name="shared", bufs=1))
        psum = ctx.enter_context(tc.psum_pool(name="psum", bufs=1))

        def held(shape, dtype, name, tag=None):
            return keep.tile(shape, dtype, name=name, tag=tag or name, align_bytes=64)

        def over(offset, shape, dtype, name):
            return shared.tile(shape, dtype, name=name, align_bytes=64, offset=offset)

        def bank(b, shape, name):
            return psum.tile(shape, F32, name=name, tag="bank%d" % b)

        def runs(ap, side=SIDE):
            return ap.rearrange("p t (c i) -> p c t i", i=side)

        def runs_packed(ap, side=SIDE):
            return ap.rearrange("p (c i) t -> p c t i", i=side)

        offsets = held([P, N // 16], U16, name="offsets")
        cw_sb = held([P, PACK], F32, name="cw_sb")
        rw_col = held([P, RUN], F32, name="rw_col")
        y_sb = [held([P, PACK, n], F32, name="y%d" % k) for k, (y0, n) in enumerate(Y_LOADS)]
        wd_raw = over(AT_WD, [P, PACK, V], F32, "wd_raw")
        wv_raw = held([P, PACK, D], F32, name="wv_raw")
        planes = [held([P, T], F32, name="plane%d" % t) for t in range(PACK)]
        x_rows = xT.rearrange("(p t) n -> p t n", t=PACK)
        y_rows = y.rearrange("(p t) n -> p t n", t=PACK)
        nc.scalar.dma_start(rw_col[:], rw[0:1, :].rearrange("o (p e) -> p (o e)", e=RUN))
        nc.scalar.dma_start(cw_sb[:], cw.rearrange("(p t) o -> p (t o)", t=PACK))
        for t in range(PACK):
            nc.sync.dma_start(planes[t][:], x_rows[:, t, :])
            if t == 0:
                nc.sync.dma_start(offsets[:], offs)
        nc.sync.dma_start(wd_raw[:], wd.rearrange("(p j) v -> p j v", j=PACK))
        for k, (y0, n) in enumerate(Y_LOADS):
            nc.sync.dma_start(y_sb[k][:], y_rows[:, :, y0 : y0 + n])
            if k == 0:
                nc.sync.dma_start(wv_raw[:], wv.rearrange("(p t) d -> p t d", t=PACK))

        def listed(c0, n):
            return offsets[:, c0 // 16 : (c0 + n) // 16]

        ones = held([P, P], F32, name="ones")
        column = held([P, P], F32, name="column")
        row = held([P, QUAD], F32, name="row")
        ident = held([P, P], F32, name="ident")
        base = held([P, 1], F32, name="base")
        nc.vector.memset(ones[:], 1.0)
        for q0 in range(0, P, QUAD):
            nc.vector.memset(base[q0 : q0 + QUAD, :], float(q0))
        nc.vector.tensor_tensor_scan(out=column[:], data0=ones[:], data1=ones[:], initial=0.0, op0=MULT, op1=ADD)
        nc.vector.transpose(out=row[:], in_=column[:, :QUAD])
        nc.vector.tensor_scalar(out=ident[:], in0=column[:], scalar1=row[:, 0:1], scalar2=base[:], op0=SUB, op1=EQUAL)
        placed = [held([P, T], F32, name="placed%d" % j, tag=tag) for j, tag in enumerate(["column", "row", "ident", "plane0"])]

        rw_all = held([P, N], F32, name="rw_all")
        rw_runs = rw_all[:].rearrange("p (n e) -> p n e", e=RUN)
        for e0 in range(0, RUN, PACK):
            spread = bank(e0 // PACK, [P, PACK, P], "spread")
            for e in range(PACK):
                nc.tensor.transpose(out=spread[:, e, :], in_=rw_col[:, e0 + e : e0 + e + 1].to_broadcast([P, P]), identity=ident[:])
            nc.scalar.activation(out=rw_runs[:, :, e0 : e0 + PACK], in_=spread[:].rearrange("p e n -> p n e"), func=COPY)
        weight = held([P, PACK, N], F32, name="weight")
        for t in range(PACK):
            nc.scalar.activation(out=weight[:, t, : 2 * CHUNK], in_=rw_all[:, : 2 * CHUNK], func=COPY, scale=cw_sb[:, t : t + 1])
        for j in range(2):
            nc.vector.memset(placed[j][:].bitcast(U32), 0)
        nc.gpsimd.memset(placed[2][:].bitcast(U32), 0)
        for t in range(PACK):
            nc.gpsimd.tensor_scalar(
                out=weight[:, t, 2 * CHUNK :], in0=rw_all[:, 2 * CHUNK :], scalar1=cw_sb[:, t : t + 1], scalar2=0.0, op0=MULT, op1=ADD
            )

        picked = held([P, PACK * PAIRED], BF16, name="picked")
        picked_halves = picked[:].rearrange("p (u n e) -> p u n e", u=2, e=2)
        picked_words = picked[:].bitcast(U32).rearrange("p (u n) -> p n u", u=2)
        rest = held([P, PACK, CHUNK], BF16, name="rest")
        for t in range(PACK):
            n = CHUNK if t == PACK - 1 else PAIRED
            for c0 in range(0, PAIRED, n):
                nc.vector.tensor_copy(out=picked_halves[:, t // 2, c0 : c0 + n, t % 2], in_=planes[t][:].indirect(listed(c0, n)))
            nc.scalar.activation(out=rest[:, t, :], in_=planes[t][:].indirect(listed(PAIRED, CHUNK)), func=COPY)
            if t == 0:
                nc.gpsimd.memset(placed[3][:].bitcast(U32), 0)

        def weave(target, c0):
            nc.scalar.copy(out=target.bitcast(U32).rearrange("p (n u) -> p n u", u=2), in_=picked_words[:, c0 : c0 + CHUNK, :])

        def quantize(codes, scales, packed, fmt):
            nc.vector.quantize_mx(out=codes.bitcast(fmt), scales=scales, in_=packed)

        x_codes = {}
        x_scales = held([P, N], U8, name="x_scales")

        def quantize_x(c0, packed, codes):
            n = codes.shape[1]
            for a in range(0, n, CHUNK):
                x_codes[(c0 + a) // CHUNK] = codes[:, a : a + CHUNK]
            quantize(codes[:], x_scales[:, c0 : c0 + n], packed[:], E4M3)

        x_packed = [held([P, CHUNK * PACK], BF16, name="x_packed%d" % c) for c in range(2)]
        for c in range(2):
            weave(x_packed[c][:], c * CHUNK)
        quantize_x(0, x_packed[0], held([P, CHUNK], U32, name="x_codes0"))

        wd_packed = held([P, PACK, P, PACK], BF16, name="wd_packed")
        wd_codes = held([P, V], U32, name="wd_codes")
        wd_scales = held([P, V], U8, name="wd_scales")
        cut = P - WD_VECTOR
        wd_columns = wd_raw[:].rearrange("p j (m t) -> p m j t", t=PACK)
        wd_dealt = wd_packed[:].rearrange("p t m j -> p m j t")

        def quantize_wd(t0):
            quantize(
                wd_codes[:, t0 * P : (t0 + 2) * P],
                wd_scales[:, t0 * P : (t0 + 2) * P],
                wd_packed[:, t0 : t0 + 2, :, :].rearrange("p t m j -> p (t m j)"),
                E4M3,
            )

        for t0 in (0, 2):
            nc.scalar.activation(out=wd_dealt[:, :cut, :, t0 : t0 + 2], in_=wd_columns[:, :cut, :, t0 : t0 + 2], func=COPY)
            nc.vector.tensor_copy(out=wd_dealt[:, cut:, :, t0 : t0 + 2], in_=wd_columns[:, cut:, :, t0 : t0 + 2])
        quantize_wd(0)
        quantize_wd(2)
        quantize_x(CHUNK, x_packed[1], over(AT_WD, [P, CHUNK], U32, "x_codes1"))
        x_high = over(AT_WD + 4 * KIB, [P, 2 * CHUNK * PACK], BF16, "x_high")
        weave(x_high[:, : CHUNK * PACK], 2 * CHUNK)
        rest_packed = x_high[:, CHUNK * PACK :].rearrange("p (n t) -> p n t", t=PACK)
        nc.vector.tensor_copy(out=runs_packed(rest_packed[:, :GROUP, :]), in_=runs(rest[:, :, :GROUP]))
        nc.scalar.activation(out=runs_packed(rest_packed[:, GROUP:, :]), in_=runs(rest[:, :, GROUP:]), func=COPY)

        def scores(gi, b, t0=0, count=PACK):
            c0 = gi * GROUP
            a = bank(b, [P, count, GROUP], "a%d" % gi)
            codes = x_codes[c0 // CHUNK]
            for t in range(t0, t0 + count):
                nc.tensor.matmul_mx(
                    out=a[:, t - t0, :],
                    lhsT=wd_codes[:, t * P : (t + 1) * P].bitcast(E4M3),
                    lhsT_scale=wd_scales[:, t * P : (t + 1) * P],
                    rhs=codes[:, c0 % CHUNK : c0 % CHUNK + GROUP].bitcast(E4M3),
                    rhs_scale=x_scales[:, c0 : c0 + GROUP],
                    start=True,
                    stop=True,
                )
            return a

        def targets(gi):
            k = max(k for k in range(len(Y_LOADS)) if Y_LOADS[k][0] <= gi * GROUP)
            y0 = gi * GROUP - Y_LOADS[k][0]
            return y_sb[k][:, :, y0 : y0 + GROUP]

        diff = {}
        slope = {}
        g_packed = {}
        g_mx = {}

        def group(name, tag=None):
            return held([P, PACK, GROUP], F32, name=name, tag=tag)

        def subtract(gi, b, tile):
            diff[gi] = tile
            nc.vector.tensor_tensor(out=tile[:], in0=scores(gi, b)[:], in1=targets(gi), op=SUB)

        def bend(gi, target):
            slope[gi] = target
            nc.scalar.activation(out=target, in_=diff[gi][:], func=TANH)

        def weigh(engine, c0, source, target, side):
            engine.tensor_tensor(
                out=runs_packed(target, side),
                in0=runs(source, side),
                in1=runs(weight[:, :, c0 : c0 + source.shape[2]], side),
                op=MULT,
            )

        def quantize_g(c0, codes, scales):
            g_mx[c0] = (codes, scales)
            quantize(codes[:], scales[:], g_packed[c0][:].rearrange("p n t -> p (n t)"), E5M2)

        def copy_out(engine, target, source):
            if engine is nc.vector:
                nc.vector.tensor_copy(out=target, in_=source)
            else:
                nc.scalar.activation(out=target, in_=source, func=COPY)

        def place(engine, j, c0, source):
            window = placed[j][:].indirect(listed(c0, source.shape[1]))
            if engine is nc.vector:
                nc.vector.tensor_copy(out=window, in_=source)
            else:
                nc.scalar.activation(out=window, in_=source, func=COPY)

        def store(j):
            nc.sync.dma_start(out[j * P : (j + 1) * P, :], placed[j][:])

        for gi in range(2):
            slope[gi] = group("slope%d" % gi)
        for t0 in (0, 2):
            for gi in range(2):
                part = held([P, 2, GROUP], F32, name="part%d_%d" % (gi, t0))
                nc.vector.tensor_tensor(out=part[:], in0=scores(gi, t0 + gi, t0, 2)[:], in1=targets(gi)[:, t0 : t0 + 2, :], op=SUB)
                nc.scalar.activation(out=slope[gi][:, t0 : t0 + 2, :], in_=part[:], func=TANH)
        quantize_x(2 * CHUNK, x_high, held([P, 2 * CHUNK], U32, name="x_codes_high", tag="part0_0"))
        g_packed[0] = held([P, CHUNK, PACK], BF16, name="g_packed0")
        for gi in range(2):
            weigh(nc.vector, gi * GROUP, slope[gi][:], g_packed[0][:, gi * GROUP : (gi + 1) * GROUP, :], SIDE)
        subtract(2, 6, group("diff2", "slope0"))
        g_mx[0] = (held([P, CHUNK], U32, name="g_codes0"), held([P, CHUNK], U8, name="g_scales0"))
        for a in (0, GROUP):
            quantize(g_mx[0][0][:, a : a + GROUP], g_mx[0][1][:, a : a + GROUP], g_packed[0][:, a : a + GROUP, :].rearrange("p n t -> p (n t)"), E5M2)
        wv_packed = held([P, D, PACK], BF16, name="wv_packed", tag="g_late")
        for j in range(PACK):
            nc.scalar.activation(out=runs_packed(wv_packed[:, j * P : (j + 1) * P, :]), in_=runs(wv_raw[:, :, j * P : (j + 1) * P]), func=COPY)
        subtract(3, 7, group("diff3", "slope1"))
        wv_codes = held([P, D], U32, name="wv_codes")
        wv_scales = held([P, D], U8, name="wv_scales")
        quantize(wv_codes[:], wv_scales[:], wv_packed[:].rearrange("p d t -> p (d t)"), E4M3)
        for gi in (2, 3):
            bend(gi, group("slope%d" % gi)[:])
        def products(b, c0, js):
            codes, scales = g_mx[c0]
            tile = bank(b, [P, len(js), codes.shape[1]], "dx%d_%d" % (c0, js[0]))
            for k, j in enumerate(js):
                nc.tensor.matmul_mx(
                    out=tile[:, k, :],
                    lhsT=wv_codes[:, j * P : (j + 1) * P].bitcast(E4M3),
                    lhsT_scale=wv_scales[:, j * P : (j + 1) * P],
                    rhs=codes[:].bitcast(E5M2),
                    rhs_scale=scales[:],
                    start=True,
                    stop=True,
                )
            return tile

        first = [products(4 + e, 0, (e, 2 + e)) for e in range(2)]
        opening0 = over(AT_G + 2 * KIB, [P, CHUNK], F32, "opening0")
        opening2 = held([P, CHUNK], F32, name="opening2")
        opening_odd = held([P, 2, CHUNK], F32, name="opening_odd")
        opening = [opening0[:], opening_odd[:, 0, :], opening2[:], opening_odd[:, 1, :]]
        slope_pair = over(AT_G - 2 * KIB, [P, PACK, CHUNK], F32, "slope_pair")
        for gi in range(4, 8):
            subtract(gi, gi - 4, group("diff%d" % gi))
            bend(gi, slope_pair[:, :, (gi - 4) * GROUP : (gi - 3) * GROUP] if gi < 6 else group("slope%d" % gi)[:])
            if gi == 4:
                copy_out(nc.scalar, opening0[:], first[0][:, 0, :])
                copy_out(nc.scalar, opening2[:], first[0][:, 1, :])
            if gi == 6:
                copy_out(nc.scalar, opening_odd[:], first[1][:])
        g_packed[CHUNK] = held([P, 2 * CHUNK, PACK], BF16, name="g_packed1", tag="g_late")
        for gi in (2, 3):
            weigh(nc.gpsimd, gi * GROUP, slope[gi], g_packed[CHUNK][:, (gi - 2) * GROUP : (gi - 1) * GROUP, :], GPSIMD_SIDE)
        weigh(nc.gpsimd, 2 * CHUNK, slope_pair[:], g_packed[CHUNK][:, CHUNK:, :], GPSIMD_SIDE)
        for j in range(PACK):
            place(nc.vector if j % 2 == 0 else nc.scalar, j, 0, opening[j])
        g_mx[CHUNK] = (held([P, 2 * CHUNK], U32, name="g_codes1"), over(AT_G + 5 * KIB // 2, [P, 2 * CHUNK], U8, "g_scales1"))
        for a in (0, CHUNK):
            quantize(
                g_mx[CHUNK][0][:, a : a + CHUNK],
                g_mx[CHUNK][1][:, a : a + CHUNK],
                g_packed[CHUNK][:, a : a + CHUNK, :].rearrange("p n t -> p (n t)"),
                E5M2,
            )
        g_packed[3 * CHUNK] = over(AT_G + KIB // 2, [P, CHUNK, PACK], BF16, "g_packed3")
        for gi in (6, 7):
            weigh(nc.vector, gi * GROUP, slope[gi], g_packed[3 * CHUNK][:, (gi - 6) * GROUP : (gi - 5) * GROUP, :], SIDE)
        closing0 = held([P, 3 * CHUNK], F32, name="closing0")
        closing_odd = held([P, 2, 3 * CHUNK], F32, name="closing_odd")
        middle = {j: bank(6 + j, [P, 1, 2 * CHUNK], "middle%d" % j) for j in range(2)}
        for a in (0, CHUNK):
            for j in range(2):
                nc.tensor.matmul_mx(
                    out=middle[j][:, 0, a : a + CHUNK],
                    lhsT=wv_codes[:, j * P : (j + 1) * P].bitcast(E4M3),
                    lhsT_scale=wv_scales[:, j * P : (j + 1) * P],
                    rhs=g_mx[CHUNK][0][:, a : a + CHUNK].bitcast(E5M2),
                    rhs_scale=g_mx[CHUNK][1][:, a : a + CHUNK],
                    start=True,
                    stop=True,
                )
        for j, b in ((3, 0), (2, 1)):
            middle[j] = products(b, CHUNK, (j,))
        copy_out(nc.vector, closing0[:, : 2 * CHUNK], middle[0][:, 0, :])
        quantize_g(3 * CHUNK, held([P, CHUNK], U32, name="g_codes3"), held([P, CHUNK], U8, name="g_scales3"))
        closing2 = held([P, 3 * CHUNK], F32, name="closing2")
        for j in (1, 3):
            copy_out(nc.scalar, closing_odd[:, j // 2, : 2 * CHUNK], middle[j][:, 0, :])
        copy_out(nc.scalar, closing2[:, : 2 * CHUNK], middle[2][:, 0, :])
        last = [products(2 + h, 3 * CHUNK, js) for h, js in enumerate([(1, 0), (2, 3)])]
        copy_out(nc.scalar, closing_odd[:, 0, 2 * CHUNK :], last[0][:, 0, :])
        copy_out(nc.scalar, closing0[:, 2 * CHUNK :], last[0][:, 1, :])
        place(nc.vector, 0, CHUNK, closing0[:, : 2 * CHUNK])
        copy_out(nc.vector, closing2[:, 2 * CHUNK :], last[1][:, 0, :])
        place(nc.vector, 0, 3 * CHUNK, closing0[:, 2 * CHUNK :])
        store(0)
        place(nc.scalar, 1, CHUNK + 384, closing_odd[:, 0, 384:])
        copy_out(nc.scalar, closing_odd[:, 1, 2 * CHUNK :], last[1][:, 1, :])
        place(nc.scalar, 1, CHUNK, closing_odd[:, 0, :384])
        store(1)
        place(nc.vector, 2, CHUNK, closing2[:])
        store(2)
        for a in (384, 0):
            place(nc.scalar, 3, CHUNK + a, closing_odd[:, 1, a : a + 384])
        store(3)
